import numpy as np, ml_dtypes
CORES = [66,74,82,90,194,202,210,218]
N = 8
BF = ml_dtypes.bfloat16
def gentries(a):
    return np.ascontiguousarray(a.reshape(8, 16, -1).transpose(0, 2, 1)).reshape(8, -1)
def gtable(e):
    e = np.asarray(e); return np.ascontiguousarray(e.reshape(8, -1, 16).transpose(0, 2, 1)).reshape(128, -1).astype(np.int32)
L, B, V, W, DAYS, INTERVALS, H = 32, 48, 1536, 4096, 2, 3, 12
def parts(rng):
    x = rng.integers(28, 100, (N, 8, 1, V)) + rng.integers(-20, 21, (N, 8, 16, V))
    z = rng.integers(0, 65536, (N, 8, V))
    e = rng.integers(-75, 46, (8, 1, W)) + rng.integers(-20, 21, (8, 16, W))
    return x, z, e
def pack(x, z, e):
    x = np.minimum(np.maximum(x, 0), 127).reshape(N, 128, V); e = np.minimum(np.maximum(e, -128), 128).reshape(1, 128, W)
    return {"x": x.astype(np.float32).astype(BF), "boat": np.stack([gtable(a) for a in z]), "enc": np.repeat(e, N, axis=0).astype(np.float32).astype(BF)}
def timed(rng, z, g):
    r = rng.integers(0, W); z[:, g] = r + W * rng.integers(0, 65536 // W, (N, V))
    return (138 * r + 811 * np.arange(DAYS * INTERVALS + DAYS)) % W
def setup_inputs(rng):
    return pack(*parts(rng))
def setup_inputs_ties(rng):
    x, z, e = parts(rng)
    x = rng.integers(20, 100, (1, 8, 16, 1)) + rng.integers(0, 2, (N, 8, 1, V))
    n = rng.choice(np.array([0, H - 1, H - 1, H, H, H + 1, 16]), (8, 1, W)); up = np.argsort(rng.random((8, 16, W)), axis=1) < n
    e = rng.choice(np.array([0, 0, 1, 1, 1, 2]), (8, 1, W)) - 1 + up
    return pack(x, z, e)
def setup_inputs_order(rng):
    x, z, e = parts(rng); b = np.arange(B); k = INTERVALS; q = b % (2 * k)
    st = np.stack([127 - 2 * b, 1 + 2 * b, np.where(q < k, 10 * (k - q), 10 * (3 * k - q)), 64 + 0 * b, np.where(b == 0, 120, np.where(b == B - 1, 127, 1 + 2 * b))])
    kind = rng.integers(0, 6, (N, 8, L)); kind[:, :, :6] = np.arange(6); kind[:, :, L - 6:] = rng.permutation(6)
    s = st[np.minimum(kind, 4)].transpose(0, 1, 3, 2).reshape(N, 8, 1, V)
    x = np.where(np.tile(kind == 5, (1, 1, B))[:, :, None, :], x, s)
    e = np.where(rng.random((8, 16, W)) < rng.random((8, 1, W)), 1, rng.integers(-1, 1, (8, 16, W)))
    return pack(x, z, e)
def setup_inputs_alike(rng):
    x, z, e = parts(rng); zz = z.reshape(N, 8, B, L).copy(); inv = pow(37, -1, W)
    for b in range(1, B):
        c = rng.choice(np.array([0, W - 1]), (N, 8, L))
        zz[:, :, b] = (c - 101 * zz[:, :, b - 1]) % W * inv % W + W * rng.integers(0, 65536 // W, (N, 8, L))
    zz[:, :, :, 1::2] = rng.choice(np.array([0, 65535, 65535, 1]), (N, 8, B, len(range(1, L, 2))))
    e[:, :, 0] = rng.integers(-10, 31, (8, 16)); e[:, :, W - 1] = rng.integers(-30, 11, (8, 16))
    g = rng.permutation(8); odd = np.arange(N)[:, None, None] % 2 == 1
    for i, (c, s) in enumerate(((0, 1), (W - 1, -1))):
        a = rng.integers(0, W, L); b = (c - 811 * DAYS * INTERVALS - 101 * a) % W * inv % W
        zz[:, g[i]] = np.where(odd, b, a) + W * rng.integers(0, 65536 // W, (N, B, L))
        e[g[i]][:, c] = s * rng.integers(112, 129, 16); e[g[i]][:, c + s] = -s * rng.integers(112, 129, 16)
    return pack(x, zz.reshape(N, 8, V), e)
def setup_inputs_flat(rng):
    x, z, e = parts(rng); g = rng.permutation(8); k = INTERVALS; last = (DAYS - 1) * k
    e[g[0]] = -128; e[g[1]] = 128
    x[:, g[1]] = np.where(rng.random((N, 1, V)) < 0.5, x[:, g[1]], 127 * rng.integers(0, 2, (N, 1, V)))
    e[g[2]] = 127; x[:, g[2]] = 127 * rng.integers(0, 2, (N, 16, V))
    e[g[3]] = rng.choice(np.array([-127, -126]), (1, W)); x[:, g[3]] = 127 * rng.integers(0, 2, (N, 1, V))
    c = timed(rng, z, g[4]); e[g[4]][:, c[:k - 1]] = -128; e[g[4]][:, c[k - 1]] = 128
    c = timed(rng, z, g[5]); e[g[5]][:, c[last]] = -128; e[g[5]][:, c[last + 1]] = rng.integers(127, 129, 16)
    c = timed(rng, z, g[6]); e[g[6]][:, c[:-1]] = -128; e[g[6]][:, c[[last, last + k - 1]]] = 0
    b = np.arange(B)[:, None]; s = np.where(b == 0, 120, np.where(b == B - 1, 127, 1 + 2 * b))
    x[:, g[6]] = np.where(rng.random((N, 1, 1, L)) < 0.5, s, x[:, g[6]].reshape(N, 16, B, L)).reshape(N, 16, V)
    return pack(x, z, e)
def setup_inputs_spread(rng):
    x = np.floor(127.99 * np.exp2(-6 * rng.random((N, 8, 1, V))) * rng.random((N, 8, 16, V))).astype(np.int64)
    z = np.minimum(np.exp2(16 * rng.random((N, 8, V))).astype(np.int64), 65535) - 1 + rng.integers(0, 2, (N, 8, V))
    e = np.rint(128 * np.exp2(-7 * rng.random((8, 1, W))) * (0.25 + 0.75 * rng.random((8, 16, W)))).astype(np.int64) * (2 * rng.integers(0, 2, (8, 1, W)) - 1)
    return pack(x, z, e)
def check_inputs(d):
    bad = []
    for k, lo, hi in (("x", 0, 127), ("boat", 0, 65535), ("enc", -128, 128)):
        v = np.asarray(d[k]).astype(np.float32)
        if not np.all((v >= lo) & (v <= hi) & (v == np.floor(v))): bad.append("range of " + k)
    v = np.asarray(d["enc"]).astype(np.float32)
    if not np.all(v == v[:1]): bad.append("enc alike on all ranks")
    return bad
def beats(xi, zi, xj, zj, e, t):
    c = (37 * zi + 101 * zj + 811 * t) & (W - 1)
    v = np.take_along_axis(e, c[:, :, None, :], 3)
    return np.add.reduce((xi + v > xj).astype(np.int64), axis=2) >= H
def reference(x, boat, enc):
    X = x.astype(np.float32).reshape(N, 8, 16, V); E = enc.astype(np.float32).reshape(N, 8, 16, W)
    Z = np.stack([gentries(a) for a in boat]).astype(np.int64)
    for day in range(DAYS):
        rowing = np.ones((N, 8, V), bool); place = np.tile(np.arange(V), (N, 8, 1))
        for k in range(INTERVALS):
            row = rowing.reshape(N, 8, B, L); rival = np.full((N, 8, B, L), -1); last = np.full((N, 8, L), -1)
            for b in range(B):
                rival[:, :, b] = np.where(row[:, :, b], last, -1)
                last = np.where(row[:, :, b], b * L + np.arange(L), last)
            rival = rival.reshape(N, 8, V); j = np.maximum(rival, 0)
            w = beats(X, Z, np.take_along_axis(X, j[:, :, None, :], 3), np.take_along_axis(Z, j, 2), E, day * INTERVALS + k) & (rival >= 0)
            w = w.reshape(N, 8, B, L); bump = np.zeros((N, 8, B, L), bool); before = np.zeros((N, 8, L), bool)
            for b in range(B):
                bump[:, :, b] = w[:, :, b] & ~before
                before = np.where(row[:, :, b], bump[:, :, b], before)
            i0, i1, i2 = np.nonzero(bump.reshape(N, 8, V)); jj = j[i0, i1, i2]
            place[i0, i1, i2] = jj; place[i0, i1, jj] = i2
            rowing[i0, i1, i2] = False; rowing[i0, i1, jj] = False
        X = np.take_along_axis(X, place[:, :, None, :], 3); Z = np.take_along_axis(Z, place, 2)
        hx, hz = np.array(X[1:, :, :, :L]), np.array(Z[1:, :, :L]); fx, fz = np.array(X[:-1, :, :, V - L:]), np.array(Z[:-1, :, V - L:])
        w = beats(hx, hz, fx, fz, E[1:], DAYS * INTERVALS + day); wx = w[:, :, None, :]
        X[1:, :, :, :L] = np.where(wx, fx, hx); Z[1:, :, :L] = np.where(w, fz, hz)
        X[:-1, :, :, V - L:] = np.where(wx, hx, fx); Z[:-1, :, V - L:] = np.where(w, hz, fz)
    return {"yx": X.reshape(N, 128, V).astype(BF), "yb": np.stack([gtable(a) for a in Z]).astype(np.float32)}

@@ -1,0 +1,494 @@
+import math
+from concourse.bass import DstId, RemoteDMATransfer
+from concourse.mybir import AluOpType as ALU, ActivationFunctionType as ACT
+
+B, V, W = 48, 1536, 4096
+HW = 16 + 16 * B
+EW = 10624
+BIG, HALF, EPS = 2.0 ** 24, 2.0 ** 21, 2.0 ** -19
+NS = {(0, 0): 28, (0, 1): 24, (0, 2): 22, (1, 0): 31, (1, 1): 24, (1, 2): 22}
+NO = min(NS.values())
+PERM_V = 8
+FIN_V = 44
+ENC_CP = ["v", "s", "v", None]
+TRIES, MOVES = 24, 60000
+MODELS = [dict(f=1.2, g=1.56, wake=60.0, pe=0.42, dma=2000.0, bw=250.0, rem=2500.0),
+          dict(f=1.1, g=1.2, wake=120.0, pe=0.42, dma=1700.0, bw=300.0, rem=3500.0),
+          dict(f=1.3, g=1.9, wake=30.0, pe=0.5, dma=2300.0, bw=200.0, rem=2000.0)]
+
+BF, F, I, U = "bfloat16", "float32", "int32", "uint16"
+SCRATCH = {"pmw": ("psum", [128, 512], F), "pmc": ("psum", [128, 512], F)}
+for _n, _s, _t in (
+        ("xn", [B, 2, 16], BF), ("bt", [B, 2], I), ("encw", [EW], BF), ("xw0", [2 * HW], BF), ("xw1", [2 * HW], BF), ("ys", [V], BF),
+        ("ye", [2, 32], BF), ("zf", [B, 2], F), ("nat", [96], U), ("ones", [128], BF), ("tmpb", [128], BF), ("idp", [128], BF),
+        ("idn", [128], BF), ("idw", [128], BF), ("idb", [128], BF), ("idc", [128], BF), ("idf", [128], F), ("idg", [128], F),
+        ("bo", [128], BF), ("usel", [144], BF), ("w8", [8], BF), ("t8", [8], BF), ("pi", [2], I), ("rc", [4], F), ("bi", [B], F),
+        ("bc", [B], F), ("ni", [3, B], F), ("kap", [6, B], BF), ("am", [B], BF), ("eps", [B], F), ("thw", [64], F), ("thc", [4], F),
+        ("ex", [8, 40], F), ("zab", [B, 3, 2], I), ("mc", [4], U), ("md", [2, 40], F), ("mt", [2, 40], F), ("ms", [2, 2], F),
+        ("uc", [2, 2], F), ("uw", [2, 32], F), ("cm", [64], BF)):
+    SCRATCH[_n] = ("sbuf", [128] + _s, _t)
+for _h in "01":
+    for _n, _s, _t in (
+            ("cmp", [752], BF), ("dv", [752], BF), ("eg", [752], BF), ("xr", [752], BF), ("xo", [2, 16 * (47 - NO)], BF), ("ll", [96], U),
+            ("l2", [B], U), ("pl", [B], U), ("el", [4], U), ("raw", [B, 2], I), ("ci", [2, B], I), ("zi", [B], I), ("pq", [B], I),
+            ("xy", [96], F), ("tt", [192], F), ("mi", [2, 96], F), ("kk", [4, 52], F), ("fa", [6, B], F), ("aa", [B], BF), ("ce", [B], F)):
+        SCRATCH[_n + _h] = ("sbuf", [128] + _s, _t)
+    for _n in ("ps", "pc", "pf"):
+        SCRATCH[_n + _h] = ("psum", [128, 512], F)
+
+SEMAPHORES = ["qv", "qs", "qp", "qg", "sent", "arr0", "arr1"] + ["dma%d" % i for i in range(20)]
+
+
+def build(g, core, T, topo, rank):
+    ops, n = [], len(T.cores)
+    Vq, Sq, Pq = g.vector, g.scalar, g.tensor
+    early = [True]
+
+    def add(eng, name, fn, r, w, fix=0.0, cyc=0.0, gat=0.0, pe=0.0, byt=0.0, kind="c"):
+        ops.append(dict(eng=eng, name=name, fn=fn, r=list(r), w=list(w), cost=(fix, cyc, gat, pe, byt), kind=kind, early=early[0], extra=False))
+
+    def ts(name, out, in0, s1, s2, op0, op1, r, w, k=64):
+        add("v", name, lambda: Vq.tensor_scalar(out, in0, s1, s2, *([op0] if op1 is None else [op0, op1])), r, w, cyc=max(64, k))
+
+    def tt(name, out, in0, in1, op, r, w, k=64):
+        add("v", name, lambda: Vq.tensor_tensor(out, in0, in1, op), r, w, cyc=max(64, k))
+
+    def cp(name, out, in_, r, w, k=64):
+        add("v", name, lambda: Vq.tensor_copy(out, in_), r, w, cyc=max(64, k))
+
+    def scan(name, out, d0, d1, init, op0, op1, r, w, k=64):
+        add("v", name, lambda: Vq.tensor_tensor_scan(out, d0, d1, init, op0, op1), r, w, cyc=max(64, k))
+
+    def mset(name, ap, val, w, k=64):
+        add("v", name, lambda: Vq.memset(ap, val), [], w, cyc=max(64, k))
+
+    def act(name, out, in_, func, r, w, k=64, bias=0.0, scale=1.0):
+        add("s", name, lambda: Sq.activation(out, in_, func, bias=bias, scale=scale), r, w, fix=30.0, cyc=max(64, k))
+
+    def vgt(name, out, win, lst, in1, op, r, w, k):
+        add("v", name, lambda: Vq.tensor_tensor(out, win.indirect(lst), in1, op), r, w, fix=50.0, gat=k)
+
+    def vgc(name, out, win, lst, r, w, k):
+        add("v", name, lambda: Vq.tensor_copy(out, win.indirect(lst)), r, w, fix=50.0, gat=k)
+
+    def sgc(name, out, win, lst, r, w, k):
+        add("s", name, lambda: Sq.activation(out, win.indirect(lst), ACT.Copy), r, w, fix=65.0, gat=k)
+
+    def mm(name, lst, r, w):
+        add("p", name, lambda: [Pq.matmul(*m[:5]) for m in lst][-1], r, w, pe=sum(m[5] * max(64, m[0].shape[-1]) for m in lst))
+
+    queued = [0.0]
+
+    def dma(q, name, out, in_, r, w, nbytes, ahead=True):
+        queued[0] = (queued[0] if ahead else 0.0) + nbytes
+        add(q, name, lambda: (g.sync if q == "y" else g.scalar).dma_start(out, in_), r, w, fix=60.0, byt=queued[0], kind="d")
+
+    def gp(name, fn, r, w, k):
+        add("g", name, fn, r, w, fix=170.0, cyc=2 * k)
+
+    dma("y", "ld_boat", T.bt[:], T.boat[:], [], ["bt"], 49152)
+    dma("s", "ld_x", T.xn[:], T.x[:], [], ["xn"], 393216)
+    Q = W // len(ENC_CP)
+    ekeys = [(Q * i, "e%d" % i) for i in range(len(ENC_CP))] + [(W + Q * i, "f%d" % i) for i in range(len(ENC_CP))] + [(2 * W, "t0"), (9008, "t1")]
+    for i in range(len(ENC_CP)):
+        dma("y", "ld_enc", T.encw[:, Q * i:Q * i + Q], T.enc[:, Q * i:Q * i + Q], [], ["e%d" % i], Q * 256)
+    for i, who in enumerate(ENC_CP):
+        if who is None:
+            dma("y", "ld_rep", T.encw[:, W + Q * i:W + Q * i + Q], T.enc[:, Q * i:Q * i + Q], [], ["f%d" % i], Q * 256)
+    for i, (a, b_) in enumerate(((2 * W, 9008), (9008, EW))):
+        dma("y", "ld_tail", T.encw[:, a:b_], T.enc[:, a - 2 * W:b_ - 2 * W], [], ["t%d" % i], (b_ - a) * 256)
+
+    def ewin(end):
+        return T.encw[:, 0:end], [k for (a, k) in ekeys if a < end]
+
+    mset("ones", T.ones[:], 1.0, ["ones"])
+    mset("w8", T.w8[:], -BIG, ["w8"])
+    mset("usel", T.usel[:], 0.0, ["usel"], 72)
+    gp("idp", lambda: g.affine_select(T.idp[:], T.ones[:], [[-1, 128]], ALU.is_equal, 0.0, 0, 1), ["ones"], ["idp"], 128)
+    gp("pi", lambda: g.iota(T.pi[:, 0:1], [[1, 1]], 0, 1), [], ["pi0"], 1)
+    gp("bi", lambda: g.iota(T.bi[:], [[1, B]], 0, 0, allow_small_or_imprecise_dtypes=True), [], ["bi"], B)
+    gp("t8", lambda: g.affine_select(T.t8[:], T.w8[:], [[-16, 8]], ALU.is_ge, 0.0, 0, 1), ["w8"], ["t8"], 8)
+    gp("usel", lambda: g.affine_select(T.usel[:, 15:143:16], T.t8[:], [[16, 8]], ALU.is_ge, 0.0, 15, -1), ["t8"], ["usel"], 8)
+    gp("bo", lambda: g.affine_select(T.tmpb[:], T.ones[:], [[-16, 8], [0, 16]], ALU.is_ge, 0.0, 0, 1), ["ones"], ["tmpb"], 128)
+    gp("bo", lambda: g.affine_select(T.bo[:], T.tmpb[:], [[16, 8], [0, 16]], ALU.is_ge, 0.0, 15, -1), ["tmpb"], ["bo"], 128)
+    mset("am", T.am[:], -1.0, ["am"])
+    mset("eps", T.eps[:], EPS, ["eps"])
+    kaps = {}
+    for (d, k), ns in sorted(NS.items()):
+        key = (k == 0, ns, int((d, k) == (1, 0)))
+        if key not in kaps:
+            i = kaps[key] = len(kaps)
+            mset("kap", T.kap[:, i, :], 4.5 / 16 - key[0], ["kap%d" % i])
+            mset("kap", T.kap[:, i, key[2]:ns + key[2]], 9.0 / 16 - key[0], ["kap%d" % i])
+    up, down = rank > 0, rank < n - 1
+    for e, t in enumerate((11.5 if up else 1000.0, 4.5 if down else -1000.0)):
+        mset("thw", T.thw[:, 32 * e:32 * e + 32], t, ["thw%d" % e])
+        mset("thc", T.thc[:, 2 * e:2 * e + 2], -t * BIG, ["thc%d" % e])
+    for d in range(2):
+        for s in [0, 3] + ([] if down else [1]) + ([] if up else [2]):
+            mset("ex", T.ex[:, 4 * d + s, :], 0.0, ["ex%d_%d%d" % (d, s, h) for h in range(2)] + ["exz%d%d" % (d, h) for h in range(2) if s in (0, 3)])
+            ops[-1]["extra"] = s in (1, 2)
+        for h in range(2):
+            mset("sent", T["xw%d" % d][:, h * HW:h * HW + 16], 255.0, ["sn%d%d" % (d, h)])
+    for H in "01":
+        mset("mi", T["mi" + H][:], 1.0, ["m%s1" % H, "m%s2" % H], 192)
+        mset("kk", T["kk" + H][:], 0.0, ["k%s%d" % (H, i) for i in range(4)], 208)
+        mset("sh", T["pc" + H][:, 63:64], BIG, ["s0" + H, "pc" + H])
+    for nm, val in (("idn", -1.0), ("idw", -16.0 * BIG), ("idb", -HALF), ("idc", HALF), ("idf", 1.0), ("idg", -1.0)):
+        act(nm, T[nm][:], T.idp[:], ACT.Identity, ["idp"], [nm], 128, scale=val)
+    ts("r", T.pi[:, 1:2], T.pi[:, 0:1], 15, None, ALU.bitwise_and, None, ["pi0"], ["pi1"])
+    for h in range(2):
+        ts("rc", T.rc[:, h:h + 1], T.pi[:, 1:2], 16.0 + HW * h, None, ALU.add, None, ["pi1"], ["rc%d" % h])
+    ts("bc", T.bc[:], T.bi[:], 65536.0, None, ALU.mult, None, ["bi"], ["bc"])
+    ts("ni", T.ni[:, 0, :], T.bi[:], 16.0, T.rc[:, 0:1], ALU.mult, ALU.add, ["bi", "rc0"], ["ni0"])
+    for k in (1, 2):
+        ts("ni", T.ni[:, k, :], T.ni[:, 0, :], -811.0 * k, None, ALU.add, None, ["ni0"], ["ni%d" % k])
+    early[0] = False
+    for i, who in enumerate(ENC_CP):
+        o, s = T.encw[:, W + Q * i:W + Q * i + Q], T.encw[:, Q * i:Q * i + Q]
+        if who == "v":
+            cp("rep", o, s, ["e%d" % i], ["f%d" % i], Q / 2)
+        elif who == "s":
+            act("rep", o, s, ACT.Identity, ["e%d" % i], ["f%d" % i], Q)
+
+    zab, ex = T.zab, T.ex
+
+    def xk(d, h):
+        return [s + "%d%d" % (d, h) for s in ("sn", "xa", "xb", "xh", "xf")]
+
+    def numbers(h, src, rk, t):
+        raw, H = T["raw%d" % h], str(h)
+        ts("rawa" + H, raw[:, :, 0], src, 37.0, 811.0 * t, ALU.mult, ALU.add, rk, ["rawa" + H])
+        ts("rawb" + H, raw[:, :, 1], src, 101.0, None, ALU.mult, None, rk, ["rawb" + H])
+        ts("ab" + H, zab[:, :, 1:3, h], raw[:], W - 1, None, ALU.bitwise_and, None, ["rawa" + H, "rawb" + H], ["ab" + H], 2 * B)
+
+    def day_start(d, h):
+        H = str(h)
+        xy, fa, ci, ll = T["xy" + H], T["fa" + H], T["ci" + H], T["ll" + H]
+        z, zk = (T.bt[:, :, h], ["bt"]) if d == 0 else (zab[:, :, 0, h], ["z" + H])
+        tt("y" + H, xy[:, 1:94:2], zab[:, 0:47, 2, h], zab[:, 1:48, 1, h], ALU.add, ["ab" + H], ["xy1" + H], 94)
+        if d == 0:
+            cp("c0a" + H, ci[:, 0, 0:47], xy[:, 1:94:2], ["xy1" + H], ["ci0" + H])
+            ts("c0b" + H, ci[:, 1, 0:47], ci[:, 0, 0:47], W - 1, None, ALU.bitwise_and, None, ["ci0" + H], ["ci1" + H])
+            cp("c0" + H, ll[:, 0:47], ci[:, 1, 0:47], ["ci1" + H], ["ll" + H])
+            act("own" + H, T["xo" + H][:, 0, :], T.xn[:, NO + 1:B, h, :], ACT.Identity, ["xn"], ["xo0" + H], 16 * (47 - NO))
+        else:
+            cp("c0" + H, ll[:, 0:47], xy[:, 1:94:2], ["xy1" + H], ["ll" + H])
+            dma("y", "own" + H, T["xo" + H][:, 1, :], T.xw1[:, h * HW + 32 + 16 * NO:(h + 1) * HW], xk(d, h), ["xo1" + H], 4096 * (47 - NO), False)
+        tt("sx" + H, fa[:, 0, 0:47], zab[:, 0:47, 1, h], zab[:, 0:47, 2, h], ALU.add, ["ab" + H], ["sx" + H], 94)
+        act("x" + H, xy[:, 0:94:2], fa[:, 0, 0:47], ACT.Identity, ["sx" + H], ["xy0" + H], scale=-1.0)
+        tt("zz" + H, fa[:, 1, :], z, T.bc[:], ALU.add, zk + ["bc"], ["zz" + H], 96)
+        tt("dz" + H, fa[:, 2, 1:48], fa[:, 1, 0:47], fa[:, 1, 1:48], ALU.subtract, ["zz" + H], ["dz" + H], 94)
+
+    def adjacent(d, h, b0, b1, rk, wk):
+        xw, o, ns = T["xw%d" % d], h * HW, (NS[(d, 0)] if b0 > 1 else 0)
+        tt("d%d_%d" % (b0, h), T["dv%d" % h][:, 16 * (b0 - 1 - ns):16 * (b1 - 1 - ns)], xw[:, o + 16 * b0:o + 16 * b1],
+           xw[:, o + 16 + 16 * b0:o + 16 + 16 * b1], ALU.subtract, rk, wk, 32 * (b1 - b0))
+
+    def interval(d, k, h):
+        H, ns = str(h), NS[(d, k)]
+        s0 = int((d, k) == (1, 0))
+        nv, xw, o = 47 - ns, T["xw%d" % d], h * HW
+        win = xw[:, o:o + HW]
+        cmp_, dv, eg, xr, ll, tb = [T[s + H] for s in ("cmp", "dv", "eg", "xr", "ll", "tt")]
+        ps, pc, pf, fa, kk, mi, aa = [T[s + H] for s in ("ps", "pc", "pf", "fa", "kk", "mi", "aa")]
+        ew, ek = ewin(W if (d, k) == (0, 0) else (2 * W + 811 * k + 15) // 16 * 16)
+        X, tag = xk(d, h), "%d%d%d" % (d, k, h)
+        XS, ls, lk = (X[1:3], T["l2" + H], "l2" + H) if s0 else (X, ll, "ll" + H)
+        ka = kaps[(k == 0, ns, s0)]
+        mm("cn0" + tag, [(pc[:, 0:47], T.idw[:], T.kap[:, ka, 0:47], True, False, 1)] + [(pc[:, 0:47], T.idw[:], aa[:, 1:48], False, False, 1)][:k],
+           ["idw", "kap%d" % ka] + ["aa" + H][:k], ["pc" + H, "s" + H, "l" + H])
+        if k > 0:
+            sgc("gx" + tag, xr[:, 0:16 * ns], win, ll[:, 48:48 + ns], X + ["lr" + H], ["xr" + H], 16 * ns)
+            vgt("gd" + tag, dv[:, 0:16 * nv], win, ll[:, 48 + ns:95], T["xo" + H][:, d, 16 * (ns - NO):16 * (47 - NO)], ALU.subtract,
+                X + ["lr" + H, "xo%d" % d + H], ["dv" + H, "dw" + H, "dx" + H], 16 * nv)
+        n1 = ns * 5 // 16 * 2
+        for C, u0, u1, pp, pk in (("0", 0, n1, ps, "ps" + H), ("1", n1, ns, (T.pmw, T.pmc)[h], ("pmw", "pmc")[h])):
+            a0, a1 = 16 * u0, 16 * u1
+            c0, out = o + 16 + 16 * s0, pp[:, 0:a1 - a0]
+            mm("su0" + C + tag, [(out, T.idp[:], xw[:, c0 + 16 + a0:c0 + 16 + a1], True, False, 1),
+                                 (out, T.idn[:], xr[:, a0:a1] if k else xw[:, c0 + a0:c0 + a1], False, False, 1)],
+               XS + ["xr" + H][:k] + ["idp", "idn"], [pk])
+            sgc("ge" + C + tag, eg[:, a0:a1], ew, ls[:, u0:u1], ek + [lk], ["eg" + C + H], a1 - a0)
+            mm("su1" + C + tag, [(out, T.idp[:], eg[:, a0:a1], False, True, 1)], ["eg" + C + H, "idp", pk], [pk])
+            act("sg" + C + tag, cmp_[:, 16 * s0 + a0:16 * s0 + a1], out, ACT.Sign, [pk], ["cs" + C + H], a1 - a0, bias=-0.5)
+        vgt("gc" + tag, cmp_[:, 16 * (ns + s0):752], ew, ll[:, ns + s0:47], dv[:, 16 * s0:16 * nv], ALU.is_gt,
+            ek + ["ll" + H, "dv" + H, "dw" + H, "dx" + H][:4 - s0], ["cv" + H, "cx" + H][:2 - s0], 16 * (nv - s0))
+        if s0:
+            vgt("gb" + tag, cmp_[:, 0:16], ew, ll[:, 0:1], dv[:, 0:16], ALU.is_gt, ek + ["ll" + H, "dx" + H], ["cx" + H], 16)
+        mm("cnt" + tag, [(pc[:, 0:47], T.usel[:, 15 - r:143 - r], cmp_[:, r:752:16], False, r == 15, 1) for r in range(16)],
+           ["usel", "cs0" + H, "cs1" + H, "cv" + H, "cx" + H, "pc" + H], ["pc" + H])
+        a_, ak = (T.am, "am") if k == 0 else (aa, "aa" + H)
+        scan("s" + tag, pc[:, 64:111], a_[:, 1:48], pc[:, 0:47], BIG, ALU.mult, ALU.max, [ak, "pc" + H], ["s" + H])
+        fm, fk = (fa[:, 2, 1:48], "dz" + H) if k == 0 else (fa[:, 3, 1:48], "fm" + H)
+        tt("g" + tag, fa[:, 4, 1:48], pc[:, 64:111], fm, ALU.max, ["s" + H, fk], ["g" + H])
+        if k == 0:
+            ts("k" + tag, kk[:, 0, 1:48], fa[:, 4, 1:48], 0.0, None, ALU.min, None, ["g" + H], ["k%s0" % H])
+        else:
+            scan("k" + tag, kk[:, k, 47:0:-1], mi[:, k - 1, 95:2:-2], fa[:, 4, 47:0:-1], 0.0, ALU.mult, ALU.min,
+                 ["g" + H, "m%s%d" % (H, k)], ["k%s%d" % (H, k)])
+        if k == 2:
+            return
+        mk, N = "m%s%d" % (H, k + 1), 811.0 * (k + 1)
+        ce, ck = (T.eps, "eps") if k == 0 else (T["ce" + H], "ce" + H)
+        scan("l" + tag, pc[:, 175:127:-1], ce[:, 47::-1], pc[:, 110:62:-1], 0.0, ALU.mult, ALU.min, ["s" + H, "s0" + H, ck], ["l" + H])
+        tt("m" + tag, mi[:, k, 1:96:2], pc[:, 128:176], a_[:], ALU.is_lt, ["l" + H, ak], [mk])
+        scan("sr" + tag, tb[:, 97:190:2], mi[:, k, 1:94:2], T.ni[:, k + 1, 0:47], -N, ALU.mult, ALU.min, [mk, "ni%d" % (k + 1)], ["sr" + H])
+        ts("lr" + tag, ll[:, 48:95], tb[:, 97:190:2], N, 0.0, ALU.add, ALU.max, ["sr" + H], ["lr" + H])
+        scan("sc" + tag, tb[:, 0:94], mi[:, k, 0:94], T["xy" + H][:, 0:94], 0.0, ALU.mult, ALU.add, [mk, "xy0" + H, "xy1" + H], ["sc" + H], 94)
+        ts("ll" + tag, ll[:, 0:47], tb[:, 1:94:2], N, 0.0, ALU.add, ALU.max, ["sc" + H], ["ll" + H])
+        act("a" + tag, aa[:], mi[:, k, 1:96:2], ACT.Identity, [mk], ["aa" + H], bias=-1.0, scale=2.0)
+        mm("fd" + tag, [(pf[:, 0:47], T.idf[:], fa[:, 2, 1:48], True, False, 4), (pf[:, 0:47], T.idc[:], aa[:, 1:48], False, False, 1),
+                        (pf[:, 0:47], T.idb[:], aa[:, 0:47], False, True, 1)], ["idf", "idb", "idc", "dz" + H, "aa" + H], ["pf" + H])
+        scan("f" + tag, fa[:, 3, 1:48], mi[:, k, 1:94:2], pf[:, 0:47], 2 * HALF, ALU.mult, ALU.add, [mk, "pf" + H], ["fm" + H])
+        if k == 0:
+            act("ce" + tag, T["ce" + H][:], mi[:, k, 1:96:2], ACT.Identity, [mk], ["ce" + H], bias=EPS, scale=1.0 - EPS)
+        else:
+            tt("ks" + tag, kk[:, 3, 1:48], kk[:, 0, 1:48], kk[:, 1, 1:48], ALU.add, ["k%s0" % H, "k%s1" % H], ["k%s3" % H], 94)
+            mm("bs" + tag, [(pf[:, 0:48], T.idf[:], fa[:, 1, :], True, False, 4), (pf[:, 0:48], T.idf[:], kk[:, 3, 0:48], False, False, 4),
+                            (pf[:, 0:48], T.idg[:], kk[:, 3, 1:49], False, True, 4)], ["idf", "idg", "zz" + H, "k%s3" % H], ["pf" + H])
+
+    def neighbours(r):
+        nb = [(r - 1, 0, 1)][:r] + [(r + 1, 3, 2)][:n - 1 - r]
+        out = []
+        for i, (q, s, t) in enumerate(nb):
+            e = topo.engines(T.cores[r], T.cores[q])
+            out.append((q, s, t, e[i * len(e) // len(nb):(i + 1) * len(e) // len(nb)]))
+        return out
+
+    def day_end(d, h):
+        H, tag, e0 = str(h), "%d%d" % (d, h), 4 * d
+        pf, kk, zi, pq, el, pl = [T[s + H] for s in ("pf", "kk", "zi", "pq", "el", "pl")]
+        o, X = h * HW, xk(d, h)
+        win = T["xw%d" % d][:, o:o + HW]
+        tt("z0" + tag, pf[:, 64:112], pf[:, 0:48], kk[:, 2, 0:48], ALU.add, ["pf" + H, "k%s2" % H], ["pf" + H])
+        tt("zi" + tag, zi[:], pf[:, 64:112], kk[:, 2, 1:49], ALU.subtract, ["pf" + H, "k%s2" % H], ["zi" + H])
+        ts("pq" + tag, pq[:], zi[:], 12, 0xFF0, ALU.logical_shift_right, ALU.bitwise_and, ["zi" + H], ["pq" + H])
+        ts("el" + tag, el[:, 0:4:2], pq[:, 0:48:47], T.rc[:, 0:1], None, ALU.add, None, ["pq" + H, "rc0"], ["el" + H])
+        ts("zq" + tag, zab[:, :, 0, h], zi[:], 65535, None, ALU.bitwise_and, None, ["zi" + H], ["z" + H])
+        numbers(h, zab[:, :, 0, h], ["z" + H], 3 if d == 0 else 7)
+        vgc("eh" + tag, ex[:, e0, 16 * h:16 * h + 16], win, el[:, 0:1], X + ["el" + H], ["ex%d_0%d" % (d, h)], 16)
+        vgc("ef" + tag, ex[:, e0 + 3, 16 * h:16 * h + 16], win, el[:, 2:3], X + ["el" + H], ["ex%d_3%d" % (d, h)], 16)
+        cp("ez" + tag, ex[:, e0:e0 + 4:3, 32 + h:38:2], zab[:, 0:48:47, :, h], ["z" + H, "ab" + H], ["exz" + tag])
+        if d == 0:
+            pv, ns = B - PERM_V, NS[(1, 0)]
+            ts("pl" + tag, pl[:], pq[:], T.rc[:, 0:1], None, ALU.add, None, ["pq" + H, "rc0"], ["pl" + H])
+            sgc("pa" + tag, T.xw1[:, o + 16:o + 16 + 16 * pv], win, pl[:, 0:pv], X + ["pl" + H], ["xa1" + H, "xh1" + H], 16 * pv)
+            vgc("pb" + tag, T.xw1[:, o + 16 + 16 * pv:o + HW], win, pl[:, pv:B], X + ["pl" + H], ["xb1" + H, "xf1" + H], 16 * PERM_V)
+            adjacent(1, h, ns + 2, 47, ["xa1" + H, "xb1" + H], ["dv" + H])
+            tt("ye" + H, T["fa" + H][:, 5, 0:ns], zab[:, 1:ns + 1, 2, h], zab[:, 2:ns + 2, 1, h], ALU.add, ["ab" + H], ["ye" + H], 2 * ns)
+            cp("le" + H, T["l2" + H][:, 0:ns], T["fa" + H][:, 5, 0:ns], ["ye" + H], ["l2" + H])
+        else:
+            ts("pl" + tag, T.nat[:, h:96:2], pq[:], T.rc[:, h:h + 1], None, ALU.add, None, ["pq" + H, "rc" + H], ["nat" + H])
+            cp("zf" + tag, T.zf[:, :, h], zab[:, :, 0, h], ["z" + H], ["zf" + H])
+
+    def meet(d):
+        e0, D = 4 * d, str(d)
+        md, mt, ms, uc, uw, cm, mc = T.md, T.mt, T.ms, T.uc, T.uw, T.cm, T.mc
+        own = ["ex%d_%d%d" % (d, s, h) for s in (0, 3) for h in range(2)] + ["exz%d0" % d, "exz%d1" % d]
+
+        def send():
+            tr = []
+            for q, s, t, es in neighbours(rank):
+                rid, pid = topo.addr(T.cores[q], core)
+                tr.append(RemoteDMATransfer(dst_ids=[DstId(rid=rid, pnc=pid)], dma_engine_mask=sum(1 << e for e in es),
+                                            remote_sem=T.sem["arr" + D], src=ex[:, e0 + s, :], dst=ex[:, e0 + t, :]))
+            return g.remote_dma_fused(tr, local_sem=T.sem.sent)
+        add("g", "send" + D, send, own, ["snd" + D], fix=500.0, kind="r")
+        ops[-1]["sent"] = sum(len(u[3]) for u in neighbours(rank))
+        add("x", "arr" + D, None, ["snd" + D], ["arr" + D], kind="a")
+        ops[-1]["tok"] = ("arr" + D, sum(len(v[3]) for u in neighbours(rank) for v in neighbours(u[0]) if v[0] == rank))
+        A = own + ["ex%d_%d0" % (d, s) for s in (1, 2)] + ["arr" + D]
+        ew, ek = ewin(EW if d == 0 else 2 * W)
+        tt("mc0" + D, ms[:], ex[:, e0:e0 + 2, 34:36], ex[:, e0 + 2:e0 + 4, 36:38], ALU.add, A, ["ms"])
+        ts("mc" + D, mc[:], ms[:], float(811 * 3 if d == 0 else 0), None, ALU.add, None, ["ms"], ["mc"])
+        tt("md" + D, md[:, :, 0:38], ex[:, e0 + 2:e0 + 4, 0:38], ex[:, e0:e0 + 2, 0:38], ALU.subtract, A, ["md"], 152)
+        vgt("m0" + D, cm[:, 0:32], ew, mc[:, 0:2], md[:, 0, 0:32], ALU.is_gt, ek + ["mc", "md"], ["cm0"], 32)
+        vgt("m1" + D, cm[:, 32:64], ew, mc[:, 2:4], md[:, 1, 0:32], ALU.is_le, ek + ["mc", "md"], ["cm1"], 32)
+        mm("mw" + D, [(T.pmw[:, 0:64], T.bo[:], cm[:], True, True, 1)], ["bo", "cm0", "cm1"], ["pmw"])
+        mm("mq" + D, [(T.pmc[:, 0:4], T.usel[:, 15 - r:143 - r], cm[:, r:64:16], r == 0, r == 15, 1) for r in range(16)], ["usel", "cm0", "cm1"], ["pmc"])
+        tt("uw" + D, uw[:], T.pmw[:, 0:64], T.thw[:], ALU.is_gt, ["pmw", "thw0", "thw1"], ["uw"])
+        tt("tx" + D, mt[:, :, 0:32], uw[:], md[:, :, 0:32], ALU.mult, ["uw", "md"], ["tx"], 128)
+        tt("uc" + D, uc[:], T.pmc[:, 0:4], T.thc[:], ALU.is_lt, ["pmc", "thc0", "thc1"], ["uc"])
+        for f in range(3 if d == 0 else 1):
+            tt("tz%d" % f + D, mt[:, :, 32 + 2 * f:34 + 2 * f], uc[:], md[:, :, 32 + 2 * f:34 + 2 * f], ALU.mult, ["uc", "md"], ["tz%d" % f])
+        if d == 0:
+            for h in range(2):
+                o, H = h * HW, str(h)
+                tt("nh" + H, T.xw1[:, o + 16:o + 32], mt[:, 0, 16 * h:16 * h + 16], ex[:, e0, 16 * h:16 * h + 16], ALU.add, ["tx"] + A, ["xh1" + H])
+                tt("nf" + H, T.xw1[:, o + HW - 16:o + HW], mt[:, 1, 16 * h:16 * h + 16], ex[:, e0 + 1, 16 * h:16 * h + 16], ALU.add, ["tx"] + A, ["xf1" + H])
+                adjacent(1, h, 47, 48, ["xa1" + H, "xb1" + H, "xf1" + H], ["dw" + H])
+                adjacent(1, h, 1, 2, ["xa1" + H, "xh1" + H], ["dx" + H])
+            tt("nz" + D, zab[:, 0:48:47, :, :], mt[:, :, 32:38], ex[:, e0:e0 + 2, 32:38], ALU.add, ["tz0", "tz1", "tz2"] + A, ["z0", "ab0", "z1", "ab1"])
+        else:
+            tt("nx" + D, T.ye[:], mt[:, :, 0:32], ex[:, e0:e0 + 2, 0:32], ALU.add, ["tx"] + A, ["ye"], 128)
+            tt("nz" + D, T.zf[:, 0:48:47, :], mt[:, :, 32:34], ex[:, e0:e0 + 2, 32:34], ALU.add, ["tz0"] + A, ["zf0", "zf1"])
+
+    cp("xw0", T.xw0[:, 16:HW], T.xn[:, :, 0, :], ["xn"], xk(0, 0)[1:], 384)
+    act("xw1", T.xw0[:, HW + 16:2 * HW], T.xn[:, :, 1, :], ACT.Identity, ["xn"], xk(0, 1)[1:], 768)
+    for h in range(2):
+        numbers(h, T.bt[:, :, h], ["bt"], 0)
+        adjacent(0, h, NS[(0, 0)] + 1, 48, xk(0, h), [s + str(h) for s in ("dv", "dw", "dx")])
+    for d in range(2):
+        for h in range(2):
+            day_start(d, h)
+        for k in range(3):
+            for h in range(2):
+                interval(d, k, h)
+        for h in range(2):
+            day_end(d, h)
+        meet(d)
+    X, c1 = xk(1, 0) + xk(1, 1) + ["nat0", "nat1"], 2 + FIN_V
+    vgc("fv", T.ys[:, 32:16 * c1], T.xw1[:, 0:2 * HW], T.nat[:, 2:c1], X, ["ysv"], 16 * FIN_V)
+    sgc("fs", T.ys[:, 16 * c1:1504], T.xw1[:, 0:2 * HW], T.nat[:, c1:94], X, ["yss"], 1504 - 16 * c1)
+    dma("y", "st_v", T.yx[:, 32:16 * c1], T.ys[:, 32:16 * c1], ["ysv"], ["o0"], 4096 * FIN_V, False)
+    dma("s", "st_s", T.yx[:, 16 * c1:1504], T.ys[:, 16 * c1:1504], ["yss"], ["o1"], 256 * (1504 - 16 * c1))
+    dma("y", "st_h", T.yx[:, 0:32], T.ye[:, 0, :], ["ye"], ["o2"], 8192, False)
+    dma("s", "st_f", T.yx[:, 1504:1536], T.ye[:, 1, :], ["ye"], ["o3"], 8192, False)
+    dma("y", "st_b", T.yb[:], T.zf[:], ["zf0", "zf1"], ["o4"], 49152, False)
+    return ops
+
+
+def depend(ops):
+    lastw, readers = {}, {}
+    for i, o in enumerate(ops):
+        dep = set(lastw[k] for k in o["r"] + o["w"] if k in lastw)
+        for k in o["w"]:
+            dep.update(readers.get(k, []))
+        o["dep"] = sorted(dep - {i})
+        for k in o["r"]:
+            readers.setdefault(k, []).append(i)
+        for k in o["w"]:
+            lastw[k], readers[k] = i, []
+
+
+def times(o, m):
+    fix, cyc, gat, pe, byt = o["cost"]
+    busy = fix + m["f"] * (0.83 * (cyc + m["g"] * gat) + m["pe"] * pe)
+    return busy, (m["dma"] + byt / m["bw"] if o["kind"] == "d" else m["rem"] if o["kind"] == "a" else busy)
+
+
+def order(ops):
+    n, seed = len(ops), [12345]
+    dep = [o["dep"] for o in ops]
+    en = ["vspgyx".index(o["eng"]) for o in ops]
+    succ = [set() for o in ops]
+    for i in range(n):
+        for j in dep[i]:
+            succ[j].add(i)
+    tms = [[times(o, m) for o in ops] for m in MODELS]
+
+    def rnd():
+        seed[0] = (seed[0] * 1103515245 + 12345) % 2147483648
+        return seed[0] / 2147483648.0
+
+    def length(seq):
+        tot = 0.0
+        for tm, m in zip(tms, MODELS):
+            free, end = [0.0] * 6, [0.0] * n
+            for i in seq:
+                st = free[en[i]]
+                for j in dep[i]:
+                    if end[j] > st:
+                        st = end[j]
+                free[en[i]] = st + tm[i][0]
+                end[i] = st + tm[i][1] + m["wake"]
+            tot += max(end)
+        return tot
+
+    best = None
+    for t in range(TRIES):
+        m, tm = MODELS[t % len(MODELS)], tms[t % len(MODELS)]
+        noise, slack, bias = 400.0 * rnd(), 30.0 + 250.0 * rnd(), 2500.0 * rnd()
+        pri = [0.0] * n
+        for i in range(n - 1, -1, -1):
+            pri[i] = tm[i][1] + max([m["wake"] + pri[j] for j in succ[i]] + [0.0])
+        pri = [p + noise * rnd() + bias * (ops[i]["name"][-1] == "0") for i, p in enumerate(pri)]
+        left, rel, free, seq = [len(d) for d in dep], [0.0] * n, [0.0] * 6, []
+        ready = [i for i in range(n) if not dep[i]]
+        while ready:
+            first = [i for i in ready if ops[i]["early"]]
+            est = {i: max(free[en[i]], rel[i]) for i in ready}
+            b = min(ready, key=lambda i: (est[i], -pri[i], i))
+            b = min(first) if first else min([i for i in ready if en[i] == en[b] and est[i] <= est[b] + slack], key=lambda i: (-pri[i], i))
+            free[en[b]] = est[b] + tm[b][0]
+            ready.remove(b)
+            seq.append(b)
+            for j in succ[b]:
+                rel[j] = max(rel[j], est[b] + tm[b][1] + m["wake"])
+                left[j] -= 1
+                if left[j] == 0:
+                    ready.append(j)
+        v = length(seq)
+        if best is None or v < best[0]:
+            best = (v, seq)
+    c, cur = best
+    n0 = sum(o["early"] for o in ops)
+    for it in range(MOVES):
+        p, k, d = n0 + int(rnd() * (n - n0)), (1, 1, 1, 2, 3)[int(rnd() * 5)], (-1, 1)[int(rnd() * 2)]
+        i, q = cur[p], p
+        while k and n0 <= q + d < n:
+            q += d
+            k -= en[cur[q]] == en[i]
+        if k:
+            continue
+        lo, hi = min(p, q), max(p, q)
+        seg, tied = cur[lo:hi + 1], {i}
+        for x in (seg[-2::-1] if d < 0 else seg[1:]):
+            if tied.intersection(succ[x] if d < 0 else dep[x]):
+                tied.add(x)
+        if cur[q] in tied:
+            continue
+        a, b = [x for x in seg if x in tied], [x for x in seg if x not in tied]
+        new = cur[:lo] + (a + b if d < 0 else b + a) + cur[hi + 1:]
+        v = length(new)
+        if v < c or rnd() < math.exp((c - v) / (150.0 * (1.0 - it / MOVES) + 3.0)):
+            c, cur = v, new
+            if c < best[0]:
+                best = (c, cur)
+    return best[1]
+
+
+def emit(g, T, ops, seq):
+    queue = {"v": g.vector, "s": g.scalar, "p": g.tensor, "g": g, "y": g.sync}
+    known, total, nd = {q: {} for q in queue}, {}, 0
+    for i in seq:
+        o = ops[i]
+        if o["kind"] == "a":
+            o["clock"] = dict([o["tok"]])
+            total.update(o["clock"])
+            continue
+        q, kn = queue[o["eng"]], known[o["eng"]]
+        need = [ops[j] for j in o["dep"] if kn.get(ops[j]["tok"][0], 0) < ops[j]["tok"][1]]
+        for p in [p for p in need if not any(u is not p and u["clock"].get(p["tok"][0], 0) >= p["tok"][1] for u in need)]:
+            q.wait_ge(T.sem[p["tok"][0]], p["tok"][1])
+            for s, c in p["clock"].items():
+                kn[s] = max(kn.get(s, 0), c)
+        ins = o["fn"]()
+        if o["kind"] == "r":
+            total["sent"] = total.get("sent", 0) + o["sent"]
+            continue
+        s, inc = ("dma%d" % nd, 16) if o["kind"] == "d" else ("q" + o["eng"], 1)
+        nd += o["kind"] == "d"
+        ins.then_inc(T.sem[s], inc)
+        total[s] = total.get(s, 0) + inc
+        o["tok"], o["clock"] = (s, total[s]), dict(kn, **{s: total[s]})
+    for s in sorted(total):
+        g.wait_ge(T.sem[s], total[s])
+
+
+ORDER = []
+
+
+def rank_program(g, core, T, topo):
+    rank = T.rank_of(core)
+    if rank is None:
+        return
+    ops = build(g, core, T, topo, rank)
+    common = [o for o in ops if not o["extra"]]
+    if not ORDER:
+        depend(common)
+        ORDER.extend(order(common))
+    depend(ops)
+    index = [i for i, o in enumerate(ops) if not o["extra"]]
+    emit(g, T, ops, [i for i, o in enumerate(ops) if o["extra"]] + [index[i] for i in ORDER])

@@ -6,15 +6,16 @@ B, V, W = 48, 1536, 4096
 HW = 16 + 16 * B
 EW = 10624
 BIG, HALF, EPS = 2.0 ** 24, 2.0 ** 21, 2.0 ** -19
-NS = {(0, 0): 28, (0, 1): 24, (0, 2): 22, (1, 0): 31, (1, 1): 24, (1, 2): 22}
+NS = {(0, 0): 28, (0, 1): 24, (0, 2): 22, (1, 0): 28, (1, 1): 24, (1, 2): 22}
 NO = min(NS.values())
 PERM_V = 8
 FIN_V = 44
 ENC_CP = ["v", "s", "v", None]
-TRIES, MOVES = 24, 60000
-MODELS = [dict(f=1.2, g=1.56, wake=60.0, pe=0.42, dma=2000.0, bw=250.0, rem=2500.0),
-          dict(f=1.1, g=1.2, wake=120.0, pe=0.42, dma=1700.0, bw=300.0, rem=3500.0),
-          dict(f=1.3, g=1.9, wake=30.0, pe=0.5, dma=2300.0, bw=200.0, rem=2000.0)]
+TRIES, MOVES = 24, 110000
+MODELS = [dict(f=1.05, g=1.56, wake=170.0, pe=0.42, dma=2200.0, bw=230.0, rem=3000.0),
+          dict(f=1.15, g=1.5, wake=130.0, pe=0.42, dma=1500.0, bw=400.0, rem=3500.0),
+          dict(f=1.1, g=1.3, wake=100.0, pe=0.55, dma=2500.0, bw=200.0, rem=4000.0),
+          dict(f=1.35, g=1.8, wake=180.0, pe=0.42, dma=1800.0, bw=300.0, rem=3500.0)]
 
 BF, F, I, U = "bfloat16", "float32", "int32", "uint16"
 SCRATCH = {"pmw": ("psum", [128, 512], F), "pmc": ("psum", [128, 512], F)}
@@ -30,7 +31,7 @@ for _n, _s, _t in (
 for _h in "01":
     for _n, _s, _t in (
             ("cmp", [752], BF), ("dv", [752], BF), ("eg", [752], BF), ("xr", [752], BF), ("xo", [2, 16 * (47 - NO)], BF), ("ll", [96], U),
-            ("l2", [B], U), ("pl", [B], U), ("el", [4], U), ("raw", [B, 2], I), ("ci", [2, B], I), ("zi", [B], I), ("pq", [B], I),
+            ("l2", [B], U), ("pl", [B], U), ("el", [4], U), ("raw", [B, 2], I), ("ci", [3, B], I), ("zi", [B], I), ("pq", [B], I),
             ("xy", [96], F), ("tt", [192], F), ("mi", [2, 96], F), ("kk", [4, 52], F), ("fa", [6, B], F), ("aa", [B], BF), ("ce", [B], F)):
         SCRATCH[_n + _h] = ("sbuf", [128] + _s, _t)
     for _n in ("ps", "pc", "pf"):
@@ -94,9 +95,9 @@ def build(g, core, T, topo, rank):
         dma("y", "ld_enc", T.encw[:, Q * i:Q * i + Q], T.enc[:, Q * i:Q * i + Q], [], ["e%d" % i], Q * 256)
     for i, who in enumerate(ENC_CP):
         if who is None:
-            dma("y", "ld_rep", T.encw[:, W + Q * i:W + Q * i + Q], T.enc[:, Q * i:Q * i + Q], [], ["f%d" % i], Q * 256)
+            dma("y", "ld_rep", T.encw[:, W + Q * i:W + Q * i + Q], T.enc[:, Q * i:Q * i + Q], ["e2"], ["f%d" % i], Q * 256, False)
     for i, (a, b_) in enumerate(((2 * W, 9008), (9008, EW))):
-        dma("y", "ld_tail", T.encw[:, a:b_], T.enc[:, a - 2 * W:b_ - 2 * W], [], ["t%d" % i], (b_ - a) * 256)
+        dma("y", "ld_tail", T.encw[:, a:b_], T.enc[:, a - 2 * W:b_ - 2 * W], ["e2"], ["t%d" % i], (b_ - a) * 256)
 
     def ewin(end):
         return T.encw[:, 0:end], [k for (a, k) in ekeys if a < end]
@@ -118,21 +119,24 @@ def build(g, core, T, topo, rank):
         key = (k == 0, ns, int((d, k) == (1, 0)))
         if key not in kaps:
             i = kaps[key] = len(kaps)
-            mset("kap", T.kap[:, i, :], 4.5 / 16 - key[0], ["kap%d" % i])
-            mset("kap", T.kap[:, i, key[2]:ns + key[2]], 9.0 / 16 - key[0], ["kap%d" % i])
+            mset("kap", T.kap[:, i, ns + key[2]:B], 4.5 / 16 - key[0], ["kap%d" % i])
+            mset("kap", T.kap[:, i, key[2]:ns + key[2]], 9.0 / 16 - key[0], ["kas%d" % i])
+            if key[2]:
+                mset("kap", T.kap[:, i, 0:1], 4.5 / 16 - key[0], ["kao"])
+    early[0] = False
     up, down = rank > 0, rank < n - 1
     for e, t in enumerate((11.5 if up else 1000.0, 4.5 if down else -1000.0)):
         mset("thw", T.thw[:, 32 * e:32 * e + 32], t, ["thw%d" % e])
         mset("thc", T.thc[:, 2 * e:2 * e + 2], -t * BIG, ["thc%d" % e])
     for d in range(2):
-        for s in [0, 3] + ([] if down else [1]) + ([] if up else [2]):
-            mset("ex", T.ex[:, 4 * d + s, :], 0.0, ["ex%d_%d%d" % (d, s, h) for h in range(2)] + ["exz%d%d" % (d, h) for h in range(2) if s in (0, 3)])
-            ops[-1]["extra"] = s in (1, 2)
+        for s in ([] if down else [1]) + ([] if up else [2]):
+            mset("ex", T.ex[:, 4 * d + s, :], 0.0, ["ex%d_%d%d" % (d, s, h) for h in range(2)])
+            ops[-1]["extra"] = True
         for h in range(2):
             mset("sent", T["xw%d" % d][:, h * HW:h * HW + 16], 255.0, ["sn%d%d" % (d, h)])
     for H in "01":
-        mset("mi", T["mi" + H][:], 1.0, ["m%s1" % H, "m%s2" % H], 192)
-        mset("kk", T["kk" + H][:], 0.0, ["k%s%d" % (H, i) for i in range(4)], 208)
+        mset("mi", T["mi" + H][:, :, 0:96:2], 1.0, ["m%s1" % H, "m%s2" % H], 96)
+        mset("kk", T["kk" + H][:, :, 0:49:48], 0.0, ["k%s%d" % (H, i) for i in range(4)])
         mset("sh", T["pc" + H][:, 63:64], BIG, ["s0" + H, "pc" + H])
     for nm, val in (("idn", -1.0), ("idw", -16.0 * BIG), ("idb", -HALF), ("idc", HALF), ("idf", 1.0), ("idg", -1.0)):
         act(nm, T[nm][:], T.idp[:], ACT.Identity, ["idp"], [nm], 128, scale=val)
@@ -143,7 +147,6 @@ def build(g, core, T, topo, rank):
     ts("ni", T.ni[:, 0, :], T.bi[:], 16.0, T.rc[:, 0:1], ALU.mult, ALU.add, ["bi", "rc0"], ["ni0"])
     for k in (1, 2):
         ts("ni", T.ni[:, k, :], T.ni[:, 0, :], -811.0 * k, None, ALU.add, None, ["ni0"], ["ni%d" % k])
-    early[0] = False
     for i, who in enumerate(ENC_CP):
         o, s = T.encw[:, W + Q * i:W + Q * i + Q], T.encw[:, Q * i:Q * i + Q]
         if who == "v":
@@ -197,13 +200,13 @@ def build(g, core, T, topo, rank):
         XS, ls, lk = (X[1:3], T["l2" + H], "l2" + H) if s0 else (X, ll, "ll" + H)
         ka = kaps[(k == 0, ns, s0)]
         mm("cn0" + tag, [(pc[:, 0:47], T.idw[:], T.kap[:, ka, 0:47], True, False, 1)] + [(pc[:, 0:47], T.idw[:], aa[:, 1:48], False, False, 1)][:k],
-           ["idw", "kap%d" % ka] + ["aa" + H][:k], ["pc" + H, "s" + H, "l" + H])
+           ["idw", "kap%d" % ka, "kas%d" % ka, "kao"] + ["aa" + H][:k], ["pc" + H, "s" + H, "l" + H])
         if k > 0:
             sgc("gx" + tag, xr[:, 0:16 * ns], win, ll[:, 48:48 + ns], X + ["lr" + H], ["xr" + H], 16 * ns)
             vgt("gd" + tag, dv[:, 0:16 * nv], win, ll[:, 48 + ns:95], T["xo" + H][:, d, 16 * (ns - NO):16 * (47 - NO)], ALU.subtract,
                 X + ["lr" + H, "xo%d" % d + H], ["dv" + H, "dw" + H, "dx" + H], 16 * nv)
         n1 = ns * 5 // 16 * 2
-        for C, u0, u1, pp, pk in (("0", 0, n1, ps, "ps" + H), ("1", n1, ns, (T.pmw, T.pmc)[h], ("pmw", "pmc")[h])):
+        for C, u0, u1, pp, pk in (("0", 0, n1, ps, "ps" + H), ("1", n1, ns, pf if s0 else (T.pmw, T.pmc)[h], "pf" + H if s0 else ("pmw", "pmc")[h])):
             a0, a1 = 16 * u0, 16 * u1
             c0, out = o + 16 + 16 * s0, pp[:, 0:a1 - a0]
             mm("su0" + C + tag, [(out, T.idp[:], xw[:, c0 + 16 + a0:c0 + 16 + a1], True, False, 1),
@@ -212,12 +215,15 @@ def build(g, core, T, topo, rank):
             sgc("ge" + C + tag, eg[:, a0:a1], ew, ls[:, u0:u1], ek + [lk], ["eg" + C + H], a1 - a0)
             mm("su1" + C + tag, [(out, T.idp[:], eg[:, a0:a1], False, True, 1)], ["eg" + C + H, "idp", pk], [pk])
             act("sg" + C + tag, cmp_[:, 16 * s0 + a0:16 * s0 + a1], out, ACT.Sign, [pk], ["cs" + C + H], a1 - a0, bias=-0.5)
-        vgt("gc" + tag, cmp_[:, 16 * (ns + s0):752], ew, ll[:, ns + s0:47], dv[:, 16 * s0:16 * nv], ALU.is_gt,
-            ek + ["ll" + H, "dv" + H, "dw" + H, "dx" + H][:4 - s0], ["cv" + H, "cx" + H][:2 - s0], 16 * (nv - s0))
-        if s0:
+        if not s0:
+            vgt("gc" + tag, cmp_[:, 16 * ns:752], ew, ll[:, ns:47], dv[:, 0:16 * nv], ALU.is_gt,
+                ek + ["ll" + H, "dv" + H, "dw" + H, "dx" + H], ["cv" + H, "cx" + H, "cy" + H], 16 * nv)
+        else:
+            vgt("gc" + tag, cmp_[:, 16 * ns + 16:736], ew, ls[:, ns:45], dv[:, 16:16 * nv - 16], ALU.is_gt, ek + [lk, "dv" + H], ["cv" + H], 16 * nv - 32)
+            vgt("gz" + tag, cmp_[:, 736:752], ew, ll[:, 46:47], dv[:, 16 * nv - 16:16 * nv], ALU.is_gt, ek + ["ll" + H, "dw" + H], ["cy" + H], 16)
             vgt("gb" + tag, cmp_[:, 0:16], ew, ll[:, 0:1], dv[:, 0:16], ALU.is_gt, ek + ["ll" + H, "dx" + H], ["cx" + H], 16)
         mm("cnt" + tag, [(pc[:, 0:47], T.usel[:, 15 - r:143 - r], cmp_[:, r:752:16], False, r == 15, 1) for r in range(16)],
-           ["usel", "cs0" + H, "cs1" + H, "cv" + H, "cx" + H, "pc" + H], ["pc" + H])
+           ["usel", "cs0" + H, "cs1" + H, "cv" + H, "cx" + H, "cy" + H, "pc" + H], ["pc" + H])
         a_, ak = (T.am, "am") if k == 0 else (aa, "aa" + H)
         scan("s" + tag, pc[:, 64:111], a_[:, 1:48], pc[:, 0:47], BIG, ALU.mult, ALU.max, [ak, "pc" + H], ["s" + H])
         fm, fk = (fa[:, 2, 1:48], "dz" + H) if k == 0 else (fa[:, 3, 1:48], "fm" + H)
@@ -276,8 +282,8 @@ def build(g, core, T, topo, rank):
             sgc("pa" + tag, T.xw1[:, o + 16:o + 16 + 16 * pv], win, pl[:, 0:pv], X + ["pl" + H], ["xa1" + H, "xh1" + H], 16 * pv)
             vgc("pb" + tag, T.xw1[:, o + 16 + 16 * pv:o + HW], win, pl[:, pv:B], X + ["pl" + H], ["xb1" + H, "xf1" + H], 16 * PERM_V)
             adjacent(1, h, ns + 2, 47, ["xa1" + H, "xb1" + H], ["dv" + H])
-            tt("ye" + H, T["fa" + H][:, 5, 0:ns], zab[:, 1:ns + 1, 2, h], zab[:, 2:ns + 2, 1, h], ALU.add, ["ab" + H], ["ye" + H], 2 * ns)
-            cp("le" + H, T["l2" + H][:, 0:ns], T["fa" + H][:, 5, 0:ns], ["ye" + H], ["l2" + H])
+            tt("ye" + H, T["fa" + H][:, 5, 0:45], zab[:, 1:46, 2, h], zab[:, 2:47, 1, h], ALU.add, ["ab" + H], ["ye" + H], 90)
+            cp("le" + H, T["l2" + H][:, 0:45], T["fa" + H][:, 5, 0:45], ["ye" + H], ["l2" + H])
         else:
             ts("pl" + tag, T.nat[:, h:96:2], pq[:], T.rc[:, h:h + 1], None, ALU.add, None, ["pq" + H, "rc" + H], ["nat" + H])
             cp("zf" + tag, T.zf[:, :, h], zab[:, :, 0, h], ["z" + H], ["zf" + H])
@@ -292,7 +298,7 @@ def build(g, core, T, topo, rank):
             for q, s, t, es in neighbours(rank):
                 rid, pid = topo.addr(T.cores[q], core)
                 tr.append(RemoteDMATransfer(dst_ids=[DstId(rid=rid, pnc=pid)], dma_engine_mask=sum(1 << e for e in es),
-                                            remote_sem=T.sem["arr" + D], src=ex[:, e0 + s, :], dst=ex[:, e0 + t, :]))
+                                            remote_sem=T.sem["arr" + D], src=ex[:, e0 + s, 0:38], dst=ex[:, e0 + t, 0:38]))
             return g.remote_dma_fused(tr, local_sem=T.sem.sent)
         add("g", "send" + D, send, own, ["snd" + D], fix=500.0, kind="r")
         ops[-1]["sent"] = sum(len(u[3]) for u in neighbours(rank))
@@ -442,7 +448,7 @@ def order(ops):
         a, b = [x for x in seg if x in tied], [x for x in seg if x not in tied]
         new = cur[:lo] + (a + b if d < 0 else b + a) + cur[hi + 1:]
         v = length(new)
-        if v < c or rnd() < math.exp((c - v) / (150.0 * (1.0 - it / MOVES) + 3.0)):
+        if v < c or rnd() < math.exp((c - v) / (170.0 * (1.0 - it / MOVES) + 3.0)):
             c, cur = v, new
             if c < best[0]:
                 best = (c, cur)

@@ -5,39 +5,39 @@ from concourse.mybir import AluOpType as ALU, ActivationFunctionType as ACT
 B, V, W = 48, 1536, 4096
 HW = 16 + 16 * B
 EW = 10624
-BIG, HALF, EPS = 2.0 ** 24, 2.0 ** 21, 2.0 ** -19
-NS = {(0, 0): 28, (0, 1): 24, (0, 2): 22, (1, 0): 28, (1, 1): 24, (1, 2): 22}
+BIG, HALF, EPS = 2.0 ** 28, 2.0 ** 21, 2.0 ** -17
+SPLIT = 0.6
+NS = {(0, 0): 28, (0, 1): 24, (0, 2): 22, (1, 0): 36, (1, 1): 24, (1, 2): 22}
 NO = min(NS.values())
 PERM_V = 8
 FIN_V = 44
 ENC_CP = ["v", "s", "v", None]
-TRIES, MOVES = 24, 110000
-MODELS = [dict(f=1.05, g=1.56, wake=170.0, pe=0.42, dma=2200.0, bw=230.0, rem=3000.0),
-          dict(f=1.15, g=1.5, wake=130.0, pe=0.42, dma=1500.0, bw=400.0, rem=3500.0),
-          dict(f=1.1, g=1.3, wake=100.0, pe=0.55, dma=2500.0, bw=200.0, rem=4000.0),
-          dict(f=1.35, g=1.8, wake=180.0, pe=0.42, dma=1800.0, bw=300.0, rem=3500.0)]
+TRIES, STARTS, MOVES = 24, 7, 40000
+MODELS = [dict(f=1.0, g=1.56, wake=200.0, pe=0.42, dma=1200.0, bw=300.0, rem=1000.0),
+          dict(f=1.15, g=1.4, wake=170.0, pe=0.42, dma=1500.0, bw=250.0, rem=1800.0),
+          dict(f=1.3, g=1.8, wake=220.0, pe=0.42, dma=1300.0, bw=300.0, rem=1500.0)]
 
 BF, F, I, U = "bfloat16", "float32", "int32", "uint16"
 SCRATCH = {"pmw": ("psum", [128, 512], F), "pmc": ("psum", [128, 512], F)}
 for _n, _s, _t in (
         ("xn", [B, 2, 16], BF), ("bt", [B, 2], I), ("encw", [EW], BF), ("xw0", [2 * HW], BF), ("xw1", [2 * HW], BF), ("ys", [V], BF),
-        ("ye", [2, 32], BF), ("zf", [B, 2], F), ("nat", [96], U), ("ones", [128], BF), ("tmpb", [128], BF), ("idp", [128], BF),
+        ("ye", [64], BF), ("zf", [B, 2], F), ("nat", [96], U), ("ones", [128], BF), ("idp", [128], BF),
         ("idn", [128], BF), ("idw", [128], BF), ("idb", [128], BF), ("idc", [128], BF), ("idf", [128], F), ("idg", [128], F),
-        ("bo", [128], BF), ("usel", [144], BF), ("w8", [8], BF), ("t8", [8], BF), ("pi", [2], I), ("rc", [4], F), ("bi", [B], F),
-        ("bc", [B], F), ("ni", [3, B], F), ("kap", [6, B], BF), ("am", [B], BF), ("eps", [B], F), ("thw", [64], F), ("thc", [4], F),
-        ("ex", [8, 40], F), ("zab", [B, 3, 2], I), ("mc", [4], U), ("md", [2, 40], F), ("mt", [2, 40], F), ("ms", [2, 2], F),
-        ("uc", [2, 2], F), ("uw", [2, 32], F), ("cm", [64], BF)):
+        ("usel", [144], BF), ("w8", [8], BF), ("t8", [8], BF), ("pi", [2], I), ("rc", [4], F), ("bi", [B], F), ("bc", [B], F),
+        ("nn", [2, 96], F), ("idh", [128], BF), ("idi", [128], BF), ("kap", [6, B], BF), ("am", [B], BF), ("eps", [B], F),
+        ("thm", [2], BF), ("zab", [B, 3, 2], I)):
     SCRATCH[_n] = ("sbuf", [128] + _s, _t)
 for _h in "01":
     for _n, _s, _t in (
             ("cmp", [752], BF), ("dv", [752], BF), ("eg", [752], BF), ("xr", [752], BF), ("xo", [2, 16 * (47 - NO)], BF), ("ll", [96], U),
-            ("l2", [B], U), ("pl", [B], U), ("el", [4], U), ("raw", [B, 2], I), ("ci", [3, B], I), ("zi", [B], I), ("pq", [B], I),
-            ("xy", [96], F), ("tt", [192], F), ("mi", [2, 96], F), ("kk", [4, 52], F), ("fa", [6, B], F), ("aa", [B], BF), ("ce", [B], F)):
+            ("l2", [B], U), ("pl", [B], U), ("raw", [B, 2], I), ("ci", [3, B], I), ("zi", [B], I), ("pq", [B], I),
+            ("xy", [96], F), ("lv", [96], F), ("tt", [192], F), ("mi", [2, 96], F), ("kk", [4, 52], F), ("fa", [6, B], F), ("aa", [B], BF), ("ce", [B], F),
+            ("el", [4], U), ("ex", [4, 48], F), ("md", [2, 24], F), ("cm", [32], BF), ("mc", [8], U), ("uc", [4], F), ("ne", [48], F)):
         SCRATCH[_n + _h] = ("sbuf", [128] + _s, _t)
     for _n in ("ps", "pc", "pf"):
         SCRATCH[_n + _h] = ("psum", [128, 512], F)
 
-SEMAPHORES = ["qv", "qs", "qp", "qg", "sent", "arr0", "arr1"] + ["dma%d" % i for i in range(20)]
+SEMAPHORES = ["qv", "qs", "qp", "qg", "sent", "arr00", "arr01", "arr10", "arr11"] + ["dma%d" % i for i in range(20)]
 
 
 def build(g, core, T, topo, rank):
@@ -110,8 +110,6 @@ def build(g, core, T, topo, rank):
     gp("bi", lambda: g.iota(T.bi[:], [[1, B]], 0, 0, allow_small_or_imprecise_dtypes=True), [], ["bi"], B)
     gp("t8", lambda: g.affine_select(T.t8[:], T.w8[:], [[-16, 8]], ALU.is_ge, 0.0, 0, 1), ["w8"], ["t8"], 8)
     gp("usel", lambda: g.affine_select(T.usel[:, 15:143:16], T.t8[:], [[16, 8]], ALU.is_ge, 0.0, 15, -1), ["t8"], ["usel"], 8)
-    gp("bo", lambda: g.affine_select(T.tmpb[:], T.ones[:], [[-16, 8], [0, 16]], ALU.is_ge, 0.0, 0, 1), ["ones"], ["tmpb"], 128)
-    gp("bo", lambda: g.affine_select(T.bo[:], T.tmpb[:], [[16, 8], [0, 16]], ALU.is_ge, 0.0, 15, -1), ["tmpb"], ["bo"], 128)
     mset("am", T.am[:], -1.0, ["am"])
     mset("eps", T.eps[:], EPS, ["eps"])
     kaps = {}
@@ -126,27 +124,30 @@ def build(g, core, T, topo, rank):
     early[0] = False
     up, down = rank > 0, rank < n - 1
     for e, t in enumerate((11.5 if up else 1000.0, 4.5 if down else -1000.0)):
-        mset("thw", T.thw[:, 32 * e:32 * e + 32], t, ["thw%d" % e])
-        mset("thc", T.thc[:, 2 * e:2 * e + 2], -t * BIG, ["thc%d" % e])
+        mset("thm", T.thm[:, e:e + 1], -t / 16, ["thm%d" % e])
     for d in range(2):
-        for s in ([] if down else [1]) + ([] if up else [2]):
-            mset("ex", T.ex[:, 4 * d + s, :], 0.0, ["ex%d_%d%d" % (d, s, h) for h in range(2)])
-            ops[-1]["extra"] = True
         for h in range(2):
             mset("sent", T["xw%d" % d][:, h * HW:h * HW + 16], 255.0, ["sn%d%d" % (d, h)])
     for H in "01":
+        for e in ([] if down else [1]) + ([] if up else [0]):
+            mset("ex", T["ex" + H][:, e:4:2, 24 * e:24 * e + 24], 0.0, ["exz0" + H, "exz1" + H])
+            ops[-1]["extra"] = True
+        for e in range(2):
+            mset("pad", T["ex" + H][:, e:4:2, 43 - 24 * e:48 - 24 * e], 0.0, ["pad" + H])
         mset("mi", T["mi" + H][:, :, 0:96:2], 1.0, ["m%s1" % H, "m%s2" % H], 96)
-        mset("kk", T["kk" + H][:, :, 0:49:48], 0.0, ["k%s%d" % (H, i) for i in range(4)])
+        mset("kk", T["kk" + H][:, :, 0:49:48], 0.0, ["k%s%d" % (H, i) for i in range(3)])
         mset("sh", T["pc" + H][:, 63:64], BIG, ["s0" + H, "pc" + H])
-    for nm, val in (("idn", -1.0), ("idw", -16.0 * BIG), ("idb", -HALF), ("idc", HALF), ("idf", 1.0), ("idg", -1.0)):
+        mset("lo", T["lv" + H][:, 1:96:2], -BIG, ["lo" + H])
+    for nm, val in (("idn", -1.0), ("idw", -16.0 * BIG), ("idb", -HALF), ("idc", HALF), ("idf", 1.0), ("idg", -1.0), ("idh", 2048.0), ("idi", -2048.0)):
         act(nm, T[nm][:], T.idp[:], ACT.Identity, ["idp"], [nm], 128, scale=val)
     ts("r", T.pi[:, 1:2], T.pi[:, 0:1], 15, None, ALU.bitwise_and, None, ["pi0"], ["pi1"])
-    for h in range(2):
-        ts("rc", T.rc[:, h:h + 1], T.pi[:, 1:2], 16.0 + HW * h, None, ALU.add, None, ["pi1"], ["rc%d" % h])
+    for i, c in enumerate((16.0, 16.0 + HW, 0.0, 24.0)):
+        ts("rc", T.rc[:, i:i + 1], T.pi[:, 1:2], c, None, ALU.add, None, ["pi1"], ["rc%d" % i])
     ts("bc", T.bc[:], T.bi[:], 65536.0, None, ALU.mult, None, ["bi"], ["bc"])
-    ts("ni", T.ni[:, 0, :], T.bi[:], 16.0, T.rc[:, 0:1], ALU.mult, ALU.add, ["bi", "rc0"], ["ni0"])
-    for k in (1, 2):
-        ts("ni", T.ni[:, k, :], T.ni[:, 0, :], -811.0 * k, None, ALU.add, None, ["ni0"], ["ni%d" % k])
+    ts("ni", T.nn[:, 0, 1:96:2], T.bi[:], 16.0, T.rc[:, 0:1], ALU.mult, ALU.add, ["bi", "rc0"], ["ni"])
+    act("ni", T.nn[:, 0, 0:96:2], T.nn[:, 0, 1:96:2], ACT.Identity, ["ni"], ["nn0"], scale=-1.0)
+    act("ni", T.nn[:, 1, 0:96:2], T.nn[:, 0, 1:96:2], ACT.Identity, ["ni"], ["nj"], scale=-1.0, bias=2048.0)
+    act("ni", T.nn[:, 1, 1:96:2], T.nn[:, 1, 0:96:2], ACT.Identity, ["nj"], ["nn1"], scale=-1.0)
     for i, who in enumerate(ENC_CP):
         o, s = T.encw[:, W + Q * i:W + Q * i + Q], T.encw[:, Q * i:Q * i + Q]
         if who == "v":
@@ -154,7 +155,7 @@ def build(g, core, T, topo, rank):
         elif who == "s":
             act("rep", o, s, ACT.Identity, ["e%d" % i], ["f%d" % i], Q)
 
-    zab, ex = T.zab, T.ex
+    zab = T.zab
 
     def xk(d, h):
         return [s + "%d%d" % (d, h) for s in ("sn", "xa", "xb", "xh", "xf")]
@@ -168,17 +169,17 @@ def build(g, core, T, topo, rank):
     def day_start(d, h):
         H = str(h)
         xy, fa, ci, ll = T["xy" + H], T["fa" + H], T["ci" + H], T["ll" + H]
-        z, zk = (T.bt[:, :, h], ["bt"]) if d == 0 else (zab[:, :, 0, h], ["z" + H])
-        tt("y" + H, xy[:, 1:94:2], zab[:, 0:47, 2, h], zab[:, 1:48, 1, h], ALU.add, ["ab" + H], ["xy1" + H], 94)
+        z, zk = (T.bt[:, :, h], ["bt"]) if d == 0 else (zab[:, :, 0, h], ["z" + H, "nz0" + H, "nz1" + H])
+        tt("y" + H, xy[:, 1:94:2], zab[:, 0:47, 2, h], zab[:, 1:48, 1, h], ALU.add, ["ab" + H, "nr0" + H, "nr1" + H], ["xy1" + H], 94)
         if d == 0:
             cp("c0a" + H, ci[:, 0, 0:47], xy[:, 1:94:2], ["xy1" + H], ["ci0" + H])
             ts("c0b" + H, ci[:, 1, 0:47], ci[:, 0, 0:47], W - 1, None, ALU.bitwise_and, None, ["ci0" + H], ["ci1" + H])
             cp("c0" + H, ll[:, 0:47], ci[:, 1, 0:47], ["ci1" + H], ["ll" + H])
             act("own" + H, T["xo" + H][:, 0, :], T.xn[:, NO + 1:B, h, :], ACT.Identity, ["xn"], ["xo0" + H], 16 * (47 - NO))
         else:
-            cp("c0" + H, ll[:, 0:47], xy[:, 1:94:2], ["xy1" + H], ["ll" + H])
-            dma("y", "own" + H, T["xo" + H][:, 1, :], T.xw1[:, h * HW + 32 + 16 * NO:(h + 1) * HW], xk(d, h), ["xo1" + H], 4096 * (47 - NO), False)
-        tt("sx" + H, fa[:, 0, 0:47], zab[:, 0:47, 1, h], zab[:, 0:47, 2, h], ALU.add, ["ab" + H], ["sx" + H], 94)
+            dma("y", "own" + H, T["xo" + H][:, 1, 0:16 * (46 - NO)], T.xw1[:, h * HW + 32 + 16 * NO:(h + 1) * HW - 16], xk(d, h)[1:3], ["xo1" + H],
+                4096 * (46 - NO), False)
+        tt("sx" + H, fa[:, 0, 0:47], zab[:, 0:47, 1, h], zab[:, 0:47, 2, h], ALU.add, ["ab" + H, "nr0" + H], ["sx" + H], 94)
         act("x" + H, xy[:, 0:94:2], fa[:, 0, 0:47], ACT.Identity, ["sx" + H], ["xy0" + H], scale=-1.0)
         tt("zz" + H, fa[:, 1, :], z, T.bc[:], ALU.add, zk + ["bc"], ["zz" + H], 96)
         tt("dz" + H, fa[:, 2, 1:48], fa[:, 1, 0:47], fa[:, 1, 1:48], ALU.subtract, ["zz" + H], ["dz" + H], 94)
@@ -199,19 +200,23 @@ def build(g, core, T, topo, rank):
         X, tag = xk(d, h), "%d%d%d" % (d, k, h)
         XS, ls, lk = (X[1:3], T["l2" + H], "l2" + H) if s0 else (X, ll, "ll" + H)
         ka = kaps[(k == 0, ns, s0)]
+        if k == 1:
+            mm("hold" + tag, [(pc[:, 192:288], T.idf[:], T.nn[:, 1, :], True, False, 4), (pc[:, 192:288:2], T.idh[:], aa[:], False, False, 1),
+                              (pc[:, 193:288:2], T.idi[:], aa[:], False, True, 1)], ["idf", "idh", "idi", "nn1", "aa" + H], ["pc" + H, "s" + H, "hold" + H])
         mm("cn0" + tag, [(pc[:, 0:47], T.idw[:], T.kap[:, ka, 0:47], True, False, 1)] + [(pc[:, 0:47], T.idw[:], aa[:, 1:48], False, False, 1)][:k],
-           ["idw", "kap%d" % ka, "kas%d" % ka, "kao"] + ["aa" + H][:k], ["pc" + H, "s" + H, "l" + H])
+           ["idw", "kap%d" % ka, "kas%d" % ka, "kao"] + ["aa" + H][:k], ["pc" + H, "s" + H, "hold" + H])
         if k > 0:
-            sgc("gx" + tag, xr[:, 0:16 * ns], win, ll[:, 48:48 + ns], X + ["lr" + H], ["xr" + H], 16 * ns)
             vgt("gd" + tag, dv[:, 0:16 * nv], win, ll[:, 48 + ns:95], T["xo" + H][:, d, 16 * (ns - NO):16 * (47 - NO)], ALU.subtract,
-                X + ["lr" + H, "xo%d" % d + H], ["dv" + H, "dw" + H, "dx" + H], 16 * nv)
-        n1 = ns * 5 // 16 * 2
+                X + ["lr" + H, "xo%d" % d + H, "xp%d" % d + H], ["dv" + H, "dw" + H, "dx" + H], 16 * nv)
+        n1 = int(ns * SPLIT) // 2 * 2
         for C, u0, u1, pp, pk in (("0", 0, n1, ps, "ps" + H), ("1", n1, ns, pf if s0 else (T.pmw, T.pmc)[h], "pf" + H if s0 else ("pmw", "pmc")[h])):
             a0, a1 = 16 * u0, 16 * u1
             c0, out = o + 16 + 16 * s0, pp[:, 0:a1 - a0]
+            if k > 0:
+                sgc("gx" + C + tag, xr[:, a0:a1], win, ll[:, 48 + u0:48 + u1], X + ["lr" + H], ["xr" + C + H], a1 - a0)
             mm("su0" + C + tag, [(out, T.idp[:], xw[:, c0 + 16 + a0:c0 + 16 + a1], True, False, 1),
                                  (out, T.idn[:], xr[:, a0:a1] if k else xw[:, c0 + a0:c0 + a1], False, False, 1)],
-               XS + ["xr" + H][:k] + ["idp", "idn"], [pk])
+               XS + ["xr" + C + H][:k] + ["idp", "idn"], [pk])
             sgc("ge" + C + tag, eg[:, a0:a1], ew, ls[:, u0:u1], ek + [lk], ["eg" + C + H], a1 - a0)
             mm("su1" + C + tag, [(out, T.idp[:], eg[:, a0:a1], False, True, 1)], ["eg" + C + H, "idp", pk], [pk])
             act("sg" + C + tag, cmp_[:, 16 * s0 + a0:16 * s0 + a1], out, ACT.Sign, [pk], ["cs" + C + H], a1 - a0, bias=-0.5)
@@ -221,7 +226,7 @@ def build(g, core, T, topo, rank):
         else:
             vgt("gc" + tag, cmp_[:, 16 * ns + 16:736], ew, ls[:, ns:45], dv[:, 16:16 * nv - 16], ALU.is_gt, ek + [lk, "dv" + H], ["cv" + H], 16 * nv - 32)
             vgt("gz" + tag, cmp_[:, 736:752], ew, ll[:, 46:47], dv[:, 16 * nv - 16:16 * nv], ALU.is_gt, ek + ["ll" + H, "dw" + H], ["cy" + H], 16)
-            vgt("gb" + tag, cmp_[:, 0:16], ew, ll[:, 0:1], dv[:, 0:16], ALU.is_gt, ek + ["ll" + H, "dx" + H], ["cx" + H], 16)
+            vgt("gb" + tag, cmp_[:, 0:16], ew, ll[:, 0:1], dv[:, 0:16], ALU.is_gt, ek + ["ll" + H, "l0" + H, "dx" + H], ["cx" + H], 16)
         mm("cnt" + tag, [(pc[:, 0:47], T.usel[:, 15 - r:143 - r], cmp_[:, r:752:16], False, r == 15, 1) for r in range(16)],
            ["usel", "cs0" + H, "cs1" + H, "cv" + H, "cx" + H, "cy" + H, "pc" + H], ["pc" + H])
         a_, ak = (T.am, "am") if k == 0 else (aa, "aa" + H)
@@ -229,7 +234,7 @@ def build(g, core, T, topo, rank):
         fm, fk = (fa[:, 2, 1:48], "dz" + H) if k == 0 else (fa[:, 3, 1:48], "fm" + H)
         tt("g" + tag, fa[:, 4, 1:48], pc[:, 64:111], fm, ALU.max, ["s" + H, fk], ["g" + H])
         if k == 0:
-            ts("k" + tag, kk[:, 0, 1:48], fa[:, 4, 1:48], 0.0, None, ALU.min, None, ["g" + H], ["k%s0" % H])
+            act("k" + tag, kk[:, 0, 1:48], fa[:, 4, 1:48], ACT.Relu, ["g" + H], ["k%s0" % H], scale=-1.0)
         else:
             scan("k" + tag, kk[:, k, 47:0:-1], mi[:, k - 1, 95:2:-2], fa[:, 4, 47:0:-1], 0.0, ALU.mult, ALU.min,
                  ["g" + H, "m%s%d" % (H, k)], ["k%s%d" % (H, k)])
@@ -237,10 +242,12 @@ def build(g, core, T, topo, rank):
             return
         mk, N = "m%s%d" % (H, k + 1), 811.0 * (k + 1)
         ce, ck = (T.eps, "eps") if k == 0 else (T["ce" + H], "ce" + H)
-        scan("l" + tag, pc[:, 175:127:-1], ce[:, 47::-1], pc[:, 110:62:-1], 0.0, ALU.mult, ALU.min, ["s" + H, "s0" + H, ck], ["l" + H])
-        tt("m" + tag, mi[:, k, 1:96:2], pc[:, 128:176], a_[:], ALU.is_lt, ["l" + H, ak], [mk])
-        scan("sr" + tag, tb[:, 97:190:2], mi[:, k, 1:94:2], T.ni[:, k + 1, 0:47], -N, ALU.mult, ALU.min, [mk, "ni%d" % (k + 1)], ["sr" + H])
-        ts("lr" + tag, ll[:, 48:95], tb[:, 97:190:2], N, 0.0, ALU.add, ALU.max, ["sr" + H], ["lr" + H])
+        lv = T["lv" + H]
+        scan("l" + tag, lv[:, 94::-2], ce[:, 47::-1], pc[:, 110:62:-1], 0.0, ALU.mult, ALU.min, ["s" + H, "s0" + H, ck], ["l" + H])
+        tt("m" + tag, mi[:, k, 1:96:2], lv[:, 0:96:2], a_[:], ALU.is_lt, ["l" + H, ak], [mk], 96)
+        scan("sr" + tag, tb[:, 96:190], pc[:, 192:286] if k else T.nn[:, 0, 0:94], lv[:, 0:94], 0.0, ALU.add, ALU.max,
+             ["l" + H, "lo" + H, "nn0", "hold" + H], ["sr" + H], 94)
+        ts("lr" + tag, ll[:, 48:95], tb[:, 97:190:2], 0.25, None, ALU.add, None, ["sr" + H], ["lr" + H])
         scan("sc" + tag, tb[:, 0:94], mi[:, k, 0:94], T["xy" + H][:, 0:94], 0.0, ALU.mult, ALU.add, [mk, "xy0" + H, "xy1" + H], ["sc" + H], 94)
         ts("ll" + tag, ll[:, 0:47], tb[:, 1:94:2], N, 0.0, ALU.add, ALU.max, ["sc" + H], ["ll" + H])
         act("a" + tag, aa[:], mi[:, k, 1:96:2], ACT.Identity, [mk], ["aa" + H], bias=-1.0, scale=2.0)
@@ -250,21 +257,35 @@ def build(g, core, T, topo, rank):
         if k == 0:
             act("ce" + tag, T["ce" + H][:], mi[:, k, 1:96:2], ACT.Identity, [mk], ["ce" + H], bias=EPS, scale=1.0 - EPS)
         else:
-            tt("ks" + tag, kk[:, 3, 1:48], kk[:, 0, 1:48], kk[:, 1, 1:48], ALU.add, ["k%s0" % H, "k%s1" % H], ["k%s3" % H], 94)
-            mm("bs" + tag, [(pf[:, 0:48], T.idf[:], fa[:, 1, :], True, False, 4), (pf[:, 0:48], T.idf[:], kk[:, 3, 0:48], False, False, 4),
-                            (pf[:, 0:48], T.idg[:], kk[:, 3, 1:49], False, True, 4)], ["idf", "idg", "zz" + H, "k%s3" % H], ["pf" + H])
+            mm("br" + tag, [(pf[:, 0:48], T.idf[:], fa[:, 1, :], True, False, 4), (pf[:, 0:48], T.idg[:], kk[:, 0, 0:48], False, False, 4),
+                            (pf[:, 0:48], T.idf[:], kk[:, 0, 1:49], False, False, 4)], ["idf", "idg", "zz" + H, "k%s0" % H], ["pf" + H])
+            mm("bs" + tag, [(pf[:, 0:48], T.idf[:], kk[:, 1, 0:48], False, False, 4),
+                            (pf[:, 0:48], T.idg[:], kk[:, 1, 1:49], False, True, 4)], ["idf", "idg", "k%s1" % H], ["pf" + H])
 
     def neighbours(r):
-        nb = [(r - 1, 0, 1)][:r] + [(r + 1, 3, 2)][:n - 1 - r]
+        nb = [(r - 1, 0)][:r] + [(r + 1, 1)][:n - 1 - r]
         out = []
-        for i, (q, s, t) in enumerate(nb):
+        for i, (q, s) in enumerate(nb):
             e = topo.engines(T.cores[r], T.cores[q])
-            out.append((q, s, t, e[i * len(e) // len(nb):(i + 1) * len(e) // len(nb)]))
+            out.append((q, s, e[i * len(e) // len(nb):(i + 1) * len(e) // len(nb)]))
         return out
 
+    def exchange(name, src, dst, r):
+        def send():
+            tr = []
+            for q, s, es in neighbours(rank):
+                rid, pid = topo.addr(T.cores[q], core)
+                tr.append(RemoteDMATransfer(dst_ids=[DstId(rid=rid, pnc=pid)], dma_engine_mask=sum(1 << e for e in es),
+                                            remote_sem=T.sem[name], src=src[s], dst=dst[s]))
+            return g.remote_dma_fused(tr, local_sem=T.sem.sent)
+        add("g", "send" + name, send, r, ["snd" + name], fix=500.0, kind="r")
+        ops[-1]["sent"] = sum(len(u[2]) for u in neighbours(rank))
+        add("x", name, None, ["snd" + name], [name], kind="a")
+        ops[-1]["tok"] = (name, sum(len(v[2]) for u in neighbours(rank) for v in neighbours(u[0]) if v[0] == rank))
+
     def day_end(d, h):
-        H, tag, e0 = str(h), "%d%d" % (d, h), 4 * d
-        pf, kk, zi, pq, el, pl = [T[s + H] for s in ("pf", "kk", "zi", "pq", "el", "pl")]
+        H, tag = str(h), "%d%d" % (d, h)
+        pf, kk, zi, pq, pl, el, ex = [T[s + H] for s in ("pf", "kk", "zi", "pq", "pl", "el", "ex")]
         o, X = h * HW, xk(d, h)
         win = T["xw%d" % d][:, o:o + HW]
         tt("z0" + tag, pf[:, 64:112], pf[:, 0:48], kk[:, 2, 0:48], ALU.add, ["pf" + H, "k%s2" % H], ["pf" + H])
@@ -273,9 +294,10 @@ def build(g, core, T, topo, rank):
         ts("el" + tag, el[:, 0:4:2], pq[:, 0:48:47], T.rc[:, 0:1], None, ALU.add, None, ["pq" + H, "rc0"], ["el" + H])
         ts("zq" + tag, zab[:, :, 0, h], zi[:], 65535, None, ALU.bitwise_and, None, ["zi" + H], ["z" + H])
         numbers(h, zab[:, :, 0, h], ["z" + H], 3 if d == 0 else 7)
-        vgc("eh" + tag, ex[:, e0, 16 * h:16 * h + 16], win, el[:, 0:1], X + ["el" + H], ["ex%d_0%d" % (d, h)], 16)
-        vgc("ef" + tag, ex[:, e0 + 3, 16 * h:16 * h + 16], win, el[:, 2:3], X + ["el" + H], ["ex%d_3%d" % (d, h)], 16)
-        cp("ez" + tag, ex[:, e0:e0 + 4:3, 32 + h:38:2], zab[:, 0:48:47, :, h], ["z" + H, "ab" + H], ["exz" + tag])
+        for e in range(2):
+            c = 24 - 24 * e
+            sgc("ew%d" % e + tag, ex[:, 2 * d + e, c:c + 16], win, el[:, 2 * e:2 * e + 1], X + ["el" + H], ["ew%d" % e + tag], 16)
+            cp("ez%d" % e + tag, ex[:, 2 * d + e, c + 16:c + 19], zab[:, 47 * e, :, h], ["z" + H, "ab" + H], ["ez%d" % e + tag])
         if d == 0:
             pv, ns = B - PERM_V, NS[(1, 0)]
             ts("pl" + tag, pl[:], pq[:], T.rc[:, 0:1], None, ALU.add, None, ["pq" + H, "rc0"], ["pl" + H])
@@ -288,47 +310,50 @@ def build(g, core, T, topo, rank):
             ts("pl" + tag, T.nat[:, h:96:2], pq[:], T.rc[:, h:h + 1], None, ALU.add, None, ["pq" + H, "rc" + H], ["nat" + H])
             cp("zf" + tag, T.zf[:, :, h], zab[:, :, 0, h], ["z" + H], ["zf" + H])
 
-    def meet(d):
-        e0, D = 4 * d, str(d)
-        md, mt, ms, uc, uw, cm, mc = T.md, T.mt, T.ms, T.uc, T.uw, T.cm, T.mc
-        own = ["ex%d_%d%d" % (d, s, h) for s in (0, 3) for h in range(2)] + ["exz%d0" % d, "exz%d1" % d]
-
-        def send():
-            tr = []
-            for q, s, t, es in neighbours(rank):
-                rid, pid = topo.addr(T.cores[q], core)
-                tr.append(RemoteDMATransfer(dst_ids=[DstId(rid=rid, pnc=pid)], dma_engine_mask=sum(1 << e for e in es),
-                                            remote_sem=T.sem["arr" + D], src=ex[:, e0 + s, 0:38], dst=ex[:, e0 + t, 0:38]))
-            return g.remote_dma_fused(tr, local_sem=T.sem.sent)
-        add("g", "send" + D, send, own, ["snd" + D], fix=500.0, kind="r")
-        ops[-1]["sent"] = sum(len(u[3]) for u in neighbours(rank))
-        add("x", "arr" + D, None, ["snd" + D], ["arr" + D], kind="a")
-        ops[-1]["tok"] = ("arr" + D, sum(len(v[3]) for u in neighbours(rank) for v in neighbours(u[0]) if v[0] == rank))
-        A = own + ["ex%d_%d0" % (d, s) for s in (1, 2)] + ["arr" + D]
+    def meet(d, h):
+        H, tag, o, e0 = str(h), "%d%d" % (d, h), h * HW, 2 * d
+        ex, md, cm, mc, uc, ne, ll, dv = [T[s + H] for s in ("ex", "md", "cm", "mc", "uc", "ne", "ll", "dv")]
+        pm, pk = (T.pmw, T.pmc)[h], ("pmw", "pmc")[h]
+        Z = ["ez0" + tag, "ez1" + tag, "pad" + H]
+        A = Z + ["ew0" + tag, "ew1" + tag]
+        exchange("arr" + tag, [ex[:, e0, 24:48], ex[:, e0 + 1, 0:24]], [ex[:, e0 + 1, 24:48], ex[:, e0, 0:24]], A)
+        Z, A = Z + ["arr" + tag, "exz" + tag], A + ["arr" + tag, "exz" + tag]
         ew, ek = ewin(EW if d == 0 else 2 * W)
-        tt("mc0" + D, ms[:], ex[:, e0:e0 + 2, 34:36], ex[:, e0 + 2:e0 + 4, 36:38], ALU.add, A, ["ms"])
-        ts("mc" + D, mc[:], ms[:], float(811 * 3 if d == 0 else 0), None, ALU.add, None, ["ms"], ["mc"])
-        tt("md" + D, md[:, :, 0:38], ex[:, e0 + 2:e0 + 4, 0:38], ex[:, e0:e0 + 2, 0:38], ALU.subtract, A, ["md"], 152)
-        vgt("m0" + D, cm[:, 0:32], ew, mc[:, 0:2], md[:, 0, 0:32], ALU.is_gt, ek + ["mc", "md"], ["cm0"], 32)
-        vgt("m1" + D, cm[:, 32:64], ew, mc[:, 2:4], md[:, 1, 0:32], ALU.is_le, ek + ["mc", "md"], ["cm1"], 32)
-        mm("mw" + D, [(T.pmw[:, 0:64], T.bo[:], cm[:], True, True, 1)], ["bo", "cm0", "cm1"], ["pmw"])
-        mm("mq" + D, [(T.pmc[:, 0:4], T.usel[:, 15 - r:143 - r], cm[:, r:64:16], r == 0, r == 15, 1) for r in range(16)], ["usel", "cm0", "cm1"], ["pmc"])
-        tt("uw" + D, uw[:], T.pmw[:, 0:64], T.thw[:], ALU.is_gt, ["pmw", "thw0", "thw1"], ["uw"])
-        tt("tx" + D, mt[:, :, 0:32], uw[:], md[:, :, 0:32], ALU.mult, ["uw", "md"], ["tx"], 128)
-        tt("uc" + D, uc[:], T.pmc[:, 0:4], T.thc[:], ALU.is_lt, ["pmc", "thc0", "thc1"], ["uc"])
-        for f in range(3 if d == 0 else 1):
-            tt("tz%d" % f + D, mt[:, :, 32 + 2 * f:34 + 2 * f], uc[:], md[:, :, 32 + 2 * f:34 + 2 * f], ALU.mult, ["uc", "md"], ["tz%d" % f])
+        mm("mt" + tag, [(pm[:, 0:2], T.idw[:], T.thm[:], True, False, 1)], ["idw", "thm0", "thm1"], [pk])
+        tt("md" + tag, md[:], ex[:, e0:e0 + 2, 0:24], ex[:, e0:e0 + 2, 24:48], ALU.subtract, A, ["md" + H], 96)
+        for e in range(2):
+            E = str(e) + tag
+            ts("mc" + E, mc[:, 2 * e:2 * e + 1], ex[:, e0 + e, 41:42], ex[:, e0 + e, 18:19], 811.0 * 3 * (1 - d), ALU.add, ALU.add, Z, ["mc%d" % e + H])
+            vgt("m" + E, cm[:, 16 * e:16 * e + 16], ew, mc[:, 2 * e:2 * e + 1], md[:, e, 0:16], (ALU.is_gt, ALU.is_le)[e],
+                ek + ["mc%d" % e + H, "md" + H], ["cm%d" % e + H], 16)
+        mm("mq" + tag, [(pm[:, 0:2], T.usel[:, 15 - r:143 - r], cm[:, r:32:16], False, r == 15, 1) for r in range(16)],
+           ["usel", "cm0" + H, "cm1" + H], [pk])
+        ts("mi" + tag, mc[:, 4:8:2], pm[:, 0:2], T.rc[:, 2:3], T.rc[:, 3:4], ALU.max, ALU.min, [pk, "rc2", "rc3"], ["mi" + H])
+        ts("uc" + tag, uc[:, 0:2], pm[:, 0:2], 0.0, None, ALU.is_lt, None, [pk], ["uc" + H])
+
+        def pick(name, out, e, f, base, r, w):
+            ts(name + str(e) + tag, out, uc[:, e:e + 1], md[:, e, 16 + f:17 + f], base, ALU.mult, ALU.add, ["uc" + H, "md" + H] + Z + r, w)
+        A = A + ["mi" + H]
+        for e in range(2):
+            win, lst, b, f = ex[:, e0 + e, :], mc[:, 4 + 2 * e:5 + 2 * e], 47 * e, 2 - e
+            if d == 1:
+                (vgc, sgc)[e]("new%d" % e + tag, T.ye[:, 32 * e + 16 * h:32 * e + 16 * h + 16], win, lst, A, ["ye%d" % e + H], 16)
+                pick("nz", T.zf[:, b, h:h + 1], e, 0, ex[:, e0 + e, 40:41], ["zf" + H], ["zf%d" % e + H])
+                continue
+            ts("pre%d" % e + tag, uc[:, 2 + e:3 + e], zab[:, 1 + 45 * e, 1 + e, h:h + 1], ex[:, e, 40 + f:41 + f], None, ALU.add, None,
+               Z + ["ab" + H], ["pre%d" % e + H])
+            pick("nc", ll[:, 46 * e:46 * e + 1], e, f, uc[:, 2 + e:3 + e], ["pre%d" % e + H], [("l0", "ll")[e] + H])
+            c = o + 16 + 16 * b
+            sgc("new%d" % e + tag, T.xw1[:, c:c + 16], win, lst, A, [("xh1", "xf1")[e] + H], 16)
+            pick("nz", zab[:, b, 0, h:h + 1], e, 0, ex[:, e, 40:41], [], ["nz%d" % e + H])
+            pick("nr", zab[:, b, f, h:h + 1], e, f, ex[:, e, 40 + f:41 + f], [], ["nr%d" % e + H])
         if d == 0:
-            for h in range(2):
-                o, H = h * HW, str(h)
-                tt("nh" + H, T.xw1[:, o + 16:o + 32], mt[:, 0, 16 * h:16 * h + 16], ex[:, e0, 16 * h:16 * h + 16], ALU.add, ["tx"] + A, ["xh1" + H])
-                tt("nf" + H, T.xw1[:, o + HW - 16:o + HW], mt[:, 1, 16 * h:16 * h + 16], ex[:, e0 + 1, 16 * h:16 * h + 16], ALU.add, ["tx"] + A, ["xf1" + H])
-                adjacent(1, h, 47, 48, ["xa1" + H, "xb1" + H, "xf1" + H], ["dw" + H])
-                adjacent(1, h, 1, 2, ["xa1" + H, "xh1" + H], ["dx" + H])
-            tt("nz" + D, zab[:, 0:48:47, :, :], mt[:, :, 32:38], ex[:, e0:e0 + 2, 32:38], ALU.add, ["tz0", "tz1", "tz2"] + A, ["z0", "ab0", "z1", "ab1"])
-        else:
-            tt("nx" + D, T.ye[:], mt[:, :, 0:32], ex[:, e0:e0 + 2, 0:32], ALU.add, ["tx"] + A, ["ye"], 128)
-            tt("nz" + D, T.zf[:, 0:48:47, :], mt[:, :, 32:34], ex[:, e0:e0 + 2, 32:34], ALU.add, ["tz0"] + A, ["zf0", "zf1"])
+            nv = 47 - NS[(1, 0)]
+            vgt("dh" + tag, dv[:, 0:16], ex[:, 0, :], mc[:, 4:5], T.xw1[:, o + 32:o + 48], ALU.subtract, A + ["xa1" + H], ["dx" + H], 16)
+            act("ne" + tag, ne[:], ex[:, 1, :], ACT.Identity, A[:-1], ["ne" + H], scale=-1.0)
+            vgt("df" + tag, dv[:, 16 * nv - 16:16 * nv], ne[:], mc[:, 6:7], T.xw1[:, o + HW - 32:o + HW - 16], ALU.add,
+                ["ne" + H, "mi" + H, "xa1" + H, "xb1" + H], ["dw" + H], 16)
+            sgc("xo" + tag, T["xo" + H][:, 1, 16 * (46 - NO):16 * (47 - NO)], ex[:, 1, :], mc[:, 6:7], A, ["xp1" + H], 16)
 
     cp("xw0", T.xw0[:, 16:HW], T.xn[:, :, 0, :], ["xn"], xk(0, 0)[1:], 384)
     act("xw1", T.xw0[:, HW + 16:2 * HW], T.xn[:, :, 1, :], ACT.Identity, ["xn"], xk(0, 1)[1:], 768)
@@ -343,15 +368,15 @@ def build(g, core, T, topo, rank):
                 interval(d, k, h)
         for h in range(2):
             day_end(d, h)
-        meet(d)
+            meet(d, h)
     X, c1 = xk(1, 0) + xk(1, 1) + ["nat0", "nat1"], 2 + FIN_V
     vgc("fv", T.ys[:, 32:16 * c1], T.xw1[:, 0:2 * HW], T.nat[:, 2:c1], X, ["ysv"], 16 * FIN_V)
     sgc("fs", T.ys[:, 16 * c1:1504], T.xw1[:, 0:2 * HW], T.nat[:, c1:94], X, ["yss"], 1504 - 16 * c1)
     dma("y", "st_v", T.yx[:, 32:16 * c1], T.ys[:, 32:16 * c1], ["ysv"], ["o0"], 4096 * FIN_V, False)
     dma("s", "st_s", T.yx[:, 16 * c1:1504], T.ys[:, 16 * c1:1504], ["yss"], ["o1"], 256 * (1504 - 16 * c1))
-    dma("y", "st_h", T.yx[:, 0:32], T.ye[:, 0, :], ["ye"], ["o2"], 8192, False)
-    dma("s", "st_f", T.yx[:, 1504:1536], T.ye[:, 1, :], ["ye"], ["o3"], 8192, False)
-    dma("y", "st_b", T.yb[:], T.zf[:], ["zf0", "zf1"], ["o4"], 49152, False)
+    dma("y", "st_h", T.yx[:, 0:32], T.ye[:, 0:32], ["ye00", "ye01"], ["o2"], 8192, False)
+    dma("s", "st_f", T.yx[:, 1504:1536], T.ye[:, 32:64], ["ye10", "ye11"], ["o3"], 8192, False)
+    dma("y", "st_b", T.yb[:], T.zf[:], ["zf00", "zf01", "zf10", "zf11"], ["o4"], 49152, False)
     return ops
 
 
@@ -382,33 +407,48 @@ def order(ops):
     for i in range(n):
         for j in dep[i]:
             succ[j].add(i)
-    tms = [[times(o, m) for o in ops] for m in MODELS]
+    tms = [[(a, b + m["wake"]) for a, b in [times(o, m) for o in ops]] for m in MODELS]
+    n0 = sum(o["early"] for o in ops)
 
     def rnd():
         seed[0] = (seed[0] * 1103515245 + 12345) % 2147483648
         return seed[0] / 2147483648.0
 
-    def length(seq):
-        tot = 0.0
-        for tm, m in zip(tms, MODELS):
-            free, end = [0.0] * 6, [0.0] * n
-            for i in seq:
+    def length(seq, lo, old):
+        tot, res = 0.0, []
+        for a, tm in enumerate(tms):
+            end, fin = (old[a][0][:], old[a][1][:]) if lo else ([0.0] * n, [0.0] * n)
+            free = [0.0] * 6
+            for i in seq[:lo]:
+                free[en[i]] = fin[i]
+            for i in seq[lo:]:
                 st = free[en[i]]
                 for j in dep[i]:
                     if end[j] > st:
                         st = end[j]
-                free[en[i]] = st + tm[i][0]
-                end[i] = st + tm[i][1] + m["wake"]
-            tot += max(end)
-        return tot
+                free[en[i]] = fin[i] = st + tm[i][0]
+                end[i] = st + tm[i][1]
+            tot += max(end) + 0.3 * sum(end) / n
+            res.append((end, fin))
+        return tot, res
 
-    best = None
-    for t in range(TRIES):
-        m, tm = MODELS[t % len(MODELS)], tms[t % len(MODELS)]
+    def path(seq, end, tm):
+        prev, last = {}, [None] * 6
+        for i in seq:
+            prev[i], last[en[i]] = last[en[i]], i
+        i, out = end.index(max(end)), []
+        while True:
+            js = [j for j in dep[i] if end[j] >= end[i] - tm[i][1] - 1e-6]
+            if not js and prev[i] is None:
+                return out
+            out += [] if js else [(i, prev[i])]
+            i = js[0] if js else prev[i]
+
+    def listed(tm):
         noise, slack, bias = 400.0 * rnd(), 30.0 + 250.0 * rnd(), 2500.0 * rnd()
         pri = [0.0] * n
         for i in range(n - 1, -1, -1):
-            pri[i] = tm[i][1] + max([m["wake"] + pri[j] for j in succ[i]] + [0.0])
+            pri[i] = tm[i][1] + max([pri[j] for j in succ[i]] + [0.0])
         pri = [p + noise * rnd() + bias * (ops[i]["name"][-1] == "0") for i, p in enumerate(pri)]
         left, rel, free, seq = [len(d) for d in dep], [0.0] * n, [0.0] * 6, []
         ready = [i for i in range(n) if not dep[i]]
@@ -421,38 +461,46 @@ def order(ops):
             ready.remove(b)
             seq.append(b)
             for j in succ[b]:
-                rel[j] = max(rel[j], est[b] + tm[b][1] + m["wake"])
+                rel[j] = max(rel[j], est[b] + tm[b][1])
                 left[j] -= 1
                 if left[j] == 0:
                     ready.append(j)
-        v = length(seq)
-        if best is None or v < best[0]:
-            best = (v, seq)
-    c, cur = best
-    n0 = sum(o["early"] for o in ops)
-    for it in range(MOVES):
-        p, k, d = n0 + int(rnd() * (n - n0)), (1, 1, 1, 2, 3)[int(rnd() * 5)], (-1, 1)[int(rnd() * 2)]
-        i, q = cur[p], p
-        while k and n0 <= q + d < n:
-            q += d
-            k -= en[cur[q]] == en[i]
-        if k:
-            continue
-        lo, hi = min(p, q), max(p, q)
-        seg, tied = cur[lo:hi + 1], {i}
-        for x in (seg[-2::-1] if d < 0 else seg[1:]):
-            if tied.intersection(succ[x] if d < 0 else dep[x]):
-                tied.add(x)
-        if cur[q] in tied:
-            continue
-        a, b = [x for x in seg if x in tied], [x for x in seg if x not in tied]
-        new = cur[:lo] + (a + b if d < 0 else b + a) + cur[hi + 1:]
-        v = length(new)
-        if v < c or rnd() < math.exp((c - v) / (170.0 * (1.0 - it / MOVES) + 3.0)):
-            c, cur = v, new
-            if c < best[0]:
-                best = (c, cur)
-    return best[1]
+        return length(seq, 0, None)[0], seq
+
+    def moved(best, moves):
+        cur, hot = best[1], None
+        c, res = length(cur, 0, None)
+        for it in range(moves):
+            k, d = (1, 1, 1, 2, 3)[int(rnd() * 5)], (-1, 1)[int(rnd() * 2)]
+            if rnd() < 0.6:
+                hot = hot or path(cur, res[it % len(tms)][0], tms[it % len(tms)])
+                p = max(n0, cur.index(hot[int(rnd() * len(hot))][d > 0]))
+            else:
+                p = n0 + int(rnd() * (n - n0))
+            i, q = cur[p], p
+            while k and n0 <= q + d < n:
+                q += d
+                k -= en[cur[q]] == en[i]
+            if k:
+                continue
+            lo, hi = min(p, q), max(p, q)
+            seg, tied = cur[lo:hi + 1], {i}
+            for x in (seg[-2::-1] if d < 0 else seg[1:]):
+                if tied.intersection(succ[x] if d < 0 else dep[x]):
+                    tied.add(x)
+            if cur[q] in tied:
+                continue
+            a, b = [x for x in seg if x in tied], [x for x in seg if x not in tied]
+            new = cur[:lo] + (a + b if d < 0 else b + a) + cur[hi + 1:]
+            v, r = length(new, lo, res)
+            if v < c or rnd() < math.exp((c - v) / (150.0 * (1.0 - it / moves) + 3.0)):
+                c, cur, res, hot = v, new, r, None
+                if c < best[0]:
+                    best = (c, cur)
+        return best
+
+    starts = [moved(min(listed(tms[t % len(tms)]) for t in range(TRIES)), MOVES // 5) for s in range(STARTS)]
+    return moved(min(starts), MOVES)[1]
 
 
 def emit(g, T, ops, seq):
@@ -479,7 +527,7 @@ def emit(g, T, ops, seq):
         ins.then_inc(T.sem[s], inc)
         total[s] = total.get(s, 0) + inc
         o["tok"], o["clock"] = (s, total[s]), dict(kn, **{s: total[s]})
-    for s in sorted(total):
+    for s in sorted(total, key=lambda s: int(s[3:]) if s[:3] == "dma" else -1):
         g.wait_ge(T.sem[s], total[s])
 
 

@@ -5,17 +5,19 @@ from concourse.mybir import AluOpType as ALU, ActivationFunctionType as ACT
 B, V, W = 48, 1536, 4096
 HW = 16 + 16 * B
 EW = 10624
-BIG, HALF, EPS = 2.0 ** 28, 2.0 ** 21, 2.0 ** -17
-SPLIT = 0.6
-NS = {(0, 0): 28, (0, 1): 24, (0, 2): 22, (1, 0): 36, (1, 1): 24, (1, 2): 22}
+BIG, HALF, EPS = 2.0 ** 30, 2.0 ** 21, 2.0 ** -19
+SPLIT = 0.7
+VP = (1, 2)
+NS = {(0, 0): 20, (0, 1): 24, (0, 2): 22, (1, 0): 42, (1, 1): 24, (1, 2): 22}
 NO = min(NS.values())
-PERM_V = 8
-FIN_V = 44
-ENC_CP = ["v", "s", "v", None]
-TRIES, STARTS, MOVES = 24, 7, 40000
-MODELS = [dict(f=1.0, g=1.56, wake=200.0, pe=0.42, dma=1200.0, bw=300.0, rem=1000.0),
-          dict(f=1.15, g=1.4, wake=170.0, pe=0.42, dma=1500.0, bw=250.0, rem=1800.0),
-          dict(f=1.3, g=1.8, wake=220.0, pe=0.42, dma=1300.0, bw=300.0, rem=1500.0)]
+PERM_V = 16
+FIN_V = 38
+ENC_A = 2048
+ENC_CP = [(W, W + 1280, "v"), (W + 1280, W + 2048, "s"), (W + 2048, W + 2880, "g"), (W + 2880, 2 * W, "y"), (2 * W, 9008, "g"), (9008, EW, "y")]
+TRIES, STARTS, MOVES = 200, 4, 5500
+MODELS = [dict(f=1.0, g=1.56, wake=220.0, pe=0.42, dma=600.0, bw=450.0, rem=1000.0),
+          dict(f=1.15, g=1.4, wake=190.0, pe=0.42, dma=1300.0, bw=230.0, rem=1800.0),
+          dict(f=1.4, g=1.85, wake=210.0, pe=0.42, dma=800.0, bw=400.0, rem=1300.0)]
 
 BF, F, I, U = "bfloat16", "float32", "int32", "uint16"
 SCRATCH = {"pmw": ("psum", [128, 512], F), "pmc": ("psum", [128, 512], F)}
@@ -24,15 +26,15 @@ for _n, _s, _t in (
         ("ye", [64], BF), ("zf", [B, 2], F), ("nat", [96], U), ("ones", [128], BF), ("idp", [128], BF),
         ("idn", [128], BF), ("idw", [128], BF), ("idb", [128], BF), ("idc", [128], BF), ("idf", [128], F), ("idg", [128], F),
         ("usel", [144], BF), ("w8", [8], BF), ("t8", [8], BF), ("pi", [2], I), ("rc", [4], F), ("bi", [B], F), ("bc", [B], F),
-        ("nn", [2, 96], F), ("idh", [128], BF), ("idi", [128], BF), ("kap", [6, B], BF), ("am", [B], BF), ("eps", [B], F),
-        ("thm", [2], BF), ("zab", [B, 3, 2], I)):
+        ("nn", [2, 96], F), ("idh", [128], BF), ("idi", [128], BF), ("idu", [128], BF), ("idv", [128], BF), ("kap", [6, B], BF), ("am", [B], BF), ("eps", [B], F),
+        ("thm", [4], BF), ("zab", [B, 3, 2], I)):
     SCRATCH[_n] = ("sbuf", [128] + _s, _t)
 for _h in "01":
     for _n, _s, _t in (
             ("cmp", [752], BF), ("dv", [752], BF), ("eg", [752], BF), ("xr", [752], BF), ("xo", [2, 16 * (47 - NO)], BF), ("ll", [96], U),
-            ("l2", [B], U), ("pl", [B], U), ("raw", [B, 2], I), ("ci", [3, B], I), ("zi", [B], I), ("pq", [B], I),
+            ("pl", [B], U), ("raw", [B, 2], I), ("ci", [3, B], I), ("zi", [B], I), ("pq", [B], I),
             ("xy", [96], F), ("lv", [96], F), ("tt", [192], F), ("mi", [2, 96], F), ("kk", [4, 52], F), ("fa", [6, B], F), ("aa", [B], BF), ("ce", [B], F),
-            ("el", [4], U), ("ex", [4, 48], F), ("md", [2, 24], F), ("cm", [32], BF), ("mc", [8], U), ("uc", [4], F), ("ne", [48], F)):
+            ("el", [4], U), ("ex", [4, 48], F), ("md", [2, 24], F), ("cm", [64], BF), ("mc", [10], U), ("uc", [6], F), ("mo", [32], F), ("ov", [2], BF)):
         SCRATCH[_n + _h] = ("sbuf", [128] + _s, _t)
     for _n in ("ps", "pc", "pf"):
         SCRATCH[_n + _h] = ("psum", [128, 512], F)
@@ -81,23 +83,27 @@ def build(g, core, T, topo, rank):
     queued = [0.0]
 
     def dma(q, name, out, in_, r, w, nbytes, ahead=True):
-        queued[0] = (queued[0] if ahead else 0.0) + nbytes
+        queued[0] = (queued[0] if ahead else 0.0) + nbytes + 60000
         add(q, name, lambda: (g.sync if q == "y" else g.scalar).dma_start(out, in_), r, w, fix=60.0, byt=queued[0], kind="d")
 
     def gp(name, fn, r, w, k):
         add("g", name, fn, r, w, fix=170.0, cyc=2 * k)
 
+    def gset(name, ap, val, w, k):
+        gp(name, lambda: g.iota(ap, [[0, k]], val, 0, allow_small_or_imprecise_dtypes=True), [], w, k)
+
+    def gsel(name, out, in_, val, r, w, k):
+        gp(name, lambda: g.affine_select(out, in_, [[0, k]], ALU.is_ge, val or 0.0, 0 if val is None else -1, 0), r, w, k)
+
     dma("y", "ld_boat", T.bt[:], T.boat[:], [], ["bt"], 49152)
     dma("s", "ld_x", T.xn[:], T.x[:], [], ["xn"], 393216)
-    Q = W // len(ENC_CP)
-    ekeys = [(Q * i, "e%d" % i) for i in range(len(ENC_CP))] + [(W + Q * i, "f%d" % i) for i in range(len(ENC_CP))] + [(2 * W, "t0"), (9008, "t1")]
-    for i in range(len(ENC_CP)):
-        dma("y", "ld_enc", T.encw[:, Q * i:Q * i + Q], T.enc[:, Q * i:Q * i + Q], [], ["e%d" % i], Q * 256)
-    for i, who in enumerate(ENC_CP):
-        if who is None:
-            dma("y", "ld_rep", T.encw[:, W + Q * i:W + Q * i + Q], T.enc[:, Q * i:Q * i + Q], ["e2"], ["f%d" % i], Q * 256, False)
-    for i, (a, b_) in enumerate(((2 * W, 9008), (9008, EW))):
-        dma("y", "ld_tail", T.encw[:, a:b_], T.enc[:, a - 2 * W:b_ - 2 * W], ["e2"], ["t%d" % i], (b_ - a) * 256)
+    ekeys = [(0, "e0"), (ENC_A, "e1")] + [(a, "f%d" % a) for a, b_, who in ENC_CP]
+    for i, (a, b_) in enumerate(((0, ENC_A), (ENC_A, W))):
+        dma("y", "ld_enc", T.encw[:, a:b_], T.enc[:, a:b_], [], ["e%d" % i], (b_ - a) * 256)
+    queued[0] = (W - ENC_A) * 256
+    for a, b_, who in ENC_CP:
+        if who == "y":
+            dma("y", "ld_rep", T.encw[:, a:b_], T.enc[:, a % W:a % W + b_ - a], ["e0"], ["f%d" % a], (b_ - a) * 256)
 
     def ewin(end):
         return T.encw[:, 0:end], [k for (a, k) in ekeys if a < end]
@@ -114,121 +120,126 @@ def build(g, core, T, topo, rank):
     mset("eps", T.eps[:], EPS, ["eps"])
     kaps = {}
     for (d, k), ns in sorted(NS.items()):
-        key = (k == 0, ns, int((d, k) == (1, 0)))
+        key = (k == 0, ns)
         if key not in kaps:
             i = kaps[key] = len(kaps)
-            mset("kap", T.kap[:, i, ns + key[2]:B], 4.5 / 16 - key[0], ["kap%d" % i])
-            mset("kap", T.kap[:, i, key[2]:ns + key[2]], 9.0 / 16 - key[0], ["kas%d" % i])
-            if key[2]:
-                mset("kap", T.kap[:, i, 0:1], 4.5 / 16 - key[0], ["kao"])
+            mset("kap", T.kap[:, i, ns:B], 4.5 / 16 - key[0], ["kap%d" % i])
+            mset("kap", T.kap[:, i, 0:ns], 9.0 / 16 - key[0], ["kas%d" % i])
     early[0] = False
     up, down = rank > 0, rank < n - 1
     for e, t in enumerate((11.5 if up else 1000.0, 4.5 if down else -1000.0)):
-        mset("thm", T.thm[:, e:e + 1], -t / 16, ["thm%d" % e])
+        gsel("thm", T.thm[:, e:e + 1], T.ones[:, 0:1], -t / 16, ["ones"], ["thm%d" % e], 1)
+    gsel("thm", T.thm[:, 2:4], T.ones[:, 0:2], -11.5 / 16, ["ones"], ["thm2"], 2)
     for d in range(2):
         for h in range(2):
-            mset("sent", T["xw%d" % d][:, h * HW:h * HW + 16], 255.0, ["sn%d%d" % (d, h)])
+            gset("sent", T["xw%d" % d][:, h * HW:h * HW + 16], 255, ["sn%d%d" % (d, h)], 16)
     for H in "01":
         for e in ([] if down else [1]) + ([] if up else [0]):
             mset("ex", T["ex" + H][:, e:4:2, 24 * e:24 * e + 24], 0.0, ["exz0" + H, "exz1" + H])
             ops[-1]["extra"] = True
         for e in range(2):
-            mset("pad", T["ex" + H][:, e:4:2, 43 - 24 * e:48 - 24 * e], 0.0, ["pad" + H])
-        mset("mi", T["mi" + H][:, :, 0:96:2], 1.0, ["m%s1" % H, "m%s2" % H], 96)
-        mset("kk", T["kk" + H][:, :, 0:49:48], 0.0, ["k%s%d" % (H, i) for i in range(3)])
+            gset("pad", T["ex" + H][:, e:4:2, 43 - 24 * e:48 - 24 * e], 0, ["pad%d" % e + H], 10)
+        gset("mi", T["mi" + H][:, :, 0:96:2], 1, ["m%s1" % H, "m%s2" % H], 96)
+        gset("kk", T["kk" + H][:, :, 0:49:48], 0, ["k%s%d" % (H, i) for i in range(3)], 8)
         mset("sh", T["pc" + H][:, 63:64], BIG, ["s0" + H, "pc" + H])
-        mset("lo", T["lv" + H][:, 1:96:2], -BIG, ["lo" + H])
-    for nm, val in (("idn", -1.0), ("idw", -16.0 * BIG), ("idb", -HALF), ("idc", HALF), ("idf", 1.0), ("idg", -1.0), ("idh", 2048.0), ("idi", -2048.0)):
+        gset("lo", T["lv" + H][:, 1:96:2], -2 ** 23, ["lo" + H], B)
+    for nm, val in (("idn", -1.0), ("idw", -16.0 * BIG), ("idb", -HALF), ("idc", HALF), ("idf", 1.0), ("idg", -1.0), ("idh", 2048.0), ("idi", -2048.0),
+                    ("idu", 48.0 * BIG), ("idv", -48.0 * BIG)):
         act(nm, T[nm][:], T.idp[:], ACT.Identity, ["idp"], [nm], 128, scale=val)
     ts("r", T.pi[:, 1:2], T.pi[:, 0:1], 15, None, ALU.bitwise_and, None, ["pi0"], ["pi1"])
-    for i, c in enumerate((16.0, 16.0 + HW, 0.0, 24.0)):
-        ts("rc", T.rc[:, i:i + 1], T.pi[:, 1:2], c, None, ALU.add, None, ["pi1"], ["rc%d" % i])
-    ts("bc", T.bc[:], T.bi[:], 65536.0, None, ALU.mult, None, ["bi"], ["bc"])
-    ts("ni", T.nn[:, 0, 1:96:2], T.bi[:], 16.0, T.rc[:, 0:1], ALU.mult, ALU.add, ["bi", "rc0"], ["ni"])
+    ts("rc", T.rc[:, 0:1], T.pi[:, 1:2], 16.0, None, ALU.add, None, ["pi1"], ["rc0"])
+    for i, c in ((1, 1.0 * HW), (2, -16.0), (3, 8.0)):
+        act("rc", T.rc[:, i:i + 1], T.rc[:, 0:1], ACT.Identity, ["rc0"], ["rc%d" % i], bias=c)
+    act("bc", T.bc[:], T.bi[:], ACT.Identity, ["bi"], ["bc"], scale=65536.0)
+    act("ni", T.nn[:, 0, 1:96:2], T.bi[:], ACT.Identity, ["bi", "rc0"], ["ni"], scale=16.0, bias=T.rc[:, 0:1])
     act("ni", T.nn[:, 0, 0:96:2], T.nn[:, 0, 1:96:2], ACT.Identity, ["ni"], ["nn0"], scale=-1.0)
     act("ni", T.nn[:, 1, 0:96:2], T.nn[:, 0, 1:96:2], ACT.Identity, ["ni"], ["nj"], scale=-1.0, bias=2048.0)
     act("ni", T.nn[:, 1, 1:96:2], T.nn[:, 1, 0:96:2], ACT.Identity, ["nj"], ["nn1"], scale=-1.0)
-    for i, who in enumerate(ENC_CP):
-        o, s = T.encw[:, W + Q * i:W + Q * i + Q], T.encw[:, Q * i:Q * i + Q]
+    for a, b_, who in ENC_CP:
+        o, s, e = T.encw[:, a:b_], T.encw[:, a % W:a % W + b_ - a], ["e0" if a % W < ENC_A else "e1"]
         if who == "v":
-            cp("rep", o, s, ["e%d" % i], ["f%d" % i], Q / 2)
+            cp("rep", o, s, e, ["f%d" % a], (b_ - a) / 2)
         elif who == "s":
-            act("rep", o, s, ACT.Identity, ["e%d" % i], ["f%d" % i], Q)
+            act("rep", o, s, ACT.Identity, e, ["f%d" % a], b_ - a)
+        elif who == "g":
+            gsel("rep", o, s, None, e, ["f%d" % a], b_ - a)
 
     zab = T.zab
 
     def xk(d, h):
         return [s + "%d%d" % (d, h) for s in ("sn", "xa", "xb", "xh", "xf")]
 
-    def numbers(h, src, rk, t):
+    def numbers(h, src, rk, t, step=1):
         raw, H = T["raw%d" % h], str(h)
-        ts("rawa" + H, raw[:, :, 0], src, 37.0, 811.0 * t, ALU.mult, ALU.add, rk, ["rawa" + H])
-        ts("rawb" + H, raw[:, :, 1], src, 101.0, None, ALU.mult, None, rk, ["rawb" + H])
-        ts("ab" + H, zab[:, :, 1:3, h], raw[:], W - 1, None, ALU.bitwise_and, None, ["rawa" + H, "rawb" + H], ["ab" + H], 2 * B)
+        ts("rawa" + H, raw[:, ::step, 0], src, 37.0, 811.0 * t, ALU.mult, ALU.add, rk, ["rawa" + H])
+        ts("rawb" + H, raw[:, ::step, 1], src, 101.0, None, ALU.mult, None, rk, ["rawb" + H])
+        ts("ab" + H, zab[:, ::step, 1:3, h], raw[:, ::step, :], W - 1, None, ALU.bitwise_and, None, ["rawa" + H, "rawb" + H], ["ab" + H], 2 * B / step)
 
     def day_start(d, h):
         H = str(h)
         xy, fa, ci, ll = T["xy" + H], T["fa" + H], T["ci" + H], T["ll" + H]
-        z, zk = (T.bt[:, :, h], ["bt"]) if d == 0 else (zab[:, :, 0, h], ["z" + H, "nz0" + H, "nz1" + H])
-        tt("y" + H, xy[:, 1:94:2], zab[:, 0:47, 2, h], zab[:, 1:48, 1, h], ALU.add, ["ab" + H, "nr0" + H, "nr1" + H], ["xy1" + H], 94)
+        z, zk = (T.bt[:, :, h], ["bt"]) if d == 0 else (zab[:, :, 0, h], ["z" + H])
+        tt("y" + H, xy[:, 1:94:2], zab[:, 0:47, 2, h], zab[:, 1:48, 1, h], ALU.add, ["ab" + H], ["xy1" + H], 94)
         if d == 0:
             cp("c0a" + H, ci[:, 0, 0:47], xy[:, 1:94:2], ["xy1" + H], ["ci0" + H])
             ts("c0b" + H, ci[:, 1, 0:47], ci[:, 0, 0:47], W - 1, None, ALU.bitwise_and, None, ["ci0" + H], ["ci1" + H])
             cp("c0" + H, ll[:, 0:47], ci[:, 1, 0:47], ["ci1" + H], ["ll" + H])
-            act("own" + H, T["xo" + H][:, 0, :], T.xn[:, NO + 1:B, h, :], ACT.Identity, ["xn"], ["xo0" + H], 16 * (47 - NO))
+            gsel("own" + H, T["xo" + H][:, 0, :], T.xn[:, NO + 1:B, h, :], None, ["xn"], ["xo0" + H], 16 * (47 - NO))
         else:
+            cp("c0" + H, ll[:, 0:47], xy[:, 1:94:2], ["xy1" + H], ["ll" + H])
             dma("y", "own" + H, T["xo" + H][:, 1, 0:16 * (46 - NO)], T.xw1[:, h * HW + 32 + 16 * NO:(h + 1) * HW - 16], xk(d, h)[1:3], ["xo1" + H],
                 4096 * (46 - NO), False)
-        tt("sx" + H, fa[:, 0, 0:47], zab[:, 0:47, 1, h], zab[:, 0:47, 2, h], ALU.add, ["ab" + H, "nr0" + H], ["sx" + H], 94)
+        tt("sx" + H, fa[:, 0, 0:47], zab[:, 0:47, 1, h], zab[:, 0:47, 2, h], ALU.add, ["ab" + H], ["sx" + H], 94)
         act("x" + H, xy[:, 0:94:2], fa[:, 0, 0:47], ACT.Identity, ["sx" + H], ["xy0" + H], scale=-1.0)
         tt("zz" + H, fa[:, 1, :], z, T.bc[:], ALU.add, zk + ["bc"], ["zz" + H], 96)
-        tt("dz" + H, fa[:, 2, 1:48], fa[:, 1, 0:47], fa[:, 1, 1:48], ALU.subtract, ["zz" + H], ["dz" + H], 94)
+        race(d, 0, h)
 
-    def adjacent(d, h, b0, b1, rk, wk):
-        xw, o, ns = T["xw%d" % d], h * HW, (NS[(d, 0)] if b0 > 1 else 0)
-        tt("d%d_%d" % (b0, h), T["dv%d" % h][:, 16 * (b0 - 1 - ns):16 * (b1 - 1 - ns)], xw[:, o + 16 * b0:o + 16 * b1],
-           xw[:, o + 16 + 16 * b0:o + 16 + 16 * b1], ALU.subtract, rk, wk, 32 * (b1 - b0))
+    def adjacent(d, h):
+        xw, o, b0 = T["xw%d" % d], h * HW, NS[(d, 0)] + 1
+        a, b = (xw[:, o + 16 * b0:o + 16 * B], xw[:, o + 16 + 16 * b0:o + HW]) if d else (T.xn[:, b0 - 1:B - 1, h, :], T.xn[:, b0:B, h, :])
+        tt("d%d%d" % (d, h), T["dv%d" % h][:, 0:16 * (B - b0)], a, b, ALU.subtract, xk(d, h) if d else ["xn"], ["dv%d" % h], 32 * (B - b0))
 
-    def interval(d, k, h):
-        H, ns = str(h), NS[(d, k)]
-        s0 = int((d, k) == (1, 0))
+    def race(d, k, h):
+        H, ns, s0 = str(h), NS[(d, k)], (d, k) == (1, 0)
         nv, xw, o = 47 - ns, T["xw%d" % d], h * HW
         win = xw[:, o:o + HW]
-        cmp_, dv, eg, xr, ll, tb = [T[s + H] for s in ("cmp", "dv", "eg", "xr", "ll", "tt")]
-        ps, pc, pf, fa, kk, mi, aa = [T[s + H] for s in ("ps", "pc", "pf", "fa", "kk", "mi", "aa")]
+        cmp_, dv, eg, xr, ll, ps, pc, pf, aa = [T[s + H] for s in ("cmp", "dv", "eg", "xr", "ll", "ps", "pc", "pf", "aa")]
         ew, ek = ewin(W if (d, k) == (0, 0) else (2 * W + 811 * k + 15) // 16 * 16)
         X, tag = xk(d, h), "%d%d%d" % (d, k, h)
-        XS, ls, lk = (X[1:3], T["l2" + H], "l2" + H) if s0 else (X, ll, "ll" + H)
-        ka = kaps[(k == 0, ns, s0)]
+        ka = kaps[(k == 0, ns)]
         if k == 1:
             mm("hold" + tag, [(pc[:, 192:288], T.idf[:], T.nn[:, 1, :], True, False, 4), (pc[:, 192:288:2], T.idh[:], aa[:], False, False, 1),
                               (pc[:, 193:288:2], T.idi[:], aa[:], False, True, 1)], ["idf", "idh", "idi", "nn1", "aa" + H], ["pc" + H, "s" + H, "hold" + H])
         mm("cn0" + tag, [(pc[:, 0:47], T.idw[:], T.kap[:, ka, 0:47], True, False, 1)] + [(pc[:, 0:47], T.idw[:], aa[:, 1:48], False, False, 1)][:k],
-           ["idw", "kap%d" % ka, "kas%d" % ka, "kao"] + ["aa" + H][:k], ["pc" + H, "s" + H, "hold" + H])
-        if k > 0:
-            vgt("gd" + tag, dv[:, 0:16 * nv], win, ll[:, 48 + ns:95], T["xo" + H][:, d, 16 * (ns - NO):16 * (47 - NO)], ALU.subtract,
-                X + ["lr" + H, "xo%d" % d + H, "xp%d" % d + H], ["dv" + H, "dw" + H, "dx" + H], 16 * nv)
+           ["idw", "kap%d" % ka, "kas%d" % ka] + ["aa" + H][:k], ["pc" + H, "s" + H, "hold" + H])
+        cuts = [ns + (nv * i // VP[k > 0]) // 2 * 2 for i in range(VP[k > 0])] + [47]
+        for i, (u0, u1) in enumerate(zip(cuts, cuts[1:])):
+            a0, a1, DV = 16 * (u0 - ns), 16 * (u1 - ns), ["dv%d" % i + H]
+            if k > 0:
+                vgt("gd%d" % i + tag, dv[:, a0:a1], win, ll[:, 48 + u0:48 + u1], T["xo" + H][:, d, 16 * (u0 - NO):16 * (u1 - NO)], ALU.subtract,
+                    X + ["lr" + H, "xo%d" % d + H, "xp%d" % d + H], DV, a1 - a0)
+            vgt("gc%d" % i + tag, cmp_[:, 16 * u0:16 * u1], ew, ll[:, u0:u1], dv[:, a0:a1], ALU.is_gt,
+                ek + ["ll" + H, "dv" + H] + DV, ["cv%d" % i + H], a1 - a0)
         n1 = int(ns * SPLIT) // 2 * 2
         for C, u0, u1, pp, pk in (("0", 0, n1, ps, "ps" + H), ("1", n1, ns, pf if s0 else (T.pmw, T.pmc)[h], "pf" + H if s0 else ("pmw", "pmc")[h])):
             a0, a1 = 16 * u0, 16 * u1
-            c0, out = o + 16 + 16 * s0, pp[:, 0:a1 - a0]
+            c0, out = o + 16, pp[:, 0:a1 - a0]
             if k > 0:
                 sgc("gx" + C + tag, xr[:, a0:a1], win, ll[:, 48 + u0:48 + u1], X + ["lr" + H], ["xr" + C + H], a1 - a0)
             mm("su0" + C + tag, [(out, T.idp[:], xw[:, c0 + 16 + a0:c0 + 16 + a1], True, False, 1),
                                  (out, T.idn[:], xr[:, a0:a1] if k else xw[:, c0 + a0:c0 + a1], False, False, 1)],
-               XS + ["xr" + C + H][:k] + ["idp", "idn"], [pk])
-            sgc("ge" + C + tag, eg[:, a0:a1], ew, ls[:, u0:u1], ek + [lk], ["eg" + C + H], a1 - a0)
+               X + ["xr" + C + H][:k] + ["idp", "idn"], [pk])
+            sgc("ge" + C + tag, eg[:, a0:a1], ew, ll[:, u0:u1], ek + ["ll" + H], ["eg" + C + H], a1 - a0)
             mm("su1" + C + tag, [(out, T.idp[:], eg[:, a0:a1], False, True, 1)], ["eg" + C + H, "idp", pk], [pk])
-            act("sg" + C + tag, cmp_[:, 16 * s0 + a0:16 * s0 + a1], out, ACT.Sign, [pk], ["cs" + C + H], a1 - a0, bias=-0.5)
-        if not s0:
-            vgt("gc" + tag, cmp_[:, 16 * ns:752], ew, ll[:, ns:47], dv[:, 0:16 * nv], ALU.is_gt,
-                ek + ["ll" + H, "dv" + H, "dw" + H, "dx" + H], ["cv" + H, "cx" + H, "cy" + H], 16 * nv)
-        else:
-            vgt("gc" + tag, cmp_[:, 16 * ns + 16:736], ew, ls[:, ns:45], dv[:, 16:16 * nv - 16], ALU.is_gt, ek + [lk, "dv" + H], ["cv" + H], 16 * nv - 32)
-            vgt("gz" + tag, cmp_[:, 736:752], ew, ll[:, 46:47], dv[:, 16 * nv - 16:16 * nv], ALU.is_gt, ek + ["ll" + H, "dw" + H], ["cy" + H], 16)
-            vgt("gb" + tag, cmp_[:, 0:16], ew, ll[:, 0:1], dv[:, 0:16], ALU.is_gt, ek + ["ll" + H, "l0" + H, "dx" + H], ["cx" + H], 16)
-        mm("cnt" + tag, [(pc[:, 0:47], T.usel[:, 15 - r:143 - r], cmp_[:, r:752:16], False, r == 15, 1) for r in range(16)],
-           ["usel", "cs0" + H, "cs1" + H, "cv" + H, "cx" + H, "cy" + H, "pc" + H], ["pc" + H])
+            act("sg" + C + tag, cmp_[:, a0:a1], out, ACT.Sign, [pk], ["cs" + C + H], a1 - a0, bias=-0.5)
+        mm("cnt" + tag, [(pc[:, 0:47], T.usel[:, 15 - r:143 - r], cmp_[:, r:752:16], False, r == 15 and not s0, 1) for r in range(16)],
+           ["usel", "cs0" + H, "cs1" + H, "cv0" + H, "cv1" + H, "cv2" + H, "pc" + H], ["pc" + H])
+
+    def settle(d, k, h):
+        H, tag = str(h), "%d%d%d" % (d, k, h)
+        ll, tb, pc, pf, fa, kk, mi, aa = [T[s + H] for s in ("ll", "tt", "pc", "pf", "fa", "kk", "mi", "aa")]
+        if k == 0:
+            tt("dz" + H, fa[:, 2, 1:48], fa[:, 1, 0:47], fa[:, 1, 1:48], ALU.subtract, ["zz" + H, "nz0" + H, "nz1" + H], ["dz" + H], 94)
         a_, ak = (T.am, "am") if k == 0 else (aa, "aa" + H)
         scan("s" + tag, pc[:, 64:111], a_[:, 1:48], pc[:, 0:47], BIG, ALU.mult, ALU.max, [ak, "pc" + H], ["s" + H])
         fm, fk = (fa[:, 2, 1:48], "dz" + H) if k == 0 else (fa[:, 3, 1:48], "fm" + H)
@@ -248,19 +259,21 @@ def build(g, core, T, topo, rank):
         scan("sr" + tag, tb[:, 96:190], pc[:, 192:286] if k else T.nn[:, 0, 0:94], lv[:, 0:94], 0.0, ALU.add, ALU.max,
              ["l" + H, "lo" + H, "nn0", "hold" + H], ["sr" + H], 94)
         ts("lr" + tag, ll[:, 48:95], tb[:, 97:190:2], 0.25, None, ALU.add, None, ["sr" + H], ["lr" + H])
-        scan("sc" + tag, tb[:, 0:94], mi[:, k, 0:94], T["xy" + H][:, 0:94], 0.0, ALU.mult, ALU.add, [mk, "xy0" + H, "xy1" + H], ["sc" + H], 94)
+        scan("sc" + tag, tb[:, 0:94], mi[:, k, 0:94], T["xy" + H][:, 0:94], 0.0, ALU.mult, ALU.add, [mk, "xy0" + H, "xy1" + H, "ny0" + H, "ny1" + H],
+             ["sc" + H], 94)
         ts("ll" + tag, ll[:, 0:47], tb[:, 1:94:2], N, 0.0, ALU.add, ALU.max, ["sc" + H], ["ll" + H])
         act("a" + tag, aa[:], mi[:, k, 1:96:2], ACT.Identity, [mk], ["aa" + H], bias=-1.0, scale=2.0)
-        mm("fd" + tag, [(pf[:, 0:47], T.idf[:], fa[:, 2, 1:48], True, False, 4), (pf[:, 0:47], T.idc[:], aa[:, 1:48], False, False, 1),
-                        (pf[:, 0:47], T.idb[:], aa[:, 0:47], False, True, 1)], ["idf", "idb", "idc", "dz" + H, "aa" + H], ["pf" + H])
-        scan("f" + tag, fa[:, 3, 1:48], mi[:, k, 1:94:2], pf[:, 0:47], 2 * HALF, ALU.mult, ALU.add, [mk, "pf" + H], ["fm" + H])
         if k == 0:
             act("ce" + tag, T["ce" + H][:], mi[:, k, 1:96:2], ACT.Identity, [mk], ["ce" + H], bias=EPS, scale=1.0 - EPS)
         else:
-            mm("br" + tag, [(pf[:, 0:48], T.idf[:], fa[:, 1, :], True, False, 4), (pf[:, 0:48], T.idg[:], kk[:, 0, 0:48], False, False, 4),
-                            (pf[:, 0:48], T.idf[:], kk[:, 0, 1:49], False, False, 4)], ["idf", "idg", "zz" + H, "k%s0" % H], ["pf" + H])
-            mm("bs" + tag, [(pf[:, 0:48], T.idf[:], kk[:, 1, 0:48], False, False, 4),
-                            (pf[:, 0:48], T.idg[:], kk[:, 1, 1:49], False, True, 4)], ["idf", "idg", "k%s1" % H], ["pf" + H])
+            p1 = pf[:, 64:112]
+            mm("br" + tag, [(p1, T.idf[:], fa[:, 1, :], True, False, 4), (p1, T.idg[:], kk[:, 0, 0:48], False, False, 4),
+                            (p1, T.idf[:], kk[:, 0, 1:49], False, False, 4)], ["idf", "idg", "zz" + H, "dz" + H, "k%s0" % H], ["pf" + H])
+            mm("bs" + tag, [(p1, T.idf[:], kk[:, 1, 0:48], False, False, 4), (p1, T.idg[:], kk[:, 1, 1:49], False, True, 4)],
+               ["idf", "idg", "k%s1" % H], ["pf" + H])
+        mm("fd" + tag, [(pf[:, 0:47], T.idf[:], fa[:, 2, 1:48], True, False, 4), (pf[:, 0:47], T.idc[:], aa[:, 1:48], False, False, 1),
+                        (pf[:, 0:47], T.idb[:], aa[:, 0:47], False, True, 1)], ["idf", "idb", "idc", "dz" + H, "aa" + H], ["pf" + H])
+        scan("f" + tag, fa[:, 3, 1:48], mi[:, k, 1:94:2], pf[:, 0:47], 2 * HALF, ALU.mult, ALU.add, [mk, "pf" + H], ["fm" + H, "pf1" + H])
 
     def neighbours(r):
         nb = [(r - 1, 0)][:r] + [(r + 1, 1)][:n - 1 - r]
@@ -288,86 +301,100 @@ def build(g, core, T, topo, rank):
         pf, kk, zi, pq, pl, el, ex = [T[s + H] for s in ("pf", "kk", "zi", "pq", "pl", "el", "ex")]
         o, X = h * HW, xk(d, h)
         win = T["xw%d" % d][:, o:o + HW]
-        tt("z0" + tag, pf[:, 64:112], pf[:, 0:48], kk[:, 2, 0:48], ALU.add, ["pf" + H, "k%s2" % H], ["pf" + H])
-        tt("zi" + tag, zi[:], pf[:, 64:112], kk[:, 2, 1:49], ALU.subtract, ["pf" + H, "k%s2" % H], ["zi" + H])
+        tt("z0" + tag, pf[:, 128:176], pf[:, 64:112], kk[:, 2, 0:48], ALU.add, ["pf" + H, "k%s2" % H], ["pf" + H])
+        tt("zi" + tag, zi[:], pf[:, 128:176], kk[:, 2, 1:49], ALU.subtract, ["pf" + H, "k%s2" % H], ["zi" + H])
         ts("pq" + tag, pq[:], zi[:], 12, 0xFF0, ALU.logical_shift_right, ALU.bitwise_and, ["zi" + H], ["pq" + H])
-        ts("el" + tag, el[:, 0:4:2], pq[:, 0:48:47], T.rc[:, 0:1], None, ALU.add, None, ["pq" + H, "rc0"], ["el" + H])
-        ts("zq" + tag, zab[:, :, 0, h], zi[:], 65535, None, ALU.bitwise_and, None, ["zi" + H], ["z" + H])
-        numbers(h, zab[:, :, 0, h], ["z" + H], 3 if d == 0 else 7)
+        if d == 0:
+            step, pe, pk = 1, pq[:, 0:48:47], "pq" + H
+            ts("zq" + tag, zab[:, :, 0, h], zi[:], 65535, None, ALU.bitwise_and, None, ["zi" + H], ["z" + H])
+        else:
+            step, pe, pk, ci = 47, T["ci" + H][:, 2, 0:2], "pe" + H, T["ci" + H]
+            ts("zh" + tag, ci[:, 1, 0:1], kk[:, 2, 1:2], -1.0, pf[:, 64:65], ALU.mult, ALU.add, ["pf1" + H, "k%s2" % H], ["zh" + H])
+            ts("zt" + tag, ci[:, 1, 1:2], kk[:, 2, 47:48], pf[:, 111:112], None, ALU.add, None, ["pf1" + H, "k%s2" % H], ["zt" + H])
+            ts("pe" + tag, pe, ci[:, 1, 0:2], 12, 0xFF0, ALU.logical_shift_right, ALU.bitwise_and, ["zh" + H, "zt" + H], [pk])
+            ts("ze" + tag, zab[:, ::47, 0, h], ci[:, 1, 0:2], 65535, None, ALU.bitwise_and, None, ["zh" + H, "zt" + H], ["z" + H])
+            ts("zq" + tag, ci[:, 0, :], zi[:], 65535, None, ALU.bitwise_and, None, ["zi" + H], ["zq" + H])
+        ts("el" + tag, el[:, 0:4:2], pe, T.rc[:, 0:1], None, ALU.add, None, [pk, "rc0"], ["el" + H])
+        numbers(h, zab[:, ::step, 0, h], ["z" + H], 3 if d == 0 else 7, step)
         for e in range(2):
             c = 24 - 24 * e
             sgc("ew%d" % e + tag, ex[:, 2 * d + e, c:c + 16], win, el[:, 2 * e:2 * e + 1], X + ["el" + H], ["ew%d" % e + tag], 16)
             cp("ez%d" % e + tag, ex[:, 2 * d + e, c + 16:c + 19], zab[:, 47 * e, :, h], ["z" + H, "ab" + H], ["ez%d" % e + tag])
         if d == 0:
-            pv, ns = B - PERM_V, NS[(1, 0)]
+            pv = B - PERM_V
             ts("pl" + tag, pl[:], pq[:], T.rc[:, 0:1], None, ALU.add, None, ["pq" + H, "rc0"], ["pl" + H])
             sgc("pa" + tag, T.xw1[:, o + 16:o + 16 + 16 * pv], win, pl[:, 0:pv], X + ["pl" + H], ["xa1" + H, "xh1" + H], 16 * pv)
             vgc("pb" + tag, T.xw1[:, o + 16 + 16 * pv:o + HW], win, pl[:, pv:B], X + ["pl" + H], ["xb1" + H, "xf1" + H], 16 * PERM_V)
-            adjacent(1, h, ns + 2, 47, ["xa1" + H, "xb1" + H], ["dv" + H])
-            tt("ye" + H, T["fa" + H][:, 5, 0:45], zab[:, 1:46, 2, h], zab[:, 2:47, 1, h], ALU.add, ["ab" + H], ["ye" + H], 90)
-            cp("le" + H, T["l2" + H][:, 0:45], T["fa" + H][:, 5, 0:45], ["ye" + H], ["l2" + H])
+            adjacent(1, h)
         else:
             ts("pl" + tag, T.nat[:, h:96:2], pq[:], T.rc[:, h:h + 1], None, ALU.add, None, ["pq" + H, "rc" + H], ["nat" + H])
-            cp("zf" + tag, T.zf[:, :, h], zab[:, :, 0, h], ["z" + H], ["zf" + H])
+            cp("zf" + tag, T.zf[:, :, h], ci[:, 0, :], ["zq" + H], ["zf" + H])
 
     def meet(d, h):
         H, tag, o, e0 = str(h), "%d%d" % (d, h), h * HW, 2 * d
-        ex, md, cm, mc, uc, ne, ll, dv = [T[s + H] for s in ("ex", "md", "cm", "mc", "uc", "ne", "ll", "dv")]
-        pm, pk = (T.pmw, T.pmc)[h], ("pmw", "pmc")[h]
-        Z = ["ez0" + tag, "ez1" + tag, "pad" + H]
+        ex, md, cm, mc, uc, mo, pc = [T[s + H] for s in ("ex", "md", "cm", "mc", "uc", "mo", "pc")]
+        pm, pk, nm = (T.pmw, T.pmc)[h], ("pmw", "pmc")[h], 4 - 2 * d
+        Z = ["ez0" + tag, "ez1" + tag, "pad0" + H, "pad1" + H]
         A = Z + ["ew0" + tag, "ew1" + tag]
         exchange("arr" + tag, [ex[:, e0, 24:48], ex[:, e0 + 1, 0:24]], [ex[:, e0 + 1, 24:48], ex[:, e0, 0:24]], A)
         Z, A = Z + ["arr" + tag, "exz" + tag], A + ["arr" + tag, "exz" + tag]
         ew, ek = ewin(EW if d == 0 else 2 * W)
-        mm("mt" + tag, [(pm[:, 0:2], T.idw[:], T.thm[:], True, False, 1)], ["idw", "thm0", "thm1"], [pk])
-        tt("md" + tag, md[:], ex[:, e0:e0 + 2, 0:24], ex[:, e0:e0 + 2, 24:48], ALU.subtract, A, ["md" + H], 96)
+        mm("mt" + tag, [(pm[:, 0:nm], T.idw[:], T.thm[:, 0:nm], True, False, 1)], ["idw", "thm0", "thm1", "thm2"], [pk])
+        tt("md" + tag, md[:, :, 0:19], ex[:, e0:e0 + 2, 0:19], ex[:, e0:e0 + 2, 24:43], ALU.subtract, A, ["md" + H], 76)
         for e in range(2):
             E = str(e) + tag
             ts("mc" + E, mc[:, 2 * e:2 * e + 1], ex[:, e0 + e, 41:42], ex[:, e0 + e, 18:19], 811.0 * 3 * (1 - d), ALU.add, ALU.add, Z, ["mc%d" % e + H])
             vgt("m" + E, cm[:, 16 * e:16 * e + 16], ew, mc[:, 2 * e:2 * e + 1], md[:, e, 0:16], (ALU.is_gt, ALU.is_le)[e],
                 ek + ["mc%d" % e + H, "md" + H], ["cm%d" % e + H], 16)
-        mm("mq" + tag, [(pm[:, 0:2], T.usel[:, 15 - r:143 - r], cm[:, r:32:16], False, r == 15, 1) for r in range(16)],
-           ["usel", "cm0" + H, "cm1" + H], [pk])
+        if d == 0:
+            for e in range(2):
+                ts("ma%d" % e + tag, mc[:, 8 + e:9 + e], zab[:, 1 + 45 * e, 1 + e, h:h + 1], ex[:, e, 18 + 23 * e:19 + 23 * e], None, ALU.add, None,
+                   Z + ["ab" + H], ["ma%d" % e + H])
+            tt("mb0" + tag, mo[:, 0:16], ex[:, 0, 0:16], T.xw1[:, o + 32:o + 48], ALU.subtract, A + ["xa1" + H], ["mb0" + H])
+            tt("mb1" + tag, mo[:, 16:32], T.xw1[:, o + HW - 32:o + HW - 16], ex[:, 1, 24:40], ALU.subtract, A + ["xa1" + H, "xb1" + H], ["mb1" + H])
+            vgt("mo" + tag, cm[:, 32:64], ew, mc[:, 8:10], mo[:], ALU.is_gt, ek + [s + H for s in ("ma0", "ma1", "mb0", "mb1")], ["cm2" + H], 32)
+        mm("mq" + tag, [(pm[:, 0:nm], T.usel[:, 15 - r:143 - r], cm[:, r:16 * nm:16], False, r == 15, 1) for r in range(16)],
+           ["usel", "cm0" + H, "cm1" + H, "cm2" + H], [pk])
         ts("mi" + tag, mc[:, 4:8:2], pm[:, 0:2], T.rc[:, 2:3], T.rc[:, 3:4], ALU.max, ALU.min, [pk, "rc2", "rc3"], ["mi" + H])
-        ts("uc" + tag, uc[:, 0:2], pm[:, 0:2], 0.0, None, ALU.is_lt, None, [pk], ["uc" + H])
 
         def pick(name, out, e, f, base, r, w):
-            ts(name + str(e) + tag, out, uc[:, e:e + 1], md[:, e, 16 + f:17 + f], base, ALU.mult, ALU.add, ["uc" + H, "md" + H] + Z + r, w)
+            ts(name + str(e) + tag, out, uc[:, e:e + 1], md[:, e, 16 + f:17 + f], base, ALU.mult, ALU.add, ["uc%d" % e + H, "md" + H] + r, w)
         A = A + ["mi" + H]
+        if d == 1:
+            ts("uc" + tag, uc[:, 0:2], pm[:, 0:2], 0.0, None, ALU.is_lt, None, [pk], ["uc0" + H, "uc1" + H])
         for e in range(2):
-            win, lst, b, f = ex[:, e0 + e, :], mc[:, 4 + 2 * e:5 + 2 * e], 47 * e, 2 - e
+            win, lst, b = ex[:, e0 + e, :], mc[:, 4 + 2 * e:5 + 2 * e], 47 * e
             if d == 1:
                 (vgc, sgc)[e]("new%d" % e + tag, T.ye[:, 32 * e + 16 * h:32 * e + 16 * h + 16], win, lst, A, ["ye%d" % e + H], 16)
-                pick("nz", T.zf[:, b, h:h + 1], e, 0, ex[:, e0 + e, 40:41], ["zf" + H], ["zf%d" % e + H])
+                pick("nz", T.zf[:, b, h:h + 1], e, 0, ex[:, e0 + e, 40:41], Z + ["zf" + H], ["zf%d" % e + H])
                 continue
-            ts("pre%d" % e + tag, uc[:, 2 + e:3 + e], zab[:, 1 + 45 * e, 1 + e, h:h + 1], ex[:, e, 40 + f:41 + f], None, ALU.add, None,
-               Z + ["ab" + H], ["pre%d" % e + H])
-            pick("nc", ll[:, 46 * e:46 * e + 1], e, f, uc[:, 2 + e:3 + e], ["pre%d" % e + H], [("l0", "ll")[e] + H])
-            c = o + 16 + 16 * b
+            ts("uc%d" % e + tag, uc[:, e:e + 1], pm[:, e:e + 1], 0.0, 1.0 - 2 * e, (ALU.is_lt, ALU.is_ge)[e], ALU.mult, [pk], ["uc%d" % e + H])
+            c, zz, y = o + 16 + 16 * b, T["fa" + H][:, 1, b:b + 1], T["xy" + H][:, 1 + 92 * e:2 + 92 * e]
             sgc("new%d" % e + tag, T.xw1[:, c:c + 16], win, lst, A, [("xh1", "xf1")[e] + H], 16)
-            pick("nz", zab[:, b, 0, h:h + 1], e, 0, ex[:, e, 40:41], [], ["nz%d" % e + H])
-            pick("nr", zab[:, b, f, h:h + 1], e, f, ex[:, e, 40 + f:41 + f], [], ["nr%d" % e + H])
+            pick("nz", zz, e, 0, zz, ["zz" + H], ["nz%d" % e + H])
+            pick("ny", y, e, 2 - e, y, ["xy1" + H, "ll" + H], ["ny%d" % e + H])
         if d == 0:
-            nv = 47 - NS[(1, 0)]
-            vgt("dh" + tag, dv[:, 0:16], ex[:, 0, :], mc[:, 4:5], T.xw1[:, o + 32:o + 48], ALU.subtract, A + ["xa1" + H], ["dx" + H], 16)
-            act("ne" + tag, ne[:], ex[:, 1, :], ACT.Identity, A[:-1], ["ne" + H], scale=-1.0)
-            vgt("df" + tag, dv[:, 16 * nv - 16:16 * nv], ne[:], mc[:, 6:7], T.xw1[:, o + HW - 32:o + HW - 16], ALU.add,
-                ["ne" + H, "mi" + H, "xa1" + H, "xb1" + H], ["dw" + H], 16)
+            ov = T["ov" + H]
+            ts("ow" + tag, uc[:, 2:4], pm[:, 2:4], 0.0, 0.5, ALU.is_lt, ALU.subtract, [pk], ["ow" + H])
+            tt("ov" + tag, ov[:], uc[:, 2:4], uc[:, 0:2], ALU.mult, ["ow" + H, "uc0" + H, "uc1" + H], ["ov" + H])
+            mm("fix" + tag, [(pc[:, 0:1], T.idv[:], ov[:, 0:1], False, False, 1), (pc[:, 46:47], T.idu[:], ov[:, 1:2], False, True, 1)],
+               ["idu", "idv", "ov" + H], ["pc" + H])
             sgc("xo" + tag, T["xo" + H][:, 1, 16 * (46 - NO):16 * (47 - NO)], ex[:, 1, :], mc[:, 6:7], A, ["xp1" + H], 16)
 
     cp("xw0", T.xw0[:, 16:HW], T.xn[:, :, 0, :], ["xn"], xk(0, 0)[1:], 384)
     act("xw1", T.xw0[:, HW + 16:2 * HW], T.xn[:, :, 1, :], ACT.Identity, ["xn"], xk(0, 1)[1:], 768)
     for h in range(2):
         numbers(h, T.bt[:, :, h], ["bt"], 0)
-        adjacent(0, h, NS[(0, 0)] + 1, 48, xk(0, h), [s + str(h) for s in ("dv", "dw", "dx")])
-    for d in range(2):
-        for h in range(2):
-            day_start(d, h)
-        for k in range(3):
-            for h in range(2):
-                interval(d, k, h)
-        for h in range(2):
+        adjacent(0, h)
+        day_start(0, h)
+        for d in range(2):
+            for k in range(3):
+                settle(d, k, h)
+                if k < 2:
+                    race(d, k + 1, h)
             day_end(d, h)
+            if d == 0:
+                day_start(1, h)
             meet(d, h)
     X, c1 = xk(1, 0) + xk(1, 1) + ["nat0", "nat1"], 2 + FIN_V
     vgc("fv", T.ys[:, 32:16 * c1], T.xw1[:, 0:2 * HW], T.nat[:, 2:c1], X, ["ysv"], 16 * FIN_V)
@@ -499,8 +526,38 @@ def order(ops):
                     best = (c, cur)
         return best
 
-    starts = [moved(min(listed(tms[t % len(tms)]) for t in range(TRIES)), MOVES // 5) for s in range(STARTS)]
-    return moved(min(starts), MOVES)[1]
+    def filled(key, pre, tm, back):
+        at, slots = [None] * n, [[] for q in range(6)]
+        for i in sorted(range(n), key=lambda i: key[i]):
+            stack = [i]
+            while stack:
+                x = stack.pop()
+                p = [j for j in pre[x] if at[j] is None]
+                if p:
+                    stack += [x] + p
+                elif at[x] is None:
+                    t = max([at[j] + tm[j][1 - back] for j in pre[x]] + [0.0]) + back * (tm[x][1] - tm[x][0])
+                    s, k = slots[en[x]], 0
+                    while k < len(s) and s[k][0] < t + tm[x][0] - 1e-9:
+                        t, k = max(t, s[k][1]), k + 1
+                    s.insert(k, (t, t + tm[x][0]))
+                    at[x] = t
+        return at
+
+    def justified(seq, a):
+        late = filled([-e for e in length(seq, 0, None)[1][a][0]], succ, tms[a], 1)
+        at = filled([i - 1e9 if i < n0 else -late[i] - tms[a][i][0] for i in range(n)], dep, tms[a], 0)
+        seq = list(range(n0)) + sorted(range(n0, n), key=lambda i: (at[i], i))
+        return length(seq, 0, None)[0], seq
+
+    pool = sorted(justified(listed(tms[t % len(tms)])[1], t // len(tms) % len(tms)) for t in range(TRIES))
+    best = None
+    for b in pool[:STARTS]:
+        for t in range(2):
+            b = moved(b, MOVES)
+            b = min([b] + [justified(b[1], a) for a in range(len(tms))])
+        best = min(best or b, b)
+    return moved(best, 3 * MOVES)[1]
 
 
 def emit(g, T, ops, seq):

import math
from concourse.bass import DstId, RemoteDMATransfer
from concourse.mybir import AluOpType as ALU, ActivationFunctionType as ACT

B, V, W = 48, 1536, 4096
HW = 16 + 16 * B
EW = 10624
BIG, HALF, EPS = 2.0 ** 30, 2.0 ** 21, 2.0 ** -19
SPLIT = 0.7
VP = (1, 2)
NS = {(0, 0): 20, (0, 1): 24, (0, 2): 22, (1, 0): 42, (1, 1): 24, (1, 2): 22}
NO = min(NS.values())
PERM_V = 16
FIN_V = 38
ENC_A = 2048
ENC_CP = [(W, W + 1280, "v"), (W + 1280, W + 2048, "s"), (W + 2048, W + 2880, "g"), (W + 2880, 2 * W, "y"), (2 * W, 9008, "g"), (9008, EW, "y")]
TRIES, STARTS, MOVES = 200, 4, 5500
MODELS = [dict(f=1.0, g=1.56, wake=220.0, pe=0.42, dma=600.0, bw=450.0, rem=1000.0),
          dict(f=1.15, g=1.4, wake=190.0, pe=0.42, dma=1300.0, bw=230.0, rem=1800.0),
          dict(f=1.4, g=1.85, wake=210.0, pe=0.42, dma=800.0, bw=400.0, rem=1300.0)]

BF, F, I, U = "bfloat16", "float32", "int32", "uint16"
SCRATCH = {"pmw": ("psum", [128, 512], F), "pmc": ("psum", [128, 512], F)}
for _n, _s, _t in (
        ("xn", [B, 2, 16], BF), ("bt", [B, 2], I), ("encw", [EW], BF), ("xw0", [2 * HW], BF), ("xw1", [2 * HW], BF), ("ys", [V], BF),
        ("ye", [64], BF), ("zf", [B, 2], F), ("nat", [96], U), ("ones", [128], BF), ("idp", [128], BF),
        ("idn", [128], BF), ("idw", [128], BF), ("idb", [128], BF), ("idc", [128], BF), ("idf", [128], F), ("idg", [128], F),
        ("usel", [144], BF), ("w8", [8], BF), ("t8", [8], BF), ("pi", [2], I), ("rc", [4], F), ("bi", [B], F), ("bc", [B], F),
        ("nn", [2, 96], F), ("idh", [128], BF), ("idi", [128], BF), ("idu", [128], BF), ("idv", [128], BF), ("kap", [6, B], BF), ("am", [B], BF), ("eps", [B], F),
        ("thm", [4], BF), ("zab", [B, 3, 2], I)):
    SCRATCH[_n] = ("sbuf", [128] + _s, _t)
for _h in "01":
    for _n, _s, _t in (
            ("cmp", [752], BF), ("dv", [752], BF), ("eg", [752], BF), ("xr", [752], BF), ("xo", [2, 16 * (47 - NO)], BF), ("ll", [96], U),
            ("pl", [B], U), ("raw", [B, 2], I), ("ci", [3, B], I), ("zi", [B], I), ("pq", [B], I),
            ("xy", [96], F), ("lv", [96], F), ("tt", [192], F), ("mi", [2, 96], F), ("kk", [4, 52], F), ("fa", [6, B], F), ("aa", [B], BF), ("ce", [B], F),
            ("el", [4], U), ("ex", [4, 48], F), ("md", [2, 24], F), ("cm", [64], BF), ("mc", [10], U), ("uc", [6], F), ("mo", [32], F), ("ov", [2], BF)):
        SCRATCH[_n + _h] = ("sbuf", [128] + _s, _t)
    for _n in ("ps", "pc", "pf"):
        SCRATCH[_n + _h] = ("psum", [128, 512], F)

SEMAPHORES = ["qv", "qs", "qp", "qg", "sent", "arr00", "arr01", "arr10", "arr11"] + ["dma%d" % i for i in range(20)]


def build(g, core, T, topo, rank):
    ops, n = [], len(T.cores)
    Vq, Sq, Pq = g.vector, g.scalar, g.tensor
    early = [True]

    def add(eng, name, fn, r, w, fix=0.0, cyc=0.0, gat=0.0, pe=0.0, byt=0.0, kind="c"):
        ops.append(dict(eng=eng, name=name, fn=fn, r=list(r), w=list(w), cost=(fix, cyc, gat, pe, byt), kind=kind, early=early[0], extra=False))

    def ts(name, out, in0, s1, s2, op0, op1, r, w, k=64):
        add("v", name, lambda: Vq.tensor_scalar(out, in0, s1, s2, *([op0] if op1 is None else [op0, op1])), r, w, cyc=max(64, k))

    def tt(name, out, in0, in1, op, r, w, k=64):
        add("v", name, lambda: Vq.tensor_tensor(out, in0, in1, op), r, w, cyc=max(64, k))

    def cp(name, out, in_, r, w, k=64):
        add("v", name, lambda: Vq.tensor_copy(out, in_), r, w, cyc=max(64, k))

    def scan(name, out, d0, d1, init, op0, op1, r, w, k=64):
        add("v", name, lambda: Vq.tensor_tensor_scan(out, d0, d1, init, op0, op1), r, w, cyc=max(64, k))

    def mset(name, ap, val, w, k=64):
        add("v", name, lambda: Vq.memset(ap, val), [], w, cyc=max(64, k))

    def act(name, out, in_, func, r, w, k=64, bias=0.0, scale=1.0):
        add("s", name, lambda: Sq.activation(out, in_, func, bias=bias, scale=scale), r, w, fix=30.0, cyc=max(64, k))

    def vgt(name, out, win, lst, in1, op, r, w, k):
        add("v", name, lambda: Vq.tensor_tensor(out, win.indirect(lst), in1, op), r, w, fix=50.0, gat=k)

    def vgc(name, out, win, lst, r, w, k):
        add("v", name, lambda: Vq.tensor_copy(out, win.indirect(lst)), r, w, fix=50.0, gat=k)

    def sgc(name, out, win, lst, r, w, k):
        add("s", name, lambda: Sq.activation(out, win.indirect(lst), ACT.Copy), r, w, fix=65.0, gat=k)

    def mm(name, lst, r, w):
        add("p", name, lambda: [Pq.matmul(*m[:5]) for m in lst][-1], r, w, pe=sum(m[5] * max(64, m[0].shape[-1]) for m in lst))

    queued = [0.0]

    def dma(q, name, out, in_, r, w, nbytes, ahead=True):
        queued[0] = (queued[0] if ahead else 0.0) + nbytes + 60000
        add(q, name, lambda: (g.sync if q == "y" else g.scalar).dma_start(out, in_), r, w, fix=60.0, byt=queued[0], kind="d")

    def gp(name, fn, r, w, k):
        add("g", name, fn, r, w, fix=170.0, cyc=2 * k)

    def gset(name, ap, val, w, k):
        gp(name, lambda: g.iota(ap, [[0, k]], val, 0, allow_small_or_imprecise_dtypes=True), [], w, k)

    def gsel(name, out, in_, val, r, w, k):
        gp(name, lambda: g.affine_select(out, in_, [[0, k]], ALU.is_ge, val or 0.0, 0 if val is None else -1, 0), r, w, k)

    dma("y", "ld_boat", T.bt[:], T.boat[:], [], ["bt"], 49152)
    dma("s", "ld_x", T.xn[:], T.x[:], [], ["xn"], 393216)
    ekeys = [(0, "e0"), (ENC_A, "e1")] + [(a, "f%d" % a) for a, b_, who in ENC_CP]
    for i, (a, b_) in enumerate(((0, ENC_A), (ENC_A, W))):
        dma("y", "ld_enc", T.encw[:, a:b_], T.enc[:, a:b_], [], ["e%d" % i], (b_ - a) * 256)
    queued[0] = (W - ENC_A) * 256
    for a, b_, who in ENC_CP:
        if who == "y":
            dma("y", "ld_rep", T.encw[:, a:b_], T.enc[:, a % W:a % W + b_ - a], ["e0"], ["f%d" % a], (b_ - a) * 256)

    def ewin(end):
        return T.encw[:, 0:end], [k for (a, k) in ekeys if a < end]

    mset("ones", T.ones[:], 1.0, ["ones"])
    mset("w8", T.w8[:], -BIG, ["w8"])
    mset("usel", T.usel[:], 0.0, ["usel"], 72)
    gp("idp", lambda: g.affine_select(T.idp[:], T.ones[:], [[-1, 128]], ALU.is_equal, 0.0, 0, 1), ["ones"], ["idp"], 128)
    gp("pi", lambda: g.iota(T.pi[:, 0:1], [[1, 1]], 0, 1), [], ["pi0"], 1)
    gp("bi", lambda: g.iota(T.bi[:], [[1, B]], 0, 0, allow_small_or_imprecise_dtypes=True), [], ["bi"], B)
    gp("t8", lambda: g.affine_select(T.t8[:], T.w8[:], [[-16, 8]], ALU.is_ge, 0.0, 0, 1), ["w8"], ["t8"], 8)
    gp("usel", lambda: g.affine_select(T.usel[:, 15:143:16], T.t8[:], [[16, 8]], ALU.is_ge, 0.0, 15, -1), ["t8"], ["usel"], 8)
    mset("am", T.am[:], -1.0, ["am"])
    mset("eps", T.eps[:], EPS, ["eps"])
    kaps = {}
    for (d, k), ns in sorted(NS.items()):
        key = (k == 0, ns)
        if key not in kaps:
            i = kaps[key] = len(kaps)
            mset("kap", T.kap[:, i, ns:B], 4.5 / 16 - key[0], ["kap%d" % i])
            mset("kap", T.kap[:, i, 0:ns], 9.0 / 16 - key[0], ["kas%d" % i])
    early[0] = False
    up, down = rank > 0, rank < n - 1
    for e, t in enumerate((11.5 if up else 1000.0, 4.5 if down else -1000.0)):
        gsel("thm", T.thm[:, e:e + 1], T.ones[:, 0:1], -t / 16, ["ones"], ["thm%d" % e], 1)
    gsel("thm", T.thm[:, 2:4], T.ones[:, 0:2], -11.5 / 16, ["ones"], ["thm2"], 2)
    for d in range(2):
        for h in range(2):
            gset("sent", T["xw%d" % d][:, h * HW:h * HW + 16], 255, ["sn%d%d" % (d, h)], 16)
    for H in "01":
        for e in ([] if down else [1]) + ([] if up else [0]):
            mset("ex", T["ex" + H][:, e:4:2, 24 * e:24 * e + 24], 0.0, ["exz0" + H, "exz1" + H])
            ops[-1]["extra"] = True
        for e in range(2):
            gset("pad", T["ex" + H][:, e:4:2, 43 - 24 * e:48 - 24 * e], 0, ["pad%d" % e + H], 10)
        gset("mi", T["mi" + H][:, :, 0:96:2], 1, ["m%s1" % H, "m%s2" % H], 96)
        gset("kk", T["kk" + H][:, :, 0:49:48], 0, ["k%s%d" % (H, i) for i in range(3)], 8)
        mset("sh", T["pc" + H][:, 63:64], BIG, ["s0" + H, "pc" + H])
        gset("lo", T["lv" + H][:, 1:96:2], -2 ** 23, ["lo" + H], B)
    for nm, val in (("idn", -1.0), ("idw", -16.0 * BIG), ("idb", -HALF), ("idc", HALF), ("idf", 1.0), ("idg", -1.0), ("idh", 2048.0), ("idi", -2048.0),
                    ("idu", 48.0 * BIG), ("idv", -48.0 * BIG)):
        act(nm, T[nm][:], T.idp[:], ACT.Identity, ["idp"], [nm], 128, scale=val)
    ts("r", T.pi[:, 1:2], T.pi[:, 0:1], 15, None, ALU.bitwise_and, None, ["pi0"], ["pi1"])
    ts("rc", T.rc[:, 0:1], T.pi[:, 1:2], 16.0, None, ALU.add, None, ["pi1"], ["rc0"])
    for i, c in ((1, 1.0 * HW), (2, -16.0), (3, 8.0)):
        act("rc", T.rc[:, i:i + 1], T.rc[:, 0:1], ACT.Identity, ["rc0"], ["rc%d" % i], bias=c)
    act("bc", T.bc[:], T.bi[:], ACT.Identity, ["bi"], ["bc"], scale=65536.0)
    act("ni", T.nn[:, 0, 1:96:2], T.bi[:], ACT.Identity, ["bi", "rc0"], ["ni"], scale=16.0, bias=T.rc[:, 0:1])
    act("ni", T.nn[:, 0, 0:96:2], T.nn[:, 0, 1:96:2], ACT.Identity, ["ni"], ["nn0"], scale=-1.0)
    act("ni", T.nn[:, 1, 0:96:2], T.nn[:, 0, 1:96:2], ACT.Identity, ["ni"], ["nj"], scale=-1.0, bias=2048.0)
    act("ni", T.nn[:, 1, 1:96:2], T.nn[:, 1, 0:96:2], ACT.Identity, ["nj"], ["nn1"], scale=-1.0)
    for a, b_, who in ENC_CP:
        o, s, e = T.encw[:, a:b_], T.encw[:, a % W:a % W + b_ - a], ["e0" if a % W < ENC_A else "e1"]
        if who == "v":
            cp("rep", o, s, e, ["f%d" % a], (b_ - a) / 2)
        elif who == "s":
            act("rep", o, s, ACT.Identity, e, ["f%d" % a], b_ - a)
        elif who == "g":
            gsel("rep", o, s, None, e, ["f%d" % a], b_ - a)

    zab = T.zab

    def xk(d, h):
        return [s + "%d%d" % (d, h) for s in ("sn", "xa", "xb", "xh", "xf")]

    def numbers(h, src, rk, t, step=1):
        raw, H = T["raw%d" % h], str(h)
        ts("rawa" + H, raw[:, ::step, 0], src, 37.0, 811.0 * t, ALU.mult, ALU.add, rk, ["rawa" + H])
        ts("rawb" + H, raw[:, ::step, 1], src, 101.0, None, ALU.mult, None, rk, ["rawb" + H])
        ts("ab" + H, zab[:, ::step, 1:3, h], raw[:, ::step, :], W - 1, None, ALU.bitwise_and, None, ["rawa" + H, "rawb" + H], ["ab" + H], 2 * B / step)

    def day_start(d, h):
        H = str(h)
        xy, fa, ci, ll = T["xy" + H], T["fa" + H], T["ci" + H], T["ll" + H]
        z, zk = (T.bt[:, :, h], ["bt"]) if d == 0 else (zab[:, :, 0, h], ["z" + H])
        tt("y" + H, xy[:, 1:94:2], zab[:, 0:47, 2, h], zab[:, 1:48, 1, h], ALU.add, ["ab" + H], ["xy1" + H], 94)
        if d == 0:
            cp("c0a" + H, ci[:, 0, 0:47], xy[:, 1:94:2], ["xy1" + H], ["ci0" + H])
            ts("c0b" + H, ci[:, 1, 0:47], ci[:, 0, 0:47], W - 1, None, ALU.bitwise_and, None, ["ci0" + H], ["ci1" + H])
            cp("c0" + H, ll[:, 0:47], ci[:, 1, 0:47], ["ci1" + H], ["ll" + H])
            gsel("own" + H, T["xo" + H][:, 0, :], T.xn[:, NO + 1:B, h, :], None, ["xn"], ["xo0" + H], 16 * (47 - NO))
        else:
            cp("c0" + H, ll[:, 0:47], xy[:, 1:94:2], ["xy1" + H], ["ll" + H])
            dma("y", "own" + H, T["xo" + H][:, 1, 0:16 * (46 - NO)], T.xw1[:, h * HW + 32 + 16 * NO:(h + 1) * HW - 16], xk(d, h)[1:3], ["xo1" + H],
                4096 * (46 - NO), False)
        tt("sx" + H, fa[:, 0, 0:47], zab[:, 0:47, 1, h], zab[:, 0:47, 2, h], ALU.add, ["ab" + H], ["sx" + H], 94)
        act("x" + H, xy[:, 0:94:2], fa[:, 0, 0:47], ACT.Identity, ["sx" + H], ["xy0" + H], scale=-1.0)
        tt("zz" + H, fa[:, 1, :], z, T.bc[:], ALU.add, zk + ["bc"], ["zz" + H], 96)
        race(d, 0, h)

    def adjacent(d, h):
        xw, o, b0 = T["xw%d" % d], h * HW, NS[(d, 0)] + 1
        a, b = (xw[:, o + 16 * b0:o + 16 * B], xw[:, o + 16 + 16 * b0:o + HW]) if d else (T.xn[:, b0 - 1:B - 1, h, :], T.xn[:, b0:B, h, :])
        tt("d%d%d" % (d, h), T["dv%d" % h][:, 0:16 * (B - b0)], a, b, ALU.subtract, xk(d, h) if d else ["xn"], ["dv%d" % h], 32 * (B - b0))

    def race(d, k, h):
        H, ns, s0 = str(h), NS[(d, k)], (d, k) == (1, 0)
        nv, xw, o = 47 - ns, T["xw%d" % d], h * HW
        win = xw[:, o:o + HW]
        cmp_, dv, eg, xr, ll, ps, pc, pf, aa = [T[s + H] for s in ("cmp", "dv", "eg", "xr", "ll", "ps", "pc", "pf", "aa")]
        ew, ek = ewin(W if (d, k) == (0, 0) else (2 * W + 811 * k + 15) // 16 * 16)
        X, tag = xk(d, h), "%d%d%d" % (d, k, h)
        ka = kaps[(k == 0, ns)]
        if k == 1:
            mm("hold" + tag, [(pc[:, 192:288], T.idf[:], T.nn[:, 1, :], True, False, 4), (pc[:, 192:288:2], T.idh[:], aa[:], False, False, 1),
                              (pc[:, 193:288:2], T.idi[:], aa[:], False, True, 1)], ["idf", "idh", "idi", "nn1", "aa" + H], ["pc" + H, "s" + H, "hold" + H])
        mm("cn0" + tag, [(pc[:, 0:47], T.idw[:], T.kap[:, ka, 0:47], True, False, 1)] + [(pc[:, 0:47], T.idw[:], aa[:, 1:48], False, False, 1)][:k],
           ["idw", "kap%d" % ka, "kas%d" % ka] + ["aa" + H][:k], ["pc" + H, "s" + H, "hold" + H])
        cuts = [ns + (nv * i // VP[k > 0]) // 2 * 2 for i in range(VP[k > 0])] + [47]
        for i, (u0, u1) in enumerate(zip(cuts, cuts[1:])):
            a0, a1, DV = 16 * (u0 - ns), 16 * (u1 - ns), ["dv%d" % i + H]
            if k > 0:
                vgt("gd%d" % i + tag, dv[:, a0:a1], win, ll[:, 48 + u0:48 + u1], T["xo" + H][:, d, 16 * (u0 - NO):16 * (u1 - NO)], ALU.subtract,
                    X + ["lr" + H, "xo%d" % d + H, "xp%d" % d + H], DV, a1 - a0)
            vgt("gc%d" % i + tag, cmp_[:, 16 * u0:16 * u1], ew, ll[:, u0:u1], dv[:, a0:a1], ALU.is_gt,
                ek + ["ll" + H, "dv" + H] + DV, ["cv%d" % i + H], a1 - a0)
        n1 = int(ns * SPLIT) // 2 * 2
        for C, u0, u1, pp, pk in (("0", 0, n1, ps, "ps" + H), ("1", n1, ns, pf if s0 else (T.pmw, T.pmc)[h], "pf" + H if s0 else ("pmw", "pmc")[h])):
            a0, a1 = 16 * u0, 16 * u1
            c0, out = o + 16, pp[:, 0:a1 - a0]
            if k > 0:
                sgc("gx" + C + tag, xr[:, a0:a1], win, ll[:, 48 + u0:48 + u1], X + ["lr" + H], ["xr" + C + H], a1 - a0)
            mm("su0" + C + tag, [(out, T.idp[:], xw[:, c0 + 16 + a0:c0 + 16 + a1], True, False, 1),
                                 (out, T.idn[:], xr[:, a0:a1] if k else xw[:, c0 + a0:c0 + a1], False, False, 1)],
               X + ["xr" + C + H][:k] + ["idp", "idn"], [pk])
            sgc("ge" + C + tag, eg[:, a0:a1], ew, ll[:, u0:u1], ek + ["ll" + H], ["eg" + C + H], a1 - a0)
            mm("su1" + C + tag, [(out, T.idp[:], eg[:, a0:a1], False, True, 1)], ["eg" + C + H, "idp", pk], [pk])
            act("sg" + C + tag, cmp_[:, a0:a1], out, ACT.Sign, [pk], ["cs" + C + H], a1 - a0, bias=-0.5)
        mm("cnt" + tag, [(pc[:, 0:47], T.usel[:, 15 - r:143 - r], cmp_[:, r:752:16], False, r == 15 and not s0, 1) for r in range(16)],
           ["usel", "cs0" + H, "cs1" + H, "cv0" + H, "cv1" + H, "cv2" + H, "pc" + H], ["pc" + H])

    def settle(d, k, h):
        H, tag = str(h), "%d%d%d" % (d, k, h)
        ll, tb, pc, pf, fa, kk, mi, aa = [T[s + H] for s in ("ll", "tt", "pc", "pf", "fa", "kk", "mi", "aa")]
        if k == 0:
            tt("dz" + H, fa[:, 2, 1:48], fa[:, 1, 0:47], fa[:, 1, 1:48], ALU.subtract, ["zz" + H, "nz0" + H, "nz1" + H], ["dz" + H], 94)
        a_, ak = (T.am, "am") if k == 0 else (aa, "aa" + H)
        scan("s" + tag, pc[:, 64:111], a_[:, 1:48], pc[:, 0:47], BIG, ALU.mult, ALU.max, [ak, "pc" + H], ["s" + H])
        fm, fk = (fa[:, 2, 1:48], "dz" + H) if k == 0 else (fa[:, 3, 1:48], "fm" + H)
        tt("g" + tag, fa[:, 4, 1:48], pc[:, 64:111], fm, ALU.max, ["s" + H, fk], ["g" + H])
        if k == 0:
            act("k" + tag, kk[:, 0, 1:48], fa[:, 4, 1:48], ACT.Relu, ["g" + H], ["k%s0" % H], scale=-1.0)
        else:
            scan("k" + tag, kk[:, k, 47:0:-1], mi[:, k - 1, 95:2:-2], fa[:, 4, 47:0:-1], 0.0, ALU.mult, ALU.min,
                 ["g" + H, "m%s%d" % (H, k)], ["k%s%d" % (H, k)])
        if k == 2:
            return
        mk, N = "m%s%d" % (H, k + 1), 811.0 * (k + 1)
        ce, ck = (T.eps, "eps") if k == 0 else (T["ce" + H], "ce" + H)
        lv = T["lv" + H]
        scan("l" + tag, lv[:, 94::-2], ce[:, 47::-1], pc[:, 110:62:-1], 0.0, ALU.mult, ALU.min, ["s" + H, "s0" + H, ck], ["l" + H])
        tt("m" + tag, mi[:, k, 1:96:2], lv[:, 0:96:2], a_[:], ALU.is_lt, ["l" + H, ak], [mk], 96)
        scan("sr" + tag, tb[:, 96:190], pc[:, 192:286] if k else T.nn[:, 0, 0:94], lv[:, 0:94], 0.0, ALU.add, ALU.max,
             ["l" + H, "lo" + H, "nn0", "hold" + H], ["sr" + H], 94)
        ts("lr" + tag, ll[:, 48:95], tb[:, 97:190:2], 0.25, None, ALU.add, None, ["sr" + H], ["lr" + H])
        scan("sc" + tag, tb[:, 0:94], mi[:, k, 0:94], T["xy" + H][:, 0:94], 0.0, ALU.mult, ALU.add, [mk, "xy0" + H, "xy1" + H, "ny0" + H, "ny1" + H],
             ["sc" + H], 94)
        ts("ll" + tag, ll[:, 0:47], tb[:, 1:94:2], N, 0.0, ALU.add, ALU.max, ["sc" + H], ["ll" + H])
        act("a" + tag, aa[:], mi[:, k, 1:96:2], ACT.Identity, [mk], ["aa" + H], bias=-1.0, scale=2.0)
        if k == 0:
            act("ce" + tag, T["ce" + H][:], mi[:, k, 1:96:2], ACT.Identity, [mk], ["ce" + H], bias=EPS, scale=1.0 - EPS)
        else:
            p1 = pf[:, 64:112]
            mm("br" + tag, [(p1, T.idf[:], fa[:, 1, :], True, False, 4), (p1, T.idg[:], kk[:, 0, 0:48], False, False, 4),
                            (p1, T.idf[:], kk[:, 0, 1:49], False, False, 4)], ["idf", "idg", "zz" + H, "dz" + H, "k%s0" % H], ["pf" + H])
            mm("bs" + tag, [(p1, T.idf[:], kk[:, 1, 0:48], False, False, 4), (p1, T.idg[:], kk[:, 1, 1:49], False, True, 4)],
               ["idf", "idg", "k%s1" % H], ["pf" + H])
        mm("fd" + tag, [(pf[:, 0:47], T.idf[:], fa[:, 2, 1:48], True, False, 4), (pf[:, 0:47], T.idc[:], aa[:, 1:48], False, False, 1),
                        (pf[:, 0:47], T.idb[:], aa[:, 0:47], False, True, 1)], ["idf", "idb", "idc", "dz" + H, "aa" + H], ["pf" + H])
        scan("f" + tag, fa[:, 3, 1:48], mi[:, k, 1:94:2], pf[:, 0:47], 2 * HALF, ALU.mult, ALU.add, [mk, "pf" + H], ["fm" + H, "pf1" + H])

    def neighbours(r):
        nb = [(r - 1, 0)][:r] + [(r + 1, 1)][:n - 1 - r]
        out = []
        for i, (q, s) in enumerate(nb):
            e = topo.engines(T.cores[r], T.cores[q])
            out.append((q, s, e[i * len(e) // len(nb):(i + 1) * len(e) // len(nb)]))
        return out

    def exchange(name, src, dst, r):
        def send():
            tr = []
            for q, s, es in neighbours(rank):
                rid, pid = topo.addr(T.cores[q], core)
                tr.append(RemoteDMATransfer(dst_ids=[DstId(rid=rid, pnc=pid)], dma_engine_mask=sum(1 << e for e in es),
                                            remote_sem=T.sem[name], src=src[s], dst=dst[s]))
            return g.remote_dma_fused(tr, local_sem=T.sem.sent)
        add("g", "send" + name, send, r, ["snd" + name], fix=500.0, kind="r")
        ops[-1]["sent"] = sum(len(u[2]) for u in neighbours(rank))
        add("x", name, None, ["snd" + name], [name], kind="a")
        ops[-1]["tok"] = (name, sum(len(v[2]) for u in neighbours(rank) for v in neighbours(u[0]) if v[0] == rank))

    def day_end(d, h):
        H, tag = str(h), "%d%d" % (d, h)
        pf, kk, zi, pq, pl, el, ex = [T[s + H] for s in ("pf", "kk", "zi", "pq", "pl", "el", "ex")]
        o, X = h * HW, xk(d, h)
        win = T["xw%d" % d][:, o:o + HW]
        tt("z0" + tag, pf[:, 128:176], pf[:, 64:112], kk[:, 2, 0:48], ALU.add, ["pf" + H, "k%s2" % H], ["pf" + H])
        tt("zi" + tag, zi[:], pf[:, 128:176], kk[:, 2, 1:49], ALU.subtract, ["pf" + H, "k%s2" % H], ["zi" + H])
        ts("pq" + tag, pq[:], zi[:], 12, 0xFF0, ALU.logical_shift_right, ALU.bitwise_and, ["zi" + H], ["pq" + H])
        if d == 0:
            step, pe, pk = 1, pq[:, 0:48:47], "pq" + H
            ts("zq" + tag, zab[:, :, 0, h], zi[:], 65535, None, ALU.bitwise_and, None, ["zi" + H], ["z" + H])
        else:
            step, pe, pk, ci = 47, T["ci" + H][:, 2, 0:2], "pe" + H, T["ci" + H]
            ts("zh" + tag, ci[:, 1, 0:1], kk[:, 2, 1:2], -1.0, pf[:, 64:65], ALU.mult, ALU.add, ["pf1" + H, "k%s2" % H], ["zh" + H])
            ts("zt" + tag, ci[:, 1, 1:2], kk[:, 2, 47:48], pf[:, 111:112], None, ALU.add, None, ["pf1" + H, "k%s2" % H], ["zt" + H])
            ts("pe" + tag, pe, ci[:, 1, 0:2], 12, 0xFF0, ALU.logical_shift_right, ALU.bitwise_and, ["zh" + H, "zt" + H], [pk])
            ts("ze" + tag, zab[:, ::47, 0, h], ci[:, 1, 0:2], 65535, None, ALU.bitwise_and, None, ["zh" + H, "zt" + H], ["z" + H])
            ts("zq" + tag, ci[:, 0, :], zi[:], 65535, None, ALU.bitwise_and, None, ["zi" + H], ["zq" + H])
        ts("el" + tag, el[:, 0:4:2], pe, T.rc[:, 0:1], None, ALU.add, None, [pk, "rc0"], ["el" + H])
        numbers(h, zab[:, ::step, 0, h], ["z" + H], 3 if d == 0 else 7, step)
        for e in range(2):
            c = 24 - 24 * e
            sgc("ew%d" % e + tag, ex[:, 2 * d + e, c:c + 16], win, el[:, 2 * e:2 * e + 1], X + ["el" + H], ["ew%d" % e + tag], 16)
            cp("ez%d" % e + tag, ex[:, 2 * d + e, c + 16:c + 19], zab[:, 47 * e, :, h], ["z" + H, "ab" + H], ["ez%d" % e + tag])
        if d == 0:
            pv = B - PERM_V
            ts("pl" + tag, pl[:], pq[:], T.rc[:, 0:1], None, ALU.add, None, ["pq" + H, "rc0"], ["pl" + H])
            sgc("pa" + tag, T.xw1[:, o + 16:o + 16 + 16 * pv], win, pl[:, 0:pv], X + ["pl" + H], ["xa1" + H, "xh1" + H], 16 * pv)
            vgc("pb" + tag, T.xw1[:, o + 16 + 16 * pv:o + HW], win, pl[:, pv:B], X + ["pl" + H], ["xb1" + H, "xf1" + H], 16 * PERM_V)
            adjacent(1, h)
        else:
            ts("pl" + tag, T.nat[:, h:96:2], pq[:], T.rc[:, h:h + 1], None, ALU.add, None, ["pq" + H, "rc" + H], ["nat" + H])
            cp("zf" + tag, T.zf[:, :, h], ci[:, 0, :], ["zq" + H], ["zf" + H])

    def meet(d, h):
        H, tag, o, e0 = str(h), "%d%d" % (d, h), h * HW, 2 * d
        ex, md, cm, mc, uc, mo, pc = [T[s + H] for s in ("ex", "md", "cm", "mc", "uc", "mo", "pc")]
        pm, pk, nm = (T.pmw, T.pmc)[h], ("pmw", "pmc")[h], 4 - 2 * d
        Z = ["ez0" + tag, "ez1" + tag, "pad0" + H, "pad1" + H]
        A = Z + ["ew0" + tag, "ew1" + tag]
        exchange("arr" + tag, [ex[:, e0, 24:48], ex[:, e0 + 1, 0:24]], [ex[:, e0 + 1, 24:48], ex[:, e0, 0:24]], A)
        Z, A = Z + ["arr" + tag, "exz" + tag], A + ["arr" + tag, "exz" + tag]
        ew, ek = ewin(EW if d == 0 else 2 * W)
        mm("mt" + tag, [(pm[:, 0:nm], T.idw[:], T.thm[:, 0:nm], True, False, 1)], ["idw", "thm0", "thm1", "thm2"], [pk])
        tt("md" + tag, md[:, :, 0:19], ex[:, e0:e0 + 2, 0:19], ex[:, e0:e0 + 2, 24:43], ALU.subtract, A, ["md" + H], 76)
        for e in range(2):
            E = str(e) + tag
            ts("mc" + E, mc[:, 2 * e:2 * e + 1], ex[:, e0 + e, 41:42], ex[:, e0 + e, 18:19], 811.0 * 3 * (1 - d), ALU.add, ALU.add, Z, ["mc%d" % e + H])
            vgt("m" + E, cm[:, 16 * e:16 * e + 16], ew, mc[:, 2 * e:2 * e + 1], md[:, e, 0:16], (ALU.is_gt, ALU.is_le)[e],
                ek + ["mc%d" % e + H, "md" + H], ["cm%d" % e + H], 16)
        if d == 0:
            for e in range(2):
                ts("ma%d" % e + tag, mc[:, 8 + e:9 + e], zab[:, 1 + 45 * e, 1 + e, h:h + 1], ex[:, e, 18 + 23 * e:19 + 23 * e], None, ALU.add, None,
                   Z + ["ab" + H], ["ma%d" % e + H])
            tt("mb0" + tag, mo[:, 0:16], ex[:, 0, 0:16], T.xw1[:, o + 32:o + 48], ALU.subtract, A + ["xa1" + H], ["mb0" + H])
            tt("mb1" + tag, mo[:, 16:32], T.xw1[:, o + HW - 32:o + HW - 16], ex[:, 1, 24:40], ALU.subtract, A + ["xa1" + H, "xb1" + H], ["mb1" + H])
            vgt("mo" + tag, cm[:, 32:64], ew, mc[:, 8:10], mo[:], ALU.is_gt, ek + [s + H for s in ("ma0", "ma1", "mb0", "mb1")], ["cm2" + H], 32)
        mm("mq" + tag, [(pm[:, 0:nm], T.usel[:, 15 - r:143 - r], cm[:, r:16 * nm:16], False, r == 15, 1) for r in range(16)],
           ["usel", "cm0" + H, "cm1" + H, "cm2" + H], [pk])
        ts("mi" + tag, mc[:, 4:8:2], pm[:, 0:2], T.rc[:, 2:3], T.rc[:, 3:4], ALU.max, ALU.min, [pk, "rc2", "rc3"], ["mi" + H])

        def pick(name, out, e, f, base, r, w):
            ts(name + str(e) + tag, out, uc[:, e:e + 1], md[:, e, 16 + f:17 + f], base, ALU.mult, ALU.add, ["uc%d" % e + H, "md" + H] + r, w)
        A = A + ["mi" + H]
        if d == 1:
            ts("uc" + tag, uc[:, 0:2], pm[:, 0:2], 0.0, None, ALU.is_lt, None, [pk], ["uc0" + H, "uc1" + H])
        for e in range(2):
            win, lst, b = ex[:, e0 + e, :], mc[:, 4 + 2 * e:5 + 2 * e], 47 * e
            if d == 1:
                (vgc, sgc)[e]("new%d" % e + tag, T.ye[:, 32 * e + 16 * h:32 * e + 16 * h + 16], win, lst, A, ["ye%d" % e + H], 16)
                pick("nz", T.zf[:, b, h:h + 1], e, 0, ex[:, e0 + e, 40:41], Z + ["zf" + H], ["zf%d" % e + H])
                continue
            ts("uc%d" % e + tag, uc[:, e:e + 1], pm[:, e:e + 1], 0.0, 1.0 - 2 * e, (ALU.is_lt, ALU.is_ge)[e], ALU.mult, [pk], ["uc%d" % e + H])
            c, zz, y = o + 16 + 16 * b, T["fa" + H][:, 1, b:b + 1], T["xy" + H][:, 1 + 92 * e:2 + 92 * e]
            sgc("new%d" % e + tag, T.xw1[:, c:c + 16], win, lst, A, [("xh1", "xf1")[e] + H], 16)
            pick("nz", zz, e, 0, zz, ["zz" + H], ["nz%d" % e + H])
            pick("ny", y, e, 2 - e, y, ["xy1" + H, "ll" + H], ["ny%d" % e + H])
        if d == 0:
            ov = T["ov" + H]
            ts("ow" + tag, uc[:, 2:4], pm[:, 2:4], 0.0, 0.5, ALU.is_lt, ALU.subtract, [pk], ["ow" + H])
            tt("ov" + tag, ov[:], uc[:, 2:4], uc[:, 0:2], ALU.mult, ["ow" + H, "uc0" + H, "uc1" + H], ["ov" + H])
            mm("fix" + tag, [(pc[:, 0:1], T.idv[:], ov[:, 0:1], False, False, 1), (pc[:, 46:47], T.idu[:], ov[:, 1:2], False, True, 1)],
               ["idu", "idv", "ov" + H], ["pc" + H])
            sgc("xo" + tag, T["xo" + H][:, 1, 16 * (46 - NO):16 * (47 - NO)], ex[:, 1, :], mc[:, 6:7], A, ["xp1" + H], 16)

    cp("xw0", T.xw0[:, 16:HW], T.xn[:, :, 0, :], ["xn"], xk(0, 0)[1:], 384)
    act("xw1", T.xw0[:, HW + 16:2 * HW], T.xn[:, :, 1, :], ACT.Identity, ["xn"], xk(0, 1)[1:], 768)
    for h in range(2):
        numbers(h, T.bt[:, :, h], ["bt"], 0)
        adjacent(0, h)
        day_start(0, h)
        for d in range(2):
            for k in range(3):
                settle(d, k, h)
                if k < 2:
                    race(d, k + 1, h)
            day_end(d, h)
            if d == 0:
                day_start(1, h)
            meet(d, h)
    X, c1 = xk(1, 0) + xk(1, 1) + ["nat0", "nat1"], 2 + FIN_V
    vgc("fv", T.ys[:, 32:16 * c1], T.xw1[:, 0:2 * HW], T.nat[:, 2:c1], X, ["ysv"], 16 * FIN_V)
    sgc("fs", T.ys[:, 16 * c1:1504], T.xw1[:, 0:2 * HW], T.nat[:, c1:94], X, ["yss"], 1504 - 16 * c1)
    dma("y", "st_v", T.yx[:, 32:16 * c1], T.ys[:, 32:16 * c1], ["ysv"], ["o0"], 4096 * FIN_V, False)
    dma("s", "st_s", T.yx[:, 16 * c1:1504], T.ys[:, 16 * c1:1504], ["yss"], ["o1"], 256 * (1504 - 16 * c1))
    dma("y", "st_h", T.yx[:, 0:32], T.ye[:, 0:32], ["ye00", "ye01"], ["o2"], 8192, False)
    dma("s", "st_f", T.yx[:, 1504:1536], T.ye[:, 32:64], ["ye10", "ye11"], ["o3"], 8192, False)
    dma("y", "st_b", T.yb[:], T.zf[:], ["zf00", "zf01", "zf10", "zf11"], ["o4"], 49152, False)
    return ops


def depend(ops):
    lastw, readers = {}, {}
    for i, o in enumerate(ops):
        dep = set(lastw[k] for k in o["r"] + o["w"] if k in lastw)
        for k in o["w"]:
            dep.update(readers.get(k, []))
        o["dep"] = sorted(dep - {i})
        for k in o["r"]:
            readers.setdefault(k, []).append(i)
        for k in o["w"]:
            lastw[k], readers[k] = i, []


def times(o, m):
    fix, cyc, gat, pe, byt = o["cost"]
    busy = fix + m["f"] * (0.83 * (cyc + m["g"] * gat) + m["pe"] * pe)
    return busy, (m["dma"] + byt / m["bw"] if o["kind"] == "d" else m["rem"] if o["kind"] == "a" else busy)


def order(ops):
    n, seed = len(ops), [12345]
    dep = [o["dep"] for o in ops]
    en = ["vspgyx".index(o["eng"]) for o in ops]
    succ = [set() for o in ops]
    for i in range(n):
        for j in dep[i]:
            succ[j].add(i)
    tms = [[(a, b + m["wake"]) for a, b in [times(o, m) for o in ops]] for m in MODELS]
    n0 = sum(o["early"] for o in ops)

    def rnd():
        seed[0] = (seed[0] * 1103515245 + 12345) % 2147483648
        return seed[0] / 2147483648.0

    def length(seq, lo, old):
        tot, res = 0.0, []
        for a, tm in enumerate(tms):
            end, fin = (old[a][0][:], old[a][1][:]) if lo else ([0.0] * n, [0.0] * n)
            free = [0.0] * 6
            for i in seq[:lo]:
                free[en[i]] = fin[i]
            for i in seq[lo:]:
                st = free[en[i]]
                for j in dep[i]:
                    if end[j] > st:
                        st = end[j]
                free[en[i]] = fin[i] = st + tm[i][0]
                end[i] = st + tm[i][1]
            tot += max(end) + 0.3 * sum(end) / n
            res.append((end, fin))
        return tot, res

    def path(seq, end, tm):
        prev, last = {}, [None] * 6
        for i in seq:
            prev[i], last[en[i]] = last[en[i]], i
        i, out = end.index(max(end)), []
        while True:
            js = [j for j in dep[i] if end[j] >= end[i] - tm[i][1] - 1e-6]
            if not js and prev[i] is None:
                return out
            out += [] if js else [(i, prev[i])]
            i = js[0] if js else prev[i]

    def listed(tm):
        noise, slack, bias = 400.0 * rnd(), 30.0 + 250.0 * rnd(), 2500.0 * rnd()
        pri = [0.0] * n
        for i in range(n - 1, -1, -1):
            pri[i] = tm[i][1] + max([pri[j] for j in succ[i]] + [0.0])
        pri = [p + noise * rnd() + bias * (ops[i]["name"][-1] == "0") for i, p in enumerate(pri)]
        left, rel, free, seq = [len(d) for d in dep], [0.0] * n, [0.0] * 6, []
        ready = [i for i in range(n) if not dep[i]]
        while ready:
            first = [i for i in ready if ops[i]["early"]]
            est = {i: max(free[en[i]], rel[i]) for i in ready}
            b = min(ready, key=lambda i: (est[i], -pri[i], i))
            b = min(first) if first else min([i for i in ready if en[i] == en[b] and est[i] <= est[b] + slack], key=lambda i: (-pri[i], i))
            free[en[b]] = est[b] + tm[b][0]
            ready.remove(b)
            seq.append(b)
            for j in succ[b]:
                rel[j] = max(rel[j], est[b] + tm[b][1])
                left[j] -= 1
                if left[j] == 0:
                    ready.append(j)
        return length(seq, 0, None)[0], seq

    def moved(best, moves):
        cur, hot = best[1], None
        c, res = length(cur, 0, None)
        for it in range(moves):
            k, d = (1, 1, 1, 2, 3)[int(rnd() * 5)], (-1, 1)[int(rnd() * 2)]
            if rnd() < 0.6:
                hot = hot or path(cur, res[it % len(tms)][0], tms[it % len(tms)])
                p = max(n0, cur.index(hot[int(rnd() * len(hot))][d > 0]))
            else:
                p = n0 + int(rnd() * (n - n0))
            i, q = cur[p], p
            while k and n0 <= q + d < n:
                q += d
                k -= en[cur[q]] == en[i]
            if k:
                continue
            lo, hi = min(p, q), max(p, q)
            seg, tied = cur[lo:hi + 1], {i}
            for x in (seg[-2::-1] if d < 0 else seg[1:]):
                if tied.intersection(succ[x] if d < 0 else dep[x]):
                    tied.add(x)
            if cur[q] in tied:
                continue
            a, b = [x for x in seg if x in tied], [x for x in seg if x not in tied]
            new = cur[:lo] + (a + b if d < 0 else b + a) + cur[hi + 1:]
            v, r = length(new, lo, res)
            if v < c or rnd() < math.exp((c - v) / (150.0 * (1.0 - it / moves) + 3.0)):
                c, cur, res, hot = v, new, r, None
                if c < best[0]:
                    best = (c, cur)
        return best

    def filled(key, pre, tm, back):
        at, slots = [None] * n, [[] for q in range(6)]
        for i in sorted(range(n), key=lambda i: key[i]):
            stack = [i]
            while stack:
                x = stack.pop()
                p = [j for j in pre[x] if at[j] is None]
                if p:
                    stack += [x] + p
                elif at[x] is None:
                    t = max([at[j] + tm[j][1 - back] for j in pre[x]] + [0.0]) + back * (tm[x][1] - tm[x][0])
                    s, k = slots[en[x]], 0
                    while k < len(s) and s[k][0] < t + tm[x][0] - 1e-9:
                        t, k = max(t, s[k][1]), k + 1
                    s.insert(k, (t, t + tm[x][0]))
                    at[x] = t
        return at

    def justified(seq, a):
        late = filled([-e for e in length(seq, 0, None)[1][a][0]], succ, tms[a], 1)
        at = filled([i - 1e9 if i < n0 else -late[i] - tms[a][i][0] for i in range(n)], dep, tms[a], 0)
        seq = list(range(n0)) + sorted(range(n0, n), key=lambda i: (at[i], i))
        return length(seq, 0, None)[0], seq

    pool = sorted(justified(listed(tms[t % len(tms)])[1], t // len(tms) % len(tms)) for t in range(TRIES))
    best = None
    for b in pool[:STARTS]:
        for t in range(2):
            b = moved(b, MOVES)
            b = min([b] + [justified(b[1], a) for a in range(len(tms))])
        best = min(best or b, b)
    return moved(best, 3 * MOVES)[1]


def emit(g, T, ops, seq):
    queue = {"v": g.vector, "s": g.scalar, "p": g.tensor, "g": g, "y": g.sync}
    known, total, nd = {q: {} for q in queue}, {}, 0
    for i in seq:
        o = ops[i]
        if o["kind"] == "a":
            o["clock"] = dict([o["tok"]])
            total.update(o["clock"])
            continue
        q, kn = queue[o["eng"]], known[o["eng"]]
        need = [ops[j] for j in o["dep"] if kn.get(ops[j]["tok"][0], 0) < ops[j]["tok"][1]]
        for p in [p for p in need if not any(u is not p and u["clock"].get(p["tok"][0], 0) >= p["tok"][1] for u in need)]:
            q.wait_ge(T.sem[p["tok"][0]], p["tok"][1])
            for s, c in p["clock"].items():
                kn[s] = max(kn.get(s, 0), c)
        ins = o["fn"]()
        if o["kind"] == "r":
            total["sent"] = total.get("sent", 0) + o["sent"]
            continue
        s, inc = ("dma%d" % nd, 16) if o["kind"] == "d" else ("q" + o["eng"], 1)
        nd += o["kind"] == "d"
        ins.then_inc(T.sem[s], inc)
        total[s] = total.get(s, 0) + inc
        o["tok"], o["clock"] = (s, total[s]), dict(kn, **{s: total[s]})
    for s in sorted(total, key=lambda s: int(s[3:]) if s[:3] == "dma" else -1):
        g.wait_ge(T.sem[s], total[s])


ORDER = []


def rank_program(g, core, T, topo):
    rank = T.rank_of(core)
    if rank is None:
        return
    ops = build(g, core, T, topo, rank)
    common = [o for o in ops if not o["extra"]]
    if not ORDER:
        depend(common)
        ORDER.extend(order(common))
    depend(ops)
    index = [i for i, o in enumerate(ops) if not o["extra"]]
    emit(g, T, ops, [i for i, o in enumerate(ops) if o["extra"]] + [index[i] for i in ORDER])
